import numpy as np
import ml_dtypes


def mxq(x, axis, fmt="e4m3"):
    dtype, down = {"e4m3": (ml_dtypes.float8_e4m3fn, 7), "e5m2": (ml_dtypes.float8_e5m2, 14)}[fmt]
    v = np.moveaxis(np.asarray(x, np.float32).astype(ml_dtypes.bfloat16).astype(np.float64), axis, -1)
    blocks = v.reshape(v.shape[:-1] + (-1, 32))
    amax = np.abs(blocks).max(-1, keepdims=True)
    byte = np.maximum(np.where(amax > 0, np.frexp(amax)[1] - 1 + 127, 0) - down, 1)
    scale = np.exp2(byte - 127.0)
    codes = (blocks / scale).astype(np.float32).astype(dtype).astype(np.float64)
    return np.moveaxis((codes * scale).reshape(v.shape), -1, axis)


WIDE = False


def mx_kscale(k):
    if not WIDE:
        return np.ones(k)
    levels = np.array([18, -18])
    if k % 512:
        return np.exp2(np.random.permutation(np.resize(levels, k // 32))).repeat(32)
    a = np.empty((k // 512, 16))
    for p in range(k // 512):
        a[p, :8] = np.random.permutation(np.resize(levels, 8))
        for g in range(8):
            far = levels[np.abs(levels - a[p, g]) >= 10]
            a[p, g + 8] = far[np.random.randint(len(far))]
    return np.exp2(a.ravel()).repeat(32)


def f64(x):
    return np.asarray(x).astype(np.float64)


def striped(idx):
    return np.tile(np.asarray(idx).reshape(-1, 16).T, (8, 1)).astype(np.uint16)


def unstriped(offs):
    return offs[:16].T.reshape(-1).astype(np.int64)


B, N, T, D, R = 1, 512, 2048, 512, 512


def setup_inputs():
    n = np.random.standard_normal
    idx = np.random.permutation(T)[:B * N]
    s = mx_kscale(D)[:, None]
    z = mx_kscale(R)[:, None]
    u = np.ones(T)
    u[idx] = mx_kscale(B * N)
    r = np.random.uniform(0.5, 2.0, T) * u
    x = n((B, D, R))
    return {
        "xT": (x * s).astype(np.float32),
        "wT": (n((D, T)) * (1.00 / np.sqrt(D)) / s / r).astype(np.float32),
        "y": n((B, R, N)).astype(np.float32),
        "wt": (np.random.uniform(0.5, 1.5, (B, R, 1)) * 1.0 / np.sqrt(R) * z).astype(np.float32),
        "ts": np.tile(r, (128, 1)).astype(np.float32),
        "xm": (x.transpose(0, 2, 1) / z).astype(np.float32),
        "offs": striped(idx),
    }


def reference(xT, wT, y, wt, ts, xm, offs):
    idx = unstriped(offs)
    pick = lambda x: x[:, idx].reshape(x.shape[0], B, N).transpose(1, 0, 2)
    w = pick(f64(wT))
    a = mxq(f64(xT), 1, "e4m3").transpose(0, 2, 1) @ mxq(w, 1, "e4m3")
    ts_ = pick(f64(ts))[:, :1, :]
    a = a * ts_
    q = a - f64(y)
    g = f64(wt) * q / (1.0 + q * q)
    g = g * ts_
    dw = mxq(f64(xm), 1, "e4m3").transpose(0, 2, 1) @ mxq(g, 1, "e5m2")
    gw = np.zeros((D, T))
    gw[:, idx] = dw.transpose(1, 0, 2).reshape(D, B * N)
    gx = mxq(g, 2, "e5m2") @ mxq(w, 2, "e4m3").transpose(0, 2, 1)
    return gw, gx

@@ -1,0 +1,240 @@
+from contextlib import ExitStack
+
+import concourse.mybir as mybir
+from concourse.masks import make_identity
+
+N, T, D, R = 512, 2048, 512, 512
+FLOPS = 3 * 2 * N * D * R
+
+F32 = mybir.dt.float32
+BF16 = mybir.dt.bfloat16
+U32 = mybir.dt.uint32
+U16 = mybir.dt.uint16
+U8 = mybir.dt.uint8
+E4M3 = mybir.dt.float8_e4m3fn_x4
+E5M2 = mybir.dt.float8_e5m2_x4
+MULT = mybir.AluOpType.mult
+SUB = mybir.AluOpType.subtract
+ACT = mybir.ActivationFunctionType
+
+P = 128
+PACK = 4
+CHUNK = 128
+CHUNKS = N // CHUNK
+
+
+def tile_attend_gcau_wx_ts_kernel(tc, xT, wT, y, wt, ts, xm, offs, out_0, out_1):
+    nc = tc.nc
+    with ExitStack() as ctx:
+        sb = ctx.enter_context(tc.tile_pool(name="sb", bufs=1))
+        ps = ctx.enter_context(tc.psum_pool(name="ps", bufs=1))
+
+        def tile(name, shape, dtype):
+            return sb.tile(shape, dtype, name=name, align_bytes=64)
+
+        def bank(tag, name):
+            return ps.tile([P, 512], F32, name=name, tag=tag)
+
+        def operand(name):
+            return tile(name + "_codes", [P, 512], U32), tile(name + "_scales", [P, 512], U8)
+
+        def quantize(op, src, fmt, lo, hi):
+            nc.vector.quantize_mx(out=op[0][:, lo:hi].bitcast(fmt), scales=op[1][:, lo:hi], in_=src[:, PACK * lo : PACK * hi])
+
+        def mx(out, lhs, lhs_fmt, lhs_cols, rhs, rhs_fmt, rhs_cols):
+            nc.tensor.matmul_mx(
+                out=out,
+                lhsT=lhs[0][:, lhs_cols].bitcast(lhs_fmt),
+                lhsT_scale=lhs[1][:, lhs_cols],
+                rhs=rhs[0][:, rhs_cols].bitcast(rhs_fmt),
+                rhs_scale=rhs[1][:, rhs_cols],
+                start=True,
+                stop=True,
+            )
+
+        offsets = sb.tile([P, N // 16], U16, name="offsets")
+        nc.sync.dma_start(offsets[:], offs)
+        x_raw = tile("x_raw", [P, PACK, R], F32)
+        nc.sync.dma_start(out=x_raw[:], in_=xT[0].rearrange("(p j) r -> p j r", j=PACK))
+        planes = [tile(f"plane{t}", [P, T], F32) for t in range(PACK)]
+        w_rows = wT.rearrange("(p t) c -> p t c", t=PACK)
+        for t in range(PACK):
+            nc.sync.dma_start(out=planes[t][:], in_=w_rows[:, t, :])
+        xm_raw = tile("xm_raw", [P, PACK, D], F32)
+        nc.sync.dma_start(out=xm_raw[:], in_=xm[0].rearrange("(p t) d -> p t d", t=PACK))
+        y_rows = y[0].rearrange("(p t) i -> p t i", t=PACK)
+        y_half = [tile(f"y{k}", [P, PACK, N // 2], F32) for k in range(2)]
+        for k in range(2):
+            nc.sync.dma_start(out=y_half[k][:], in_=y_rows[:, :, k * (N // 2) : (k + 1) * (N // 2)])
+
+        ts_win = tile("ts_win", [P, T], F32)
+        nc.vector.memset(ts_win[:], 0.0)
+        ones = tile("ones", [P, 1], F32)
+        nc.vector.memset(ones[:], 1.0)
+        nc.scalar.dma_start(out=ts_win[0:1, :], in_=ts[0:1, :])
+        wt_sb = tile("wt_sb", [P, PACK], F32)
+        nc.scalar.dma_start(out=wt_sb[:], in_=wt[0].rearrange("(p t) o -> p (t o)", t=PACK))
+        warm = tile("warm", [P, 1], F32)
+        nc.scalar.activation(out=warm[:], in_=ones[:], func=ACT.Abs_reciprocal_sqrt, bias=ones[:])
+        ident = tile("ident", [P, P], F32)
+        make_identity(nc, ident[:])
+
+        ts_row = tile("ts_row", [P, N], F32)
+        nc.vector.tensor_copy(ts_row[:], ts_win[:].indirect(offsets[:]))
+        windows = [tile(f"window{m}", [P, T], F32) for m in range(D // P)]
+        for m in range(D // P):
+            nc.vector.memset(windows[m][:], 0.0)
+        ts_turn = bank("C0", "ts_turn")
+        for j in range(CHUNKS):
+            nc.tensor.transpose(ts_turn[:, j * P : (j + 1) * P], ts_row[:, j * P : (j + 1) * P], ident[:])
+        ts_col = tile("ts_col", [P, CHUNKS], F32)
+        nc.scalar.copy(out=ts_col[:], in_=ts_turn[:, 0 : N : P])
+        ts_back = bank("C1", "ts_back")
+        for j in range(CHUNKS):
+            nc.tensor.transpose(ts_back[:, j * P : (j + 1) * P], ts_col[:, j : j + 1].to_broadcast([P, P]), ident[:])
+        ts_all = tile("ts_all", [P, N], F32)
+        nc.scalar.copy(out=ts_all[:], in_=ts_back[:])
+
+        def ts_chunk(j):
+            return ts_all[:, j * CHUNK : (j + 1) * CHUNK].unsqueeze(2).to_broadcast([P, CHUNK, PACK])
+
+        factor = [tile(f"factor{j}", [P, CHUNK, PACK], F32) for j in range(CHUNKS)]
+        for j in range(CHUNKS):
+            nc.gpsimd.tensor_tensor(factor[j][:], ts_chunk(j), wt_sb[:].unsqueeze(1).to_broadcast([P, CHUNK, PACK]), MULT)
+
+        x_bf = tile("x_bf", [P, R * PACK], BF16)
+        nc.scalar.copy(
+            out=x_bf[:].rearrange("p (t m j) -> p m j t", t=PACK, j=PACK),
+            in_=x_raw[:].rearrange("p j (m t) -> p m j t", t=PACK),
+        )
+        x_q = operand("x")
+        quantize(x_q, x_bf, E4M3, 0, R)
+
+        w_bf = tile("w_bf", [P, N * PACK], BF16)
+        w_q = operand("w")
+        wi_bf = tile("wi_bf", [P, D * PACK], BF16)
+
+        def turn(src, u, dst_bank):
+            words = src[:].bitcast(F32)
+            for s in range(PACK):
+                nc.tensor.transpose(dst_bank[:, s * P : (s + 1) * P], words[:, 2 * s + u : 2 * N : 2 * PACK], ident[:])
+
+        def lay_out(dst, u, src_bank):
+            nc.scalar.copy(
+                out=dst[:].rearrange("q (p u e s) -> q u p e s", u=2, e=2, s=PACK)[:, u],
+                in_=src_bank[:].bitcast(BF16).rearrange("q (s p e) -> q p e s", s=PACK, e=2),
+            )
+
+        for t in range(PACK - 1):
+            nc.vector.tensor_copy(w_bf[:, t : N * PACK : PACK], planes[t][:].indirect(offsets[:]))
+            if t == 1:
+                w_turn0 = bank("B0", "w_turn0")
+                turn(w_bf, 0, w_turn0)
+                lay_out(wi_bf, 0, w_turn0)
+
+        scores = [bank(f"A{j}", f"scores{j}") for j in range(CHUNKS)]
+        half = N // 2
+        t = PACK - 1
+        for k in range(2):
+            nc.vector.tensor_copy(
+                w_bf[:, k * half * PACK + t : (k + 1) * half * PACK : PACK],
+                planes[t][:].indirect(offsets[:, k * half // 16 : (k + 1) * half // 16]),
+            )
+            quantize(w_q, w_bf, E4M3, k * half, (k + 1) * half)
+            for j in range(2 * k, 2 * k + 2):
+                for b in range(PACK):
+                    mx(scores[j][:, b * CHUNK : (b + 1) * CHUNK], x_q, E4M3, slice(b * P, (b + 1) * P), w_q, E4M3, slice(j * CHUNK, (j + 1) * CHUNK))
+
+        xm_bf = tile("xm_bf", [P, D * PACK], BF16)
+        for k in range(2):
+            nc.scalar.copy(
+                out=xm_bf[:, k * 1024 : (k + 1) * 1024].rearrange("p (d t) -> p d t", t=PACK),
+                in_=xm_raw[:, :, k * 256 : (k + 1) * 256].rearrange("p t d -> p d t"),
+            )
+
+        h_bf = tile("h_bf", [P, N * PACK], BF16)
+        h_q = operand("h")
+        a = [tile(f"a{j}", [P, CHUNK, PACK], F32) for j in range(CHUNKS)]
+        q = [tile(f"q{j}", [P, CHUNK, PACK], F32) for j in range(CHUNKS)]
+        sq = [tile(f"sq{j}", [P, CHUNK, PACK], F32) for j in range(CHUNKS)]
+        root = [tile(f"root{j}", [P, CHUNK, PACK], F32) for j in range(CHUNKS)]
+        rec = [tile(f"rec{j}", [P, CHUNK, PACK], F32) for j in range(CHUNKS)]
+        num = [tile(f"num{j}", [P, CHUNK, PACK], F32) for j in range(CHUNKS)]
+
+        def scale(j):
+            nc.vector.tensor_tensor(a[j][:], scores[j][:].rearrange("p (t i) -> p i t", t=PACK), ts_chunk(j), MULT)
+
+        def residual(j):
+            y_chunk = y_half[j // 2][:, :, (j % 2) * CHUNK : (j % 2 + 1) * CHUNK].rearrange("p t i -> p i t")
+            nc.vector.tensor_tensor(q[j][:], a[j][:], y_chunk, SUB)
+            nc.scalar.activation(out=sq[j][:], in_=q[j][:], func=ACT.Square)
+            nc.scalar.activation(out=root[j][:], in_=sq[j][:], func=ACT.Abs_reciprocal_sqrt, bias=ones[:])
+            nc.scalar.activation(out=rec[j][:], in_=root[j][:], func=ACT.Square)
+
+        def numerator(j):
+            nc.vector.tensor_tensor(num[j][:], q[j][:], factor[j][:], MULT)
+
+        def finish(j):
+            nc.vector.tensor_tensor(
+                h_bf[:, j * 512 : (j + 1) * 512].rearrange("p (i t) -> p i t", t=PACK), num[j][:], rec[j][:], MULT
+            )
+
+        xm_q = operand("xm")
+        scale(0)
+        scale(1)
+        residual(0)
+        residual(1)
+        scale(2)
+        numerator(0)
+        residual(2)
+        scale(3)
+        finish(0)
+        residual(3)
+        numerator(1)
+        quantize(h_q, h_bf, E5M2, 0, 128)
+        finish(1)
+        numerator(2)
+        quantize(h_q, h_bf, E5M2, 128, 256)
+        finish(2)
+        numerator(3)
+        quantize(h_q, h_bf, E5M2, 256, 384)
+        quantize(xm_q, xm_bf, E4M3, 0, D)
+        finish(3)
+        quantize(h_q, h_bf, E5M2, 384, 512)
+
+        w_turn1 = bank("B1", "w_turn1")
+        turn(w_bf, 1, w_turn1)
+        lay_out(wi_bf, 1, w_turn1)
+
+        dw = [tile(f"dw{m}", [P, N], F32) for m in range(D // P)]
+        for m in range(D // P):
+            acc = bank(f"A{m}", f"dw_acc{m}")
+            mx(acc[:], xm_q, E4M3, slice(m * P, (m + 1) * P), h_q, E5M2, slice(0, N))
+            nc.scalar.copy(out=dw[m][:], in_=acc[:])
+
+        def scatter(m):
+            nc.vector.tensor_copy(windows[m][:].indirect(offsets[:]), dw[m][:])
+            nc.sync.dma_start(out=out_0[m * P : (m + 1) * P, :], in_=windows[m][:])
+
+        wi_q = operand("wi")
+        quantize(wi_q, wi_bf, E4M3, 0, D)
+        scatter(0)
+        scatter(1)
+
+        hi_bf = tile("hi_bf", [P, R * PACK], BF16)
+        for u in range(2):
+            h_turn = bank(f"A{u}", f"h_turn{u}")
+            turn(h_bf, u, h_turn)
+            lay_out(hi_bf, u, h_turn)
+        hi_q = operand("hi")
+        quantize(hi_q, hi_bf, E5M2, 0, R)
+        gx = tile("gx", [P, R // P, D], F32)
+        gx_rows = out_1[0].rearrange("(b p) d -> p b d", p=P)
+        for b in range(R // P):
+            acc = bank(("B0", "B1", "C0", "C1")[b], f"gx_acc{b}")
+            mx(acc[:], hi_q, E5M2, slice(b * P, (b + 1) * P), wi_q, E4M3, slice(0, D))
+            nc.scalar.copy(out=gx[:, b, :], in_=acc[:])
+            if b % 2 == 1:
+                nc.sync.dma_start(out=gx_rows[:, b - 1 : b + 1, :], in_=gx[:, b - 1 : b + 1, :])
+        scatter(2)
+        scatter(3)

@@ -54,6 +54,10 @@ def tile_attend_gcau_wx_ts_kernel(tc, xT, wT, y, wt, ts, xm, offs, out_0, out_1)
 
         offsets = sb.tile([P, N // 16], U16, name="offsets")
         nc.sync.dma_start(offsets[:], offs)
+        ts_cols = tile("ts_cols", [P, T // P], F32)
+        nc.sync.dma_start(out=ts_cols[:], in_=ts[0].rearrange("(p c) -> p c", p=P))
+        wt_sb = tile("wt_sb", [P, PACK], F32)
+        nc.sync.dma_start(out=wt_sb[:], in_=wt[0].rearrange("(p t) o -> p (t o)", t=PACK))
         x_raw = tile("x_raw", [P, PACK, R], F32)
         nc.sync.dma_start(out=x_raw[:], in_=xT[0].rearrange("(p j) r -> p j r", j=PACK))
         planes = [tile(f"plane{t}", [P, T], F32) for t in range(PACK)]
@@ -67,33 +71,28 @@ def tile_attend_gcau_wx_ts_kernel(tc, xT, wT, y, wt, ts, xm, offs, out_0, out_1)
         for k in range(2):
             nc.sync.dma_start(out=y_half[k][:], in_=y_rows[:, :, k * (N // 2) : (k + 1) * (N // 2)])
 
-        ts_win = tile("ts_win", [P, T], F32)
-        nc.vector.memset(ts_win[:], 0.0)
         ones = tile("ones", [P, 1], F32)
         nc.vector.memset(ones[:], 1.0)
-        nc.scalar.dma_start(out=ts_win[0:1, :], in_=ts[0:1, :])
-        wt_sb = tile("wt_sb", [P, PACK], F32)
-        nc.scalar.dma_start(out=wt_sb[:], in_=wt[0].rearrange("(p t) o -> p (t o)", t=PACK))
         warm = tile("warm", [P, 1], F32)
         nc.scalar.activation(out=warm[:], in_=ones[:], func=ACT.Abs_reciprocal_sqrt, bias=ones[:])
         ident = tile("ident", [P, P], F32)
         make_identity(nc, ident[:])
 
-        ts_row = tile("ts_row", [P, N], F32)
-        nc.vector.tensor_copy(ts_row[:], ts_win[:].indirect(offsets[:]))
         windows = [tile(f"window{m}", [P, T], F32) for m in range(D // P)]
         for m in range(D // P):
             nc.vector.memset(windows[m][:], 0.0)
-        ts_turn = bank("C0", "ts_turn")
-        for j in range(CHUNKS):
-            nc.tensor.transpose(ts_turn[:, j * P : (j + 1) * P], ts_row[:, j * P : (j + 1) * P], ident[:])
-        ts_col = tile("ts_col", [P, CHUNKS], F32)
-        nc.scalar.copy(out=ts_col[:], in_=ts_turn[:, 0 : N : P])
-        ts_back = bank("C1", "ts_back")
-        for j in range(CHUNKS):
-            nc.tensor.transpose(ts_back[:, j * P : (j + 1) * P], ts_col[:, j : j + 1].to_broadcast([P, P]), ident[:])
+        ts_win = tile("ts_win", [P, T], F32)
+        for g in range(PACK):
+            spread = bank(f"A{g}", f"spread{g}")
+            for e in range(PACK):
+                c = PACK * g + e
+                nc.tensor.transpose(spread[:, e * P : (e + 1) * P], ts_cols[:, c : c + 1].to_broadcast([P, P]), ident[:])
+            nc.scalar.copy(
+                out=ts_win[:].rearrange("m (p g e) -> m g p e", g=PACK, e=PACK)[:, g],
+                in_=spread[:].rearrange("m (e p) -> m p e", e=PACK),
+            )
         ts_all = tile("ts_all", [P, N], F32)
-        nc.scalar.copy(out=ts_all[:], in_=ts_back[:])
+        nc.vector.tensor_copy(ts_all[:], ts_win[:].indirect(offsets[:]))
 
         def ts_chunk(j):
             return ts_all[:, j * CHUNK : (j + 1) * CHUNK].unsqueeze(2).to_broadcast([P, CHUNK, PACK])
@@ -207,7 +206,8 @@ def tile_attend_gcau_wx_ts_kernel(tc, xT, wT, y, wt, ts, xm, offs, out_0, out_1)
         lay_out(wi_bf, 1, w_turn1)
 
         dw = [tile(f"dw{m}", [P, N], F32) for m in range(D // P)]
-        for m in range(D // P):
+
+        def table_block(m):
             acc = bank(f"A{m}", f"dw_acc{m}")
             mx(acc[:], xm_q, E4M3, slice(m * P, (m + 1) * P), h_q, E5M2, slice(0, N))
             nc.scalar.copy(out=dw[m][:], in_=acc[:])
@@ -216,18 +216,22 @@ def tile_attend_gcau_wx_ts_kernel(tc, xT, wT, y, wt, ts, xm, offs, out_0, out_1)
             nc.vector.tensor_copy(windows[m][:].indirect(offsets[:]), dw[m][:])
             nc.sync.dma_start(out=out_0[m * P : (m + 1) * P, :], in_=windows[m][:])
 
+        table_block(0)
         wi_q = operand("wi")
         quantize(wi_q, wi_bf, E4M3, 0, D)
         scatter(0)
-        scatter(1)
 
         hi_bf = tile("hi_bf", [P, R * PACK], BF16)
         for u in range(2):
-            h_turn = bank(f"A{u}", f"h_turn{u}")
+            h_turn = bank(f"C{u}", f"h_turn{u}")
             turn(h_bf, u, h_turn)
             lay_out(hi_bf, u, h_turn)
         hi_q = operand("hi")
         quantize(hi_q, hi_bf, E5M2, 0, R)
+        for m in range(1, D // P):
+            table_block(m)
+            scatter(m)
+
         gx = tile("gx", [P, R // P, D], F32)
         gx_rows = out_1[0].rearrange("(b p) d -> p b d", p=P)
         for b in range(R // P):
@@ -235,6 +239,4 @@ def tile_attend_gcau_wx_ts_kernel(tc, xT, wT, y, wt, ts, xm, offs, out_0, out_1)
             mx(acc[:], hi_q, E5M2, slice(b * P, (b + 1) * P), wi_q, E4M3, slice(0, D))
             nc.scalar.copy(out=gx[:, b, :], in_=acc[:])
             if b % 2 == 1:
-                nc.sync.dma_start(out=gx_rows[:, b - 1 : b + 1, :], in_=gx[:, b - 1 : b + 1, :])
-        scatter(2)
-        scatter(3)
+                nc.scalar.dma_start(out=gx_rows[:, b - 1 : b + 1, :], in_=gx[:, b - 1 : b + 1, :])

@@ -9,6 +9,7 @@ FLOPS = 3 * 2 * N * D * R
 F32 = mybir.dt.float32
 BF16 = mybir.dt.bfloat16
 U32 = mybir.dt.uint32
+I32 = mybir.dt.int32
 U16 = mybir.dt.uint16
 U8 = mybir.dt.uint8
 E4M3 = mybir.dt.float8_e4m3fn_x4
@@ -30,7 +31,7 @@ def tile_attend_gcau_wx_ts_kernel(tc, xT, wT, y, wt, ts, xm, offs, out_0, out_1)
         ps = ctx.enter_context(tc.psum_pool(name="ps", bufs=1))
 
         def tile(name, shape, dtype):
-            return sb.tile(shape, dtype, name=name, align_bytes=64)
+            return sb.tile(shape, dtype, name=name, tag=name, align_bytes=64)
 
         def bank(tag, name):
             return ps.tile([P, 512], F32, name=name, tag=tag)
@@ -80,7 +81,8 @@ def tile_attend_gcau_wx_ts_kernel(tc, xT, wT, y, wt, ts, xm, offs, out_0, out_1)
 
         windows = [tile(f"window{m}", [P, T], F32) for m in range(D // P)]
         for m in range(D // P):
-            nc.vector.memset(windows[m][:], 0.0)
+            engine = nc.vector if m < 2 else nc.gpsimd
+            engine.memset(windows[m][:].bitcast(I32), 0)
         ts_win = tile("ts_win", [P, T], F32)
         for g in range(PACK):
             spread = bank(f"A{g}", f"spread{g}")
@@ -92,14 +94,12 @@ def tile_attend_gcau_wx_ts_kernel(tc, xT, wT, y, wt, ts, xm, offs, out_0, out_1)
                 in_=spread[:].rearrange("m (e p) -> m p e", e=PACK),
             )
         ts_all = tile("ts_all", [P, N], F32)
-        nc.vector.tensor_copy(ts_all[:], ts_win[:].indirect(offsets[:]))
+        factor = tile("factor", [P, PACK, N], F32)
 
-        def ts_chunk(j):
-            return ts_all[:, j * CHUNK : (j + 1) * CHUNK].unsqueeze(2).to_broadcast([P, CHUNK, PACK])
-
-        factor = [tile(f"factor{j}", [P, CHUNK, PACK], F32) for j in range(CHUNKS)]
-        for j in range(CHUNKS):
-            nc.gpsimd.tensor_tensor(factor[j][:], ts_chunk(j), wt_sb[:].unsqueeze(1).to_broadcast([P, CHUNK, PACK]), MULT)
+        def item_scales():
+            nc.vector.tensor_copy(ts_all[:], ts_win[:].indirect(offsets[:]))
+            for t in range(PACK):
+                nc.scalar.activation(out=factor[:, t, :], in_=ts_all[:], func=ACT.Copy, scale=wt_sb[:, t : t + 1])
 
         x_bf = tile("x_bf", [P, R * PACK], BF16)
         nc.scalar.copy(
@@ -111,7 +111,7 @@ def tile_attend_gcau_wx_ts_kernel(tc, xT, wT, y, wt, ts, xm, offs, out_0, out_1)
 
         w_bf = tile("w_bf", [P, N * PACK], BF16)
         w_q = operand("w")
-        wi_bf = tile("wi_bf", [P, D * PACK], BF16)
+        wi_q = operand("wi")
 
         def turn(src, u, dst_bank):
             words = src[:].bitcast(F32)
@@ -124,12 +124,23 @@ def tile_attend_gcau_wx_ts_kernel(tc, xT, wT, y, wt, ts, xm, offs, out_0, out_1)
                 in_=src_bank[:].bitcast(BF16).rearrange("q (s p e) -> q p e s", s=PACK, e=2),
             )
 
+        def slot_major_half(u, src_bank, tag):
+            half_bf = sb.tile([P, D * PACK // 2], BF16, name=f"wi_bf{u}", tag=tag, align_bytes=64)
+            nc.scalar.copy(
+                out=half_bf[:].rearrange("q (p e s) -> q p e s", e=2, s=PACK),
+                in_=src_bank[:].bitcast(BF16).rearrange("q (s p e) -> q p e s", s=PACK, e=2),
+            )
+            cols = slice(u * D // 2, (u + 1) * D // 2)
+            nc.vector.quantize_mx(out=wi_q[0][:, cols].bitcast(E4M3), scales=wi_q[1][:, cols], in_=half_bf[:])
+
         for t in range(PACK - 1):
             nc.vector.tensor_copy(w_bf[:, t : N * PACK : PACK], planes[t][:].indirect(offsets[:]))
+            if t == 0:
+                item_scales()
             if t == 1:
                 w_turn0 = bank("B0", "w_turn0")
                 turn(w_bf, 0, w_turn0)
-                lay_out(wi_bf, 0, w_turn0)
+                slot_major_half(0, w_turn0, "wi_bf0")
 
         scores = [bank(f"A{j}", f"scores{j}") for j in range(CHUNKS)]
         half = N // 2
@@ -147,68 +158,92 @@ def tile_attend_gcau_wx_ts_kernel(tc, xT, wT, y, wt, ts, xm, offs, out_0, out_1)
         xm_bf = tile("xm_bf", [P, D * PACK], BF16)
         for k in range(2):
             nc.scalar.copy(
-                out=xm_bf[:, k * 1024 : (k + 1) * 1024].rearrange("p (d t) -> p d t", t=PACK),
-                in_=xm_raw[:, :, k * 256 : (k + 1) * 256].rearrange("p t d -> p d t"),
+                out=xm_bf[:, k * 1024 : (k + 1) * 1024].rearrange("p (c e t) -> p c t e", e=PACK, t=PACK),
+                in_=xm_raw[:, :, k * 256 : (k + 1) * 256].rearrange("p t (c e) -> p c t e", e=PACK),
             )
 
         h_bf = tile("h_bf", [P, N * PACK], BF16)
         h_q = operand("h")
-        a = [tile(f"a{j}", [P, CHUNK, PACK], F32) for j in range(CHUNKS)]
-        q = [tile(f"q{j}", [P, CHUNK, PACK], F32) for j in range(CHUNKS)]
-        sq = [tile(f"sq{j}", [P, CHUNK, PACK], F32) for j in range(CHUNKS)]
-        root = [tile(f"root{j}", [P, CHUNK, PACK], F32) for j in range(CHUNKS)]
-        rec = [tile(f"rec{j}", [P, CHUNK, PACK], F32) for j in range(CHUNKS)]
-        num = [tile(f"num{j}", [P, CHUNK, PACK], F32) for j in range(CHUNKS)]
+        a = [tile(f"a{j}", [P, PACK, CHUNK], F32) for j in range(CHUNKS)]
+        q = [tile(f"q{j}", [P, PACK, CHUNK], F32) for j in range(CHUNKS)]
+        sq = [tile(f"sq{j}", [P, PACK, CHUNK], F32) for j in range(CHUNKS)]
+        root = [tile(f"root{j}", [P, PACK, CHUNK], F32) for j in range(CHUNKS)]
+        rec = [tile(f"rec{j}", [P, PACK, CHUNK], F32) for j in range(CHUNKS)]
+        num = [tile(f"num{j}", [P, PACK, CHUNK], F32) for j in range(CHUNKS)]
 
         def scale(j):
-            nc.vector.tensor_tensor(a[j][:], scores[j][:].rearrange("p (t i) -> p i t", t=PACK), ts_chunk(j), MULT)
+            ts_chunk = ts_all[:, j * CHUNK : (j + 1) * CHUNK].unsqueeze(1).to_broadcast([P, PACK, CHUNK])
+            nc.vector.tensor_tensor(a[j][:], scores[j][:].rearrange("p (t i) -> p t i", t=PACK), ts_chunk, MULT)
 
         def residual(j):
-            y_chunk = y_half[j // 2][:, :, (j % 2) * CHUNK : (j % 2 + 1) * CHUNK].rearrange("p t i -> p i t")
-            nc.vector.tensor_tensor(q[j][:], a[j][:], y_chunk, SUB)
+            nc.vector.tensor_tensor(q[j][:], a[j][:], y_half[j // 2][:, :, (j % 2) * CHUNK : (j % 2 + 1) * CHUNK], SUB)
+
+        def square(j):
             nc.scalar.activation(out=sq[j][:], in_=q[j][:], func=ACT.Square)
+
+        def inverse_root(j):
             nc.scalar.activation(out=root[j][:], in_=sq[j][:], func=ACT.Abs_reciprocal_sqrt, bias=ones[:])
+
+        def inverse(j):
             nc.scalar.activation(out=rec[j][:], in_=root[j][:], func=ACT.Square)
 
         def numerator(j):
-            nc.vector.tensor_tensor(num[j][:], q[j][:], factor[j][:], MULT)
+            nc.vector.tensor_tensor(num[j][:], q[j][:], factor[:, :, j * CHUNK : (j + 1) * CHUNK], MULT)
 
         def finish(j):
             nc.vector.tensor_tensor(
-                h_bf[:, j * 512 : (j + 1) * 512].rearrange("p (i t) -> p i t", t=PACK), num[j][:], rec[j][:], MULT
+                h_bf[:, j * 512 : (j + 1) * 512].rearrange("p (c e t) -> p c t e", e=2, t=PACK),
+                num[j][:].rearrange("p t (c e) -> p c t e", e=2),
+                rec[j][:].rearrange("p t (c e) -> p c t e", e=2),
+                MULT,
             )
+
+        def quantize_h(j):
+            quantize(h_q, h_bf, E5M2, j * CHUNK, (j + 1) * CHUNK)
 
         xm_q = operand("xm")
         scale(0)
         scale(1)
         residual(0)
+        square(0)
         residual(1)
+        square(1)
+        inverse_root(0)
+        inverse_root(1)
         scale(2)
-        numerator(0)
-        residual(2)
         scale(3)
-        finish(0)
+        inverse(0)
+        residual(2)
+        square(2)
+        inverse(1)
         residual(3)
+        square(3)
+        inverse_root(2)
+        inverse_root(3)
+        inverse(2)
+        inverse(3)
+        numerator(0)
         numerator(1)
-        quantize(h_q, h_bf, E5M2, 0, 128)
+        finish(0)
         finish(1)
         numerator(2)
-        quantize(h_q, h_bf, E5M2, 128, 256)
-        finish(2)
+        quantize_h(0)
         numerator(3)
-        quantize(h_q, h_bf, E5M2, 256, 384)
+        quantize_h(1)
         quantize(xm_q, xm_bf, E4M3, 0, D)
+        finish(2)
         finish(3)
-        quantize(h_q, h_bf, E5M2, 384, 512)
+        quantize_h(2)
+        quantize_h(3)
 
-        w_turn1 = bank("B1", "w_turn1")
+        w_turn1 = bank("A0", "w_turn1")
         turn(w_bf, 1, w_turn1)
-        lay_out(wi_bf, 1, w_turn1)
+        slot_major_half(1, w_turn1, f"root{CHUNKS - 1}")
 
         dw = [tile(f"dw{m}", [P, N], F32) for m in range(D // P)]
 
         def table_block(m):
-            acc = bank(f"A{m}", f"dw_acc{m}")
+            acc = bank(("B1", "A1", "A2", "A3")[m], f"dw_acc{m}")
             mx(acc[:], xm_q, E4M3, slice(m * P, (m + 1) * P), h_q, E5M2, slice(0, N))
             nc.scalar.copy(out=dw[m][:], in_=acc[:])
 
@@ -217,8 +252,6 @@ def tile_attend_gcau_wx_ts_kernel(tc, xT, wT, y, wt, ts, xm, offs, out_0, out_1)
             nc.sync.dma_start(out=out_0[m * P : (m + 1) * P, :], in_=windows[m][:])
 
         table_block(0)
-        wi_q = operand("wi")
-        quantize(wi_q, wi_bf, E4M3, 0, D)
         scatter(0)
 
         hi_bf = tile("hi_bf", [P, R * PACK], BF16)
@@ -235,8 +268,11 @@ def tile_attend_gcau_wx_ts_kernel(tc, xT, wT, y, wt, ts, xm, offs, out_0, out_1)
         gx = tile("gx", [P, R // P, D], F32)
         gx_rows = out_1[0].rearrange("(b p) d -> p b d", p=P)
         for b in range(R // P):
-            acc = bank(("B0", "B1", "C0", "C1")[b], f"gx_acc{b}")
+            acc = bank(("B0", "A0", "C0", "C1")[b], f"gx_acc{b}")
             mx(acc[:], hi_q, E5M2, slice(b * P, (b + 1) * P), wi_q, E4M3, slice(0, D))
-            nc.scalar.copy(out=gx[:, b, :], in_=acc[:])
+            nc.scalar.copy(
+                out=gx[:, b, :].rearrange("r (p u e) -> r p u e", u=2, e=2),
+                in_=acc[:].rearrange("r (u p e) -> r p u e", u=2, e=2),
+            )
             if b % 2 == 1:
                 nc.scalar.dma_start(out=gx_rows[:, b - 1 : b + 1, :], in_=gx[:, b - 1 : b + 1, :])

@@ -22,6 +22,7 @@ P = 128
 PACK = 4
 CHUNK = 128
 CHUNKS = N // CHUNK
+DIRECT = 2
 
 
 def tile_attend_gcau_wx_ts_kernel(tc, xT, wT, y, wt, ts, xm, offs, out_0, out_1):
@@ -54,23 +55,21 @@ def tile_attend_gcau_wx_ts_kernel(tc, xT, wT, y, wt, ts, xm, offs, out_0, out_1)
             )
 
         offsets = sb.tile([P, N // 16], U16, name="offsets")
-        nc.sync.dma_start(offsets[:], offs)
         ts_cols = tile("ts_cols", [P, T // P], F32)
-        nc.sync.dma_start(out=ts_cols[:], in_=ts[0].rearrange("(p c) -> p c", p=P))
+        nc.scalar.dma_start(out=ts_cols[:], in_=ts[0].rearrange("(p c) -> p c", p=P))
         wt_sb = tile("wt_sb", [P, PACK], F32)
-        nc.sync.dma_start(out=wt_sb[:], in_=wt[0].rearrange("(p t) o -> p (t o)", t=PACK))
+        nc.scalar.dma_start(out=wt_sb[:], in_=wt[0].rearrange("(p t) o -> p (t o)", t=PACK))
         x_raw = tile("x_raw", [P, PACK, R], F32)
         nc.sync.dma_start(out=x_raw[:], in_=xT[0].rearrange("(p j) r -> p j r", j=PACK))
+        nc.sync.dma_start(offsets[:], offs)
         planes = [tile(f"plane{t}", [P, T], F32) for t in range(PACK)]
         w_rows = wT.rearrange("(p t) c -> p t c", t=PACK)
         for t in range(PACK):
             nc.sync.dma_start(out=planes[t][:], in_=w_rows[:, t, :])
+        y_sb = tile("y_sb", [P, PACK, N], F32)
+        nc.sync.dma_start(out=y_sb[:], in_=y[0].rearrange("(p t) i -> p t i", t=PACK))
         xm_raw = tile("xm_raw", [P, PACK, D], F32)
         nc.sync.dma_start(out=xm_raw[:], in_=xm[0].rearrange("(p t) d -> p t d", t=PACK))
-        y_rows = y[0].rearrange("(p t) i -> p t i", t=PACK)
-        y_half = [tile(f"y{k}", [P, PACK, N // 2], F32) for k in range(2)]
-        for k in range(2):
-            nc.sync.dma_start(out=y_half[k][:], in_=y_rows[:, :, k * (N // 2) : (k + 1) * (N // 2)])
 
         ones = tile("ones", [P, 1], F32)
         nc.vector.memset(ones[:], 1.0)
@@ -94,10 +93,15 @@ def tile_attend_gcau_wx_ts_kernel(tc, xT, wT, y, wt, ts, xm, offs, out_0, out_1)
                 in_=spread[:].rearrange("m (e p) -> m p e", e=PACK),
             )
         ts_all = tile("ts_all", [P, N], F32)
+        ts_slot = tile("ts_slot", [P, CHUNKS], F32)
         factor = tile("factor", [P, PACK, N], F32)
 
         def item_scales():
             nc.vector.tensor_copy(ts_all[:], ts_win[:].indirect(offsets[:]))
+            ts_turn = bank("C0", "ts_turn")
+            for j in range(DIRECT, CHUNKS):
+                nc.tensor.transpose(ts_turn[:, j * P : (j + 1) * P], ts_all[:, j * P : (j + 1) * P], ident[:])
+            nc.scalar.copy(out=ts_slot[:, DIRECT:CHUNKS], in_=ts_turn[:, DIRECT * P : N : P])
             for t in range(PACK):
                 nc.scalar.activation(out=factor[:, t, :], in_=ts_all[:], func=ACT.Copy, scale=wt_sb[:, t : t + 1])
 
@@ -152,19 +156,29 @@ def tile_attend_gcau_wx_ts_kernel(tc, xT, wT, y, wt, ts, xm, offs, out_0, out_1)
             )
             quantize(w_q, w_bf, E4M3, k * half, (k + 1) * half)
             for j in range(2 * k, 2 * k + 2):
-                for b in range(PACK):
-                    mx(scores[j][:, b * CHUNK : (b + 1) * CHUNK], x_q, E4M3, slice(b * P, (b + 1) * P), w_q, E4M3, slice(j * CHUNK, (j + 1) * CHUNK))
+                slots = slice(j * CHUNK, (j + 1) * CHUNK)
+                if j < DIRECT:
+                    for b in range(PACK):
+                        mx(scores[j][:, b * CHUNK : (b + 1) * CHUNK], x_q, E4M3, slice(b * P, (b + 1) * P), w_q, E4M3, slots)
+                else:
+                    mx(scores[j][:], w_q, E4M3, slots, x_q, E4M3, slice(0, R))
 
-        xm_bf = tile("xm_bf", [P, D * PACK], BF16)
-        for k in range(2):
-            nc.scalar.copy(
-                out=xm_bf[:, k * 1024 : (k + 1) * 1024].rearrange("p (c e t) -> p c t e", e=PACK, t=PACK),
-                in_=xm_raw[:, :, k * 256 : (k + 1) * 256].rearrange("p t (c e) -> p c t e", e=PACK),
+        xm_q = operand("xm")
+
+        def xm_block(m, copy, tag):
+            xm_bf = sb.tile([P, P * PACK], BF16, name=f"xm_bf{m}", tag=tag, align_bytes=64)
+            copy(
+                out=xm_bf[:].rearrange("p (c e t) -> p c t e", e=PACK, t=PACK),
+                in_=xm_raw[:, :, m * P : (m + 1) * P].rearrange("p t (c e) -> p c t e", e=PACK),
             )
+            cols = slice(m * P, (m + 1) * P)
+            nc.vector.quantize_mx(out=xm_q[0][:, cols].bitcast(E4M3), scales=xm_q[1][:, cols], in_=xm_bf[:])
 
         h_bf = tile("h_bf", [P, N * PACK], BF16)
         h_q = operand("h")
-        a = [tile(f"a{j}", [P, PACK, CHUNK], F32) for j in range(CHUNKS)]
+        nc.gpsimd.memset(h_q[0][:, half:N].bitcast(I32), 0)
+        nc.gpsimd.memset(h_q[1][:, half:N].bitcast(I32), 0)
+        a = [tile(f"a{j}", [P, R], F32) for j in range(CHUNKS)]
         q = [tile(f"q{j}", [P, PACK, CHUNK], F32) for j in range(CHUNKS)]
         sq = [tile(f"sq{j}", [P, PACK, CHUNK], F32) for j in range(CHUNKS)]
         root = [tile(f"root{j}", [P, PACK, CHUNK], F32) for j in range(CHUNKS)]
@@ -172,11 +186,21 @@ def tile_attend_gcau_wx_ts_kernel(tc, xT, wT, y, wt, ts, xm, offs, out_0, out_1)
         num = [tile(f"num{j}", [P, PACK, CHUNK], F32) for j in range(CHUNKS)]
 
         def scale(j):
-            ts_chunk = ts_all[:, j * CHUNK : (j + 1) * CHUNK].unsqueeze(1).to_broadcast([P, PACK, CHUNK])
-            nc.vector.tensor_tensor(a[j][:], scores[j][:].rearrange("p (t i) -> p t i", t=PACK), ts_chunk, MULT)
+            if j < DIRECT:
+                ts_chunk = ts_all[:, j * CHUNK : (j + 1) * CHUNK].unsqueeze(1).to_broadcast([P, PACK, CHUNK])
+                nc.vector.tensor_tensor(
+                    a[j][:].rearrange("p (t i) -> p t i", t=PACK), scores[j][:].rearrange("p (t i) -> p t i", t=PACK), ts_chunk, MULT
+                )
+                return a[j]
+            nc.scalar.activation(out=a[j][:], in_=scores[j][:], func=ACT.Copy, scale=ts_slot[:, j : j + 1])
+            turned = bank(("C1", "B1", "B1", "B0")[j], f"turned{j}")
+            for t in range(PACK):
+                nc.tensor.transpose(turned[:, t * P : (t + 1) * P], a[j][:, t * P : (t + 1) * P], ident[:])
+            return turned
 
-        def residual(j):
-            nc.vector.tensor_tensor(q[j][:], a[j][:], y_half[j // 2][:, :, (j % 2) * CHUNK : (j % 2 + 1) * CHUNK], SUB)
+        def residual(j, scaled):
+            y_chunk = y_sb[:, :, j * CHUNK : (j + 1) * CHUNK]
+            nc.vector.tensor_tensor(q[j][:], scaled[:].rearrange("p (t i) -> p t i", t=PACK), y_chunk, SUB)
 
         def square(j):
             nc.scalar.activation(out=sq[j][:], in_=q[j][:], func=ACT.Square)
@@ -201,58 +225,56 @@ def tile_attend_gcau_wx_ts_kernel(tc, xT, wT, y, wt, ts, xm, offs, out_0, out_1)
         def quantize_h(j):
             quantize(h_q, h_bf, E5M2, j * CHUNK, (j + 1) * CHUNK)
 
-        xm_q = operand("xm")
-        scale(0)
-        scale(1)
-        residual(0)
+        scaled = [scale(j) for j in range(CHUNKS)]
+        for j in range(CHUNKS):
+            residual(j, scaled[j])
         square(0)
-        residual(1)
         square(1)
         inverse_root(0)
         inverse_root(1)
-        scale(2)
-        scale(3)
         inverse(0)
-        residual(2)
         square(2)
         inverse(1)
-        residual(3)
         square(3)
         inverse_root(2)
         inverse_root(3)
         inverse(2)
         inverse(3)
-        numerator(0)
-        numerator(1)
+        for j in range(CHUNKS):
+            numerator(j)
         finish(0)
         finish(1)
-        numerator(2)
+        xm_block(0, nc.vector.tensor_copy, "xm_bf0")
         quantize_h(0)
-        numerator(3)
         quantize_h(1)
-        quantize(xm_q, xm_bf, E4M3, 0, D)
+
+        dw = [tile(f"dw{m}", [P, N], F32) for m in range(D // P)]
+
+        def table_block(m, lo, hi, tag):
+            acc = bank(tag, f"dw_acc{m}_{lo}")
+            mx(acc[:], xm_q, E4M3, slice(m * P, (m + 1) * P), h_q, E5M2, slice(0, N))
+            nc.scalar.copy(out=dw[m][:, lo:hi], in_=acc[:, lo:hi])
+
+        def scatter(m, lo, hi):
+            nc.vector.tensor_copy(windows[m][:].indirect(offsets[:, lo // 16 : hi // 16]), dw[m][:, lo:hi])
+            if hi == N:
+                nc.sync.dma_start(out=out_0[m * P : (m + 1) * P, :], in_=windows[m][:])
+
+        table_block(0, 0, half, "C1")
         finish(2)
         finish(3)
         quantize_h(2)
         quantize_h(3)
-
-        w_turn1 = bank("A0", "w_turn1")
+        table_block(0, half, N, "A0")
+        scatter(0, 0, half)
+        xm_block(1, nc.scalar.copy, "rec2")
+        w_turn1 = bank("B0", "w_turn1")
         turn(w_bf, 1, w_turn1)
         slot_major_half(1, w_turn1, f"root{CHUNKS - 1}")
-
-        dw = [tile(f"dw{m}", [P, N], F32) for m in range(D // P)]
-
-        def table_block(m):
-            acc = bank(("B1", "A1", "A2", "A3")[m], f"dw_acc{m}")
-            mx(acc[:], xm_q, E4M3, slice(m * P, (m + 1) * P), h_q, E5M2, slice(0, N))
-            nc.scalar.copy(out=dw[m][:], in_=acc[:])
-
-        def scatter(m):
-            nc.vector.tensor_copy(windows[m][:].indirect(offsets[:]), dw[m][:])
-            nc.sync.dma_start(out=out_0[m * P : (m + 1) * P, :], in_=windows[m][:])
-
-        table_block(0)
-        scatter(0)
+        scatter(0, half, N)
+        table_block(1, 0, N, "A1")
+        scatter(1, 0, N)
+        xm_block(2, nc.scalar.copy, "rec3")
 
         hi_bf = tile("hi_bf", [P, R * PACK], BF16)
         for u in range(2):
@@ -261,18 +283,18 @@ def tile_attend_gcau_wx_ts_kernel(tc, xT, wT, y, wt, ts, xm, offs, out_0, out_1)
             lay_out(hi_bf, u, h_turn)
         hi_q = operand("hi")
         quantize(hi_q, hi_bf, E5M2, 0, R)
-        for m in range(1, D // P):
-            table_block(m)
-            scatter(m)
+        xm_block(3, nc.scalar.copy, "dw0")
+        for m in range(2, D // P):
+            table_block(m, 0, N, f"A{m}")
+            scatter(m, 0, N)
 
         gx = tile("gx", [P, R // P, D], F32)
         gx_rows = out_1[0].rearrange("(b p) d -> p b d", p=P)
         for b in range(R // P):
-            acc = bank(("B0", "A0", "C0", "C1")[b], f"gx_acc{b}")
+            acc = bank(("B1", "B0", "C0", "C1")[b], f"gx_acc{b}")
             mx(acc[:], hi_q, E5M2, slice(b * P, (b + 1) * P), wi_q, E4M3, slice(0, D))
             nc.scalar.copy(
                 out=gx[:, b, :].rearrange("r (p u e) -> r p u e", u=2, e=2),
                 in_=acc[:].rearrange("r (u p e) -> r p u e", u=2, e=2),
             )
-            if b % 2 == 1:
-                nc.scalar.dma_start(out=gx_rows[:, b - 1 : b + 1, :], in_=gx[:, b - 1 : b + 1, :])
+            nc.scalar.dma_start(out=gx_rows[:, b, :], in_=gx[:, b, :])

@@ -22,7 +22,10 @@ P = 128
 PACK = 4
 CHUNK = 128
 CHUNKS = N // CHUNK
+HALF = N // 2
 DIRECT = 2
+WINDOWS = 3
+VECTOR_MEMSETS = 2
 
 
 def tile_attend_gcau_wx_ts_kernel(tc, xT, wT, y, wt, ts, xm, offs, out_0, out_1):
@@ -78,10 +81,11 @@ def tile_attend_gcau_wx_ts_kernel(tc, xT, wT, y, wt, ts, xm, offs, out_0, out_1)
         ident = tile("ident", [P, P], F32)
         make_identity(nc, ident[:])
 
-        windows = [tile(f"window{m}", [P, T], F32) for m in range(D // P)]
-        for m in range(D // P):
-            engine = nc.vector if m < 2 else nc.gpsimd
+        windows = [tile(f"window{m}", [P, T], F32) for m in range(WINDOWS)]
+        for m in range(WINDOWS):
+            engine = nc.vector if m < VECTOR_MEMSETS else nc.gpsimd
             engine.memset(windows[m][:].bitcast(I32), 0)
+
         ts_win = tile("ts_win", [P, T], F32)
         for g in range(PACK):
             spread = bank(f"A{g}", f"spread{g}")
@@ -147,19 +151,18 @@ def tile_attend_gcau_wx_ts_kernel(tc, xT, wT, y, wt, ts, xm, offs, out_0, out_1)
                 slot_major_half(0, w_turn0, "wi_bf0")
 
         scores = [bank(f"A{j}", f"scores{j}") for j in range(CHUNKS)]
-        half = N // 2
-        t = PACK - 1
+        last = PACK - 1
         for k in range(2):
             nc.vector.tensor_copy(
-                w_bf[:, k * half * PACK + t : (k + 1) * half * PACK : PACK],
-                planes[t][:].indirect(offsets[:, k * half // 16 : (k + 1) * half // 16]),
+                w_bf[:, k * HALF * PACK + last : (k + 1) * HALF * PACK : PACK],
+                planes[last][:].indirect(offsets[:, k * HALF // 16 : (k + 1) * HALF // 16]),
             )
-            quantize(w_q, w_bf, E4M3, k * half, (k + 1) * half)
+            quantize(w_q, w_bf, E4M3, k * HALF, (k + 1) * HALF)
             for j in range(2 * k, 2 * k + 2):
                 slots = slice(j * CHUNK, (j + 1) * CHUNK)
                 if j < DIRECT:
-                    for b in range(PACK):
-                        mx(scores[j][:, b * CHUNK : (b + 1) * CHUNK], x_q, E4M3, slice(b * P, (b + 1) * P), w_q, E4M3, slots)
+                    for t in range(PACK):
+                        mx(scores[j][:, t * CHUNK : (t + 1) * CHUNK], x_q, E4M3, slice(t * P, (t + 1) * P), w_q, E4M3, slots)
                 else:
                     mx(scores[j][:], w_q, E4M3, slots, x_q, E4M3, slice(0, R))
 
@@ -176,16 +179,17 @@ def tile_attend_gcau_wx_ts_kernel(tc, xT, wT, y, wt, ts, xm, offs, out_0, out_1)
 
         h_bf = tile("h_bf", [P, N * PACK], BF16)
         h_q = operand("h")
-        nc.gpsimd.memset(h_q[0][:, half:N].bitcast(I32), 0)
-        nc.gpsimd.memset(h_q[1][:, half:N].bitcast(I32), 0)
+        nc.gpsimd.memset(h_q[0][:, HALF:N].bitcast(I32), 0)
+        nc.gpsimd.memset(h_q[1][:, HALF:N].bitcast(I32), 0)
         a = [tile(f"a{j}", [P, R], F32) for j in range(CHUNKS)]
         q = [tile(f"q{j}", [P, PACK, CHUNK], F32) for j in range(CHUNKS)]
         sq = [tile(f"sq{j}", [P, PACK, CHUNK], F32) for j in range(CHUNKS)]
         root = [tile(f"root{j}", [P, PACK, CHUNK], F32) for j in range(CHUNKS)]
         rec = [tile(f"rec{j}", [P, PACK, CHUNK], F32) for j in range(CHUNKS)]
         num = [tile(f"num{j}", [P, PACK, CHUNK], F32) for j in range(CHUNKS)]
+        turned_tag = {2: "B1", 3: "B0"}
 
-        def scale(j):
+        def times_ts(j):
             if j < DIRECT:
                 ts_chunk = ts_all[:, j * CHUNK : (j + 1) * CHUNK].unsqueeze(1).to_broadcast([P, PACK, CHUNK])
                 nc.vector.tensor_tensor(
@@ -193,14 +197,14 @@ def tile_attend_gcau_wx_ts_kernel(tc, xT, wT, y, wt, ts, xm, offs, out_0, out_1)
                 )
                 return a[j]
             nc.scalar.activation(out=a[j][:], in_=scores[j][:], func=ACT.Copy, scale=ts_slot[:, j : j + 1])
-            turned = bank(("C1", "B1", "B1", "B0")[j], f"turned{j}")
+            turned = bank(turned_tag[j], f"turned{j}")
             for t in range(PACK):
                 nc.tensor.transpose(turned[:, t * P : (t + 1) * P], a[j][:, t * P : (t + 1) * P], ident[:])
             return turned
 
-        def residual(j, scaled):
+        def residual(j, scaled_chunk):
             y_chunk = y_sb[:, :, j * CHUNK : (j + 1) * CHUNK]
-            nc.vector.tensor_tensor(q[j][:], scaled[:].rearrange("p (t i) -> p t i", t=PACK), y_chunk, SUB)
+            nc.vector.tensor_tensor(q[j][:], scaled_chunk[:].rearrange("p (t i) -> p t i", t=PACK), y_chunk, SUB)
 
         def square(j):
             nc.scalar.activation(out=sq[j][:], in_=q[j][:], func=ACT.Square)
@@ -216,7 +220,7 @@ def tile_attend_gcau_wx_ts_kernel(tc, xT, wT, y, wt, ts, xm, offs, out_0, out_1)
 
         def finish(j):
             nc.vector.tensor_tensor(
-                h_bf[:, j * 512 : (j + 1) * 512].rearrange("p (c e t) -> p c t e", e=2, t=PACK),
+                h_bf[:, j * CHUNK * PACK : (j + 1) * CHUNK * PACK].rearrange("p (c e t) -> p c t e", e=2, t=PACK),
                 num[j][:].rearrange("p t (c e) -> p c t e", e=2),
                 rec[j][:].rearrange("p t (c e) -> p c t e", e=2),
                 MULT,
@@ -225,7 +229,7 @@ def tile_attend_gcau_wx_ts_kernel(tc, xT, wT, y, wt, ts, xm, offs, out_0, out_1)
         def quantize_h(j):
             quantize(h_q, h_bf, E5M2, j * CHUNK, (j + 1) * CHUNK)
 
-        scaled = [scale(j) for j in range(CHUNKS)]
+        scaled = [times_ts(j) for j in range(CHUNKS)]
         for j in range(CHUNKS):
             residual(j, scaled[j])
         square(0)
@@ -256,22 +260,22 @@ def tile_attend_gcau_wx_ts_kernel(tc, xT, wT, y, wt, ts, xm, offs, out_0, out_1)
             nc.scalar.copy(out=dw[m][:, lo:hi], in_=acc[:, lo:hi])
 
         def scatter(m, lo, hi):
-            nc.vector.tensor_copy(windows[m][:].indirect(offsets[:, lo // 16 : hi // 16]), dw[m][:, lo:hi])
+            nc.vector.tensor_copy(windows[m % WINDOWS][:].indirect(offsets[:, lo // 16 : hi // 16]), dw[m][:, lo:hi])
             if hi == N:
-                nc.sync.dma_start(out=out_0[m * P : (m + 1) * P, :], in_=windows[m][:])
+                nc.sync.dma_start(out=out_0[m * P : (m + 1) * P, :], in_=windows[m % WINDOWS][:])
 
-        table_block(0, 0, half, "C1")
+        table_block(0, 0, HALF, "C1")
         finish(2)
         finish(3)
         quantize_h(2)
         quantize_h(3)
-        table_block(0, half, N, "A0")
-        scatter(0, 0, half)
+        table_block(0, HALF, N, "A0")
+        scatter(0, 0, HALF)
         xm_block(1, nc.scalar.copy, "rec2")
         w_turn1 = bank("B0", "w_turn1")
         turn(w_bf, 1, w_turn1)
-        slot_major_half(1, w_turn1, f"root{CHUNKS - 1}")
-        scatter(0, half, N)
+        slot_major_half(1, w_turn1, "root3")
+        scatter(0, HALF, N)
         table_block(1, 0, N, "A1")
         scatter(1, 0, N)
         xm_block(2, nc.scalar.copy, "rec3")

@@ -25,6 +25,7 @@ CHUNKS = N // CHUNK
 HALF = N // 2
 DIRECT = 2
 WINDOWS = 3
+X_SPLIT = 108
 VECTOR_MEMSETS = 2
 
 
@@ -32,6 +33,7 @@ def tile_attend_gcau_wx_ts_kernel(tc, xT, wT, y, wt, ts, xm, offs, out_0, out_1)
     nc = tc.nc
     with ExitStack() as ctx:
         sb = ctx.enter_context(tc.tile_pool(name="sb", bufs=1))
+        reuse = ctx.enter_context(tc.tile_pool(name="reuse", bufs=1))
         ps = ctx.enter_context(tc.psum_pool(name="ps", bufs=1))
 
         def tile(name, shape, dtype):
@@ -59,18 +61,23 @@ def tile_attend_gcau_wx_ts_kernel(tc, xT, wT, y, wt, ts, xm, offs, out_0, out_1)
 
         offsets = sb.tile([P, N // 16], U16, name="offsets")
         ts_cols = tile("ts_cols", [P, T // P], F32)
-        nc.scalar.dma_start(out=ts_cols[:], in_=ts[0].rearrange("(p c) -> p c", p=P))
+        nc.sync.dma_start(out=ts_cols[:], in_=ts[0].rearrange("(p c) -> p c", p=P))
         wt_sb = tile("wt_sb", [P, PACK], F32)
-        nc.scalar.dma_start(out=wt_sb[:], in_=wt[0].rearrange("(p t) o -> p (t o)", t=PACK))
-        x_raw = tile("x_raw", [P, PACK, R], F32)
-        nc.sync.dma_start(out=x_raw[:], in_=xT[0].rearrange("(p j) r -> p j r", j=PACK))
-        nc.sync.dma_start(offsets[:], offs)
         planes = [tile(f"plane{t}", [P, T], F32) for t in range(PACK)]
         w_rows = wT.rearrange("(p t) c -> p t c", t=PACK)
         for t in range(PACK):
             nc.sync.dma_start(out=planes[t][:], in_=w_rows[:, t, :])
-        y_sb = tile("y_sb", [P, PACK, N], F32)
-        nc.sync.dma_start(out=y_sb[:], in_=y[0].rearrange("(p t) i -> p t i", t=PACK))
+            if t == 0:
+                nc.sync.dma_start(offsets[:], offs)
+                nc.sync.dma_start(out=wt_sb[:], in_=wt[0].rearrange("(p t) o -> p (t o)", t=PACK))
+        x_rows = xT[0].rearrange("(p j) r -> p j r", j=PACK)
+        x_raw = [tile(f"x_raw{k}", [P, PACK, R // 2], F32) for k in range(2)]
+        for k in range(2):
+            nc.sync.dma_start(out=x_raw[k][:], in_=x_rows[:, :, k * R // 2 : (k + 1) * R // 2])
+        y_rows = y[0].rearrange("(p t) i -> p t i", t=PACK)
+        y_sb = [tile(f"y_sb{k}", [P, PACK, HALF], F32) for k in range(2)]
+        for k in range(2):
+            nc.sync.dma_start(out=y_sb[k][:], in_=y_rows[:, :, k * HALF : (k + 1) * HALF])
         xm_raw = tile("xm_raw", [P, PACK, D], F32)
         nc.sync.dma_start(out=xm_raw[:], in_=xm[0].rearrange("(p t) d -> p t d", t=PACK))
 
@@ -81,12 +88,11 @@ def tile_attend_gcau_wx_ts_kernel(tc, xT, wT, y, wt, ts, xm, offs, out_0, out_1)
         ident = tile("ident", [P, P], F32)
         make_identity(nc, ident[:])
 
-        windows = [tile(f"window{m}", [P, T], F32) for m in range(WINDOWS)]
-        for m in range(WINDOWS):
-            engine = nc.vector if m < VECTOR_MEMSETS else nc.gpsimd
-            engine.memset(windows[m][:].bitcast(I32), 0)
+        windows = [tile(f"window{m}", [P, T], F32) for m in range(VECTOR_MEMSETS)]
+        for m in range(VECTOR_MEMSETS):
+            nc.vector.memset(windows[m][:].bitcast(I32), 0)
 
-        ts_win = tile("ts_win", [P, T], F32)
+        ts_win = reuse.tile([P, T], F32, name="ts_win", offset=0, align_bytes=64)
         for g in range(PACK):
             spread = bank(f"A{g}", f"spread{g}")
             for e in range(PACK):
@@ -109,15 +115,17 @@ def tile_attend_gcau_wx_ts_kernel(tc, xT, wT, y, wt, ts, xm, offs, out_0, out_1)
             for t in range(PACK):
                 nc.scalar.activation(out=factor[:, t, :], in_=ts_all[:], func=ACT.Copy, scale=wt_sb[:, t : t + 1])
 
-        x_bf = tile("x_bf", [P, R * PACK], BF16)
-        nc.scalar.copy(
-            out=x_bf[:].rearrange("p (t m j) -> p m j t", t=PACK, j=PACK),
-            in_=x_raw[:].rearrange("p j (m t) -> p m j t", t=PACK),
-        )
+        x_bf = reuse.tile([P, R * PACK], BF16, name="x_bf", offset=2 * N * PACK, align_bytes=64)
         x_q = operand("x")
-        quantize(x_q, x_bf, E4M3, 0, R)
 
-        w_bf = tile("w_bf", [P, N * PACK], BF16)
+        def x_part(copy, lo, hi):
+            k, first = divmod(lo, P // 2)
+            copy(
+                out=x_bf[:].rearrange("p (t m j) -> p m j t", t=PACK, j=PACK)[:, lo:hi],
+                in_=x_raw[k][:].rearrange("p j (m t) -> p m j t", t=PACK)[:, first : first + hi - lo],
+            )
+
+        w_bf = reuse.tile([P, N * PACK], BF16, name="w_bf", offset=0, align_bytes=64)
         w_q = operand("w")
         wi_q = operand("wi")
 
@@ -141,30 +149,32 @@ def tile_attend_gcau_wx_ts_kernel(tc, xT, wT, y, wt, ts, xm, offs, out_0, out_1)
             cols = slice(u * D // 2, (u + 1) * D // 2)
             nc.vector.quantize_mx(out=wi_q[0][:, cols].bitcast(E4M3), scales=wi_q[1][:, cols], in_=half_bf[:])
 
-        for t in range(PACK - 1):
+        item_scales()
+        for t in range(PACK):
             nc.vector.tensor_copy(w_bf[:, t : N * PACK : PACK], planes[t][:].indirect(offsets[:]))
-            if t == 0:
-                item_scales()
             if t == 1:
                 w_turn0 = bank("B0", "w_turn0")
                 turn(w_bf, 0, w_turn0)
                 slot_major_half(0, w_turn0, "wi_bf0")
 
         scores = [bank(f"A{j}", f"scores{j}") for j in range(CHUNKS)]
-        last = PACK - 1
-        for k in range(2):
-            nc.vector.tensor_copy(
-                w_bf[:, k * HALF * PACK + last : (k + 1) * HALF * PACK : PACK],
-                planes[last][:].indirect(offsets[:, k * HALF // 16 : (k + 1) * HALF // 16]),
-            )
-            quantize(w_q, w_bf, E4M3, k * HALF, (k + 1) * HALF)
-            for j in range(2 * k, 2 * k + 2):
-                slots = slice(j * CHUNK, (j + 1) * CHUNK)
-                if j < DIRECT:
-                    for t in range(PACK):
-                        mx(scores[j][:, t * CHUNK : (t + 1) * CHUNK], x_q, E4M3, slice(t * P, (t + 1) * P), w_q, E4M3, slots)
-                else:
-                    mx(scores[j][:], w_q, E4M3, slots, x_q, E4M3, slice(0, R))
+        quantize(w_q, w_bf, E4M3, 0, N)
+        x_part(nc.scalar.copy, 0, P // 2)
+        x_part(nc.vector.tensor_copy, P // 2, X_SPLIT)
+        x_part(nc.scalar.copy, X_SPLIT, P)
+        quantize(x_q, x_bf, E4M3, 0, R)
+        for j in range(CHUNKS):
+            slots = slice(j * CHUNK, (j + 1) * CHUNK)
+            if j < DIRECT:
+                for t in range(PACK):
+                    mx(scores[j][:, t * CHUNK : (t + 1) * CHUNK], x_q, E4M3, slice(t * P, (t + 1) * P), w_q, E4M3, slots)
+            else:
+                mx(scores[j][:], w_q, E4M3, slots, x_q, E4M3, slice(0, R))
+        w_turn1 = bank("C1", "w_turn1")
+        turn(w_bf, 1, w_turn1)
+        slot_major_half(1, w_turn1, "wi_bf1")
+        windows.append(reuse.tile([P, T], F32, name="window2", offset=0, align_bytes=64))
+        nc.gpsimd.memset(windows[2][:].bitcast(I32), 0)
 
         xm_q = operand("xm")
 
@@ -203,7 +213,7 @@ def tile_attend_gcau_wx_ts_kernel(tc, xT, wT, y, wt, ts, xm, offs, out_0, out_1)
             return turned
 
         def residual(j, scaled_chunk):
-            y_chunk = y_sb[:, :, j * CHUNK : (j + 1) * CHUNK]
+            y_chunk = y_sb[j // 2][:, :, j % 2 * CHUNK : (j % 2 + 1) * CHUNK]
             nc.vector.tensor_tensor(q[j][:], scaled_chunk[:].rearrange("p (t i) -> p t i", t=PACK), y_chunk, SUB)
 
         def square(j):
@@ -248,7 +258,7 @@ def tile_attend_gcau_wx_ts_kernel(tc, xT, wT, y, wt, ts, xm, offs, out_0, out_1)
             numerator(j)
         finish(0)
         finish(1)
-        xm_block(0, nc.vector.tensor_copy, "xm_bf0")
+        xm_block(0, nc.vector.tensor_copy, "a1")
         quantize_h(0)
         quantize_h(1)
 
@@ -272,9 +282,6 @@ def tile_attend_gcau_wx_ts_kernel(tc, xT, wT, y, wt, ts, xm, offs, out_0, out_1)
         table_block(0, HALF, N, "A0")
         scatter(0, 0, HALF)
         xm_block(1, nc.scalar.copy, "rec2")
-        w_turn1 = bank("B0", "w_turn1")
-        turn(w_bf, 1, w_turn1)
-        slot_major_half(1, w_turn1, "root3")
         scatter(0, HALF, N)
         table_block(1, 0, N, "A1")
         scatter(1, 0, N)

@@ -25,7 +25,7 @@ CHUNKS = N // CHUNK
 HALF = N // 2
 DIRECT = 2
 WINDOWS = 3
-X_SPLIT = 108
+X_SPLIT = 84
 VECTOR_MEMSETS = 2
 
 
@@ -33,7 +33,6 @@ def tile_attend_gcau_wx_ts_kernel(tc, xT, wT, y, wt, ts, xm, offs, out_0, out_1)
     nc = tc.nc
     with ExitStack() as ctx:
         sb = ctx.enter_context(tc.tile_pool(name="sb", bufs=1))
-        reuse = ctx.enter_context(tc.tile_pool(name="reuse", bufs=1))
         ps = ctx.enter_context(tc.psum_pool(name="ps", bufs=1))
 
         def tile(name, shape, dtype):
@@ -70,14 +69,10 @@ def tile_attend_gcau_wx_ts_kernel(tc, xT, wT, y, wt, ts, xm, offs, out_0, out_1)
             if t == 0:
                 nc.sync.dma_start(offsets[:], offs)
                 nc.sync.dma_start(out=wt_sb[:], in_=wt[0].rearrange("(p t) o -> p (t o)", t=PACK))
-        x_rows = xT[0].rearrange("(p j) r -> p j r", j=PACK)
-        x_raw = [tile(f"x_raw{k}", [P, PACK, R // 2], F32) for k in range(2)]
-        for k in range(2):
-            nc.sync.dma_start(out=x_raw[k][:], in_=x_rows[:, :, k * R // 2 : (k + 1) * R // 2])
-        y_rows = y[0].rearrange("(p t) i -> p t i", t=PACK)
-        y_sb = [tile(f"y_sb{k}", [P, PACK, HALF], F32) for k in range(2)]
-        for k in range(2):
-            nc.sync.dma_start(out=y_sb[k][:], in_=y_rows[:, :, k * HALF : (k + 1) * HALF])
+        x_raw = tile("x_raw", [P, PACK, R], F32)
+        nc.sync.dma_start(out=x_raw[:], in_=xT[0].rearrange("(p j) r -> p j r", j=PACK))
+        y_sb = tile("y_sb", [P, PACK, N], F32)
+        nc.sync.dma_start(out=y_sb[:], in_=y[0].rearrange("(p t) i -> p t i", t=PACK))
         xm_raw = tile("xm_raw", [P, PACK, D], F32)
         nc.sync.dma_start(out=xm_raw[:], in_=xm[0].rearrange("(p t) d -> p t d", t=PACK))
 
@@ -88,11 +83,12 @@ def tile_attend_gcau_wx_ts_kernel(tc, xT, wT, y, wt, ts, xm, offs, out_0, out_1)
         ident = tile("ident", [P, P], F32)
         make_identity(nc, ident[:])
 
-        windows = [tile(f"window{m}", [P, T], F32) for m in range(VECTOR_MEMSETS)]
-        for m in range(VECTOR_MEMSETS):
-            nc.vector.memset(windows[m][:].bitcast(I32), 0)
+        windows = [tile(f"window{m}", [P, T], F32) for m in range(WINDOWS)]
+        for m in range(WINDOWS):
+            engine = nc.vector if m < VECTOR_MEMSETS else nc.gpsimd
+            engine.memset(windows[m][:].bitcast(I32), 0)
 
-        ts_win = reuse.tile([P, T], F32, name="ts_win", offset=0, align_bytes=64)
+        ts_win = tile("ts_win", [P, T], F32)
         for g in range(PACK):
             spread = bank(f"A{g}", f"spread{g}")
             for e in range(PACK):
@@ -106,26 +102,28 @@ def tile_attend_gcau_wx_ts_kernel(tc, xT, wT, y, wt, ts, xm, offs, out_0, out_1)
         ts_slot = tile("ts_slot", [P, CHUNKS], F32)
         factor = tile("factor", [P, PACK, N], F32)
 
-        def item_scales():
+        def gather_scales():
             nc.vector.tensor_copy(ts_all[:], ts_win[:].indirect(offsets[:]))
+
+        def item_scales():
             ts_turn = bank("C0", "ts_turn")
             for j in range(DIRECT, CHUNKS):
                 nc.tensor.transpose(ts_turn[:, j * P : (j + 1) * P], ts_all[:, j * P : (j + 1) * P], ident[:])
             nc.scalar.copy(out=ts_slot[:, DIRECT:CHUNKS], in_=ts_turn[:, DIRECT * P : N : P])
+
+        def row_factors():
             for t in range(PACK):
                 nc.scalar.activation(out=factor[:, t, :], in_=ts_all[:], func=ACT.Copy, scale=wt_sb[:, t : t + 1])
 
-        x_bf = reuse.tile([P, R * PACK], BF16, name="x_bf", offset=2 * N * PACK, align_bytes=64)
         x_q = operand("x")
 
-        def x_part(copy, lo, hi):
-            k, first = divmod(lo, P // 2)
+        def x_part(x_bf, copy, lo, hi):
             copy(
-                out=x_bf[:].rearrange("p (t m j) -> p m j t", t=PACK, j=PACK)[:, lo:hi],
-                in_=x_raw[k][:].rearrange("p j (m t) -> p m j t", t=PACK)[:, first : first + hi - lo],
+                out=x_bf[:].rearrange("p (t m j) -> p m j t", t=PACK, j=PACK)[:, :, :, lo:hi],
+                in_=x_raw[:].rearrange("p j (m t) -> p m j t", t=PACK)[:, :, :, lo:hi],
             )
 
-        w_bf = reuse.tile([P, N * PACK], BF16, name="w_bf", offset=0, align_bytes=64)
+        w_bf = sb.tile([P, N * PACK], BF16, name="w_bf", tag="ts_win", align_bytes=64)
         w_q = operand("w")
         wi_q = operand("wi")
 
@@ -149,20 +147,23 @@ def tile_attend_gcau_wx_ts_kernel(tc, xT, wT, y, wt, ts, xm, offs, out_0, out_1)
             cols = slice(u * D // 2, (u + 1) * D // 2)
             nc.vector.quantize_mx(out=wi_q[0][:, cols].bitcast(E4M3), scales=wi_q[1][:, cols], in_=half_bf[:])
 
+        picked = tile("picked", [P, 2, N], BF16)
+        for t in range(2):
+            nc.vector.tensor_copy(picked[:, t, :], planes[t][:].indirect(offsets[:]))
+        gather_scales()
+        nc.scalar.copy(out=w_bf[:].rearrange("p (i t) -> p i t", t=PACK)[:, :, 0:2], in_=picked[:].rearrange("p t i -> p i t"))
         item_scales()
-        for t in range(PACK):
+        row_factors()
+        for t in range(2, PACK):
             nc.vector.tensor_copy(w_bf[:, t : N * PACK : PACK], planes[t][:].indirect(offsets[:]))
-            if t == 1:
-                w_turn0 = bank("B0", "w_turn0")
-                turn(w_bf, 0, w_turn0)
-                slot_major_half(0, w_turn0, "wi_bf0")
 
         scores = [bank(f"A{j}", f"scores{j}") for j in range(CHUNKS)]
         quantize(w_q, w_bf, E4M3, 0, N)
-        x_part(nc.scalar.copy, 0, P // 2)
-        x_part(nc.vector.tensor_copy, P // 2, X_SPLIT)
-        x_part(nc.scalar.copy, X_SPLIT, P)
-        quantize(x_q, x_bf, E4M3, 0, R)
+        x_bf = sb.tile([P, R * PACK], BF16, name="x_bf", tag="wt_sb", align_bytes=64)
+        x_part(x_bf, nc.vector.tensor_copy, 0, 2)
+        x_part(x_bf, nc.scalar.copy, 2, 4)
+        quantize(x_q, x_bf, E4M3, 0, R // 2)
+        quantize(x_q, x_bf, E4M3, R // 2, R)
         for j in range(CHUNKS):
             slots = slice(j * CHUNK, (j + 1) * CHUNK)
             if j < DIRECT:
@@ -170,11 +171,9 @@ def tile_attend_gcau_wx_ts_kernel(tc, xT, wT, y, wt, ts, xm, offs, out_0, out_1)
                     mx(scores[j][:, t * CHUNK : (t + 1) * CHUNK], x_q, E4M3, slice(t * P, (t + 1) * P), w_q, E4M3, slots)
             else:
                 mx(scores[j][:], w_q, E4M3, slots, x_q, E4M3, slice(0, R))
-        w_turn1 = bank("C1", "w_turn1")
-        turn(w_bf, 1, w_turn1)
-        slot_major_half(1, w_turn1, "wi_bf1")
-        windows.append(reuse.tile([P, T], F32, name="window2", offset=0, align_bytes=64))
-        nc.gpsimd.memset(windows[2][:].bitcast(I32), 0)
+        w_turn0 = bank("C1", "w_turn0")
+        turn(w_bf, 0, w_turn0)
+        slot_major_half(0, w_turn0, "x_raw")
 
         xm_q = operand("xm")
 
@@ -213,7 +212,7 @@ def tile_attend_gcau_wx_ts_kernel(tc, xT, wT, y, wt, ts, xm, offs, out_0, out_1)
             return turned
 
         def residual(j, scaled_chunk):
-            y_chunk = y_sb[j // 2][:, :, j % 2 * CHUNK : (j % 2 + 1) * CHUNK]
+            y_chunk = y_sb[:, :, j * CHUNK : (j + 1) * CHUNK]
             nc.vector.tensor_tensor(q[j][:], scaled_chunk[:].rearrange("p (t i) -> p t i", t=PACK), y_chunk, SUB)
 
         def square(j):
@@ -274,16 +273,19 @@ def tile_attend_gcau_wx_ts_kernel(tc, xT, wT, y, wt, ts, xm, offs, out_0, out_1)
             if hi == N:
                 nc.sync.dma_start(out=out_0[m * P : (m + 1) * P, :], in_=windows[m % WINDOWS][:])
 
-        table_block(0, 0, HALF, "C1")
+        table_block(0, 0, HALF, "A0")
         finish(2)
         finish(3)
         quantize_h(2)
         quantize_h(3)
-        table_block(0, HALF, N, "A0")
+        table_block(0, HALF, N, "A1")
         scatter(0, 0, HALF)
         xm_block(1, nc.scalar.copy, "rec2")
+        w_turn1 = bank("B0", "w_turn1")
+        turn(w_bf, 1, w_turn1)
+        slot_major_half(1, w_turn1, "root3")
         scatter(0, HALF, N)
-        table_block(1, 0, N, "A1")
+        table_block(1, 0, N, "A2")
         scatter(1, 0, N)
         xm_block(2, nc.scalar.copy, "rec3")
 
@@ -296,7 +298,7 @@ def tile_attend_gcau_wx_ts_kernel(tc, xT, wT, y, wt, ts, xm, offs, out_0, out_1)
         quantize(hi_q, hi_bf, E5M2, 0, R)
         xm_block(3, nc.scalar.copy, "dw0")
         for m in range(2, D // P):
-            table_block(m, 0, N, f"A{m}")
+            table_block(m, 0, N, f"A{(m + 1) % 4}")
             scatter(m, 0, N)
 
         gx = tile("gx", [P, R // P, D], F32)

@@ -25,6 +25,7 @@ CHUNKS = N // CHUNK
 HALF = N // 2
 DIRECT = 2
 WINDOWS = 3
+VSQ = (1,)
 X_SPLIT = 84
 VECTOR_MEMSETS = 2
 
@@ -167,8 +168,9 @@ def tile_attend_gcau_wx_ts_kernel(tc, xT, wT, y, wt, ts, xm, offs, out_0, out_1)
         for j in range(CHUNKS):
             slots = slice(j * CHUNK, (j + 1) * CHUNK)
             if j < DIRECT:
-                for t in range(PACK):
-                    mx(scores[j][:, t * CHUNK : (t + 1) * CHUNK], x_q, E4M3, slice(t * P, (t + 1) * P), w_q, E4M3, slots)
+                for e in range(2):
+                    t = 2 * j + e
+                    mx(scores[j][:, e * HALF : (e + 1) * HALF], x_q, E4M3, slice(t * P, (t + 1) * P), w_q, E4M3, slice(0, HALF))
             else:
                 mx(scores[j][:], w_q, E4M3, slots, x_q, E4M3, slice(0, R))
         w_turn0 = bank("C1", "w_turn0")
@@ -177,117 +179,114 @@ def tile_attend_gcau_wx_ts_kernel(tc, xT, wT, y, wt, ts, xm, offs, out_0, out_1)
 
         xm_q = operand("xm")
 
-        def xm_block(m, copy, tag):
-            xm_bf = sb.tile([P, P * PACK], BF16, name=f"xm_bf{m}", tag=tag, align_bytes=64)
+        def xm_block(lo, hi, copy, tag):
+            xm_bf = sb.tile([P, (hi - lo) * PACK], BF16, name=f"xm_bf{lo}", tag=tag, align_bytes=64)
             copy(
                 out=xm_bf[:].rearrange("p (c e t) -> p c t e", e=PACK, t=PACK),
-                in_=xm_raw[:, :, m * P : (m + 1) * P].rearrange("p t (c e) -> p c t e", e=PACK),
+                in_=xm_raw[:, :, lo:hi].rearrange("p t (c e) -> p c t e", e=PACK),
             )
-            cols = slice(m * P, (m + 1) * P)
-            nc.vector.quantize_mx(out=xm_q[0][:, cols].bitcast(E4M3), scales=xm_q[1][:, cols], in_=xm_bf[:])
+            nc.vector.quantize_mx(out=xm_q[0][:, lo:hi].bitcast(E4M3), scales=xm_q[1][:, lo:hi], in_=xm_bf[:])
 
         h_bf = tile("h_bf", [P, N * PACK], BF16)
         h_q = operand("h")
         nc.gpsimd.memset(h_q[0][:, HALF:N].bitcast(I32), 0)
         nc.gpsimd.memset(h_q[1][:, HALF:N].bitcast(I32), 0)
         a = [tile(f"a{j}", [P, R], F32) for j in range(CHUNKS)]
-        q = [tile(f"q{j}", [P, PACK, CHUNK], F32) for j in range(CHUNKS)]
-        sq = [tile(f"sq{j}", [P, PACK, CHUNK], F32) for j in range(CHUNKS)]
-        root = [tile(f"root{j}", [P, PACK, CHUNK], F32) for j in range(CHUNKS)]
-        rec = [tile(f"rec{j}", [P, PACK, CHUNK], F32) for j in range(CHUNKS)]
-        num = [tile(f"num{j}", [P, PACK, CHUNK], F32) for j in range(CHUNKS)]
-        turned_tag = {2: "B1", 3: "B0"}
+        q = [tile(f"q{k}", [P, PACK, HALF], F32) for k in range(2)]
+        sq = [tile(f"sq{j}", [P, R], F32) for j in range(CHUNKS)]
+        root = [tile(f"root{j}", [P, R], F32) for j in range(CHUNKS)]
+        rec = [tile(f"rec{k}", [P, PACK, HALF], F32) for k in range(2)]
+
+        def chunk_of(halves, j):
+            if j < DIRECT:
+                return halves[0][:, 2 * j : 2 * j + 2, :]
+            return halves[1][:, :, (j - DIRECT) * CHUNK : (j - DIRECT + 1) * CHUNK]
+
+        def shaped(flat, j):
+            return flat[:].rearrange("p (t i) -> p t i", t=2 if j < DIRECT else PACK)
 
         def times_ts(j):
             if j < DIRECT:
-                ts_chunk = ts_all[:, j * CHUNK : (j + 1) * CHUNK].unsqueeze(1).to_broadcast([P, PACK, CHUNK])
-                nc.vector.tensor_tensor(
-                    a[j][:].rearrange("p (t i) -> p t i", t=PACK), scores[j][:].rearrange("p (t i) -> p t i", t=PACK), ts_chunk, MULT
-                )
+                nc.vector.tensor_tensor(shaped(a[j], j), shaped(scores[j], j), ts_all[:, 0:HALF].unsqueeze(1).to_broadcast([P, 2, HALF]), MULT)
                 return a[j]
             nc.scalar.activation(out=a[j][:], in_=scores[j][:], func=ACT.Copy, scale=ts_slot[:, j : j + 1])
-            turned = bank(turned_tag[j], f"turned{j}")
+            turned = bank(f"B{j - DIRECT}", f"turned{j}")
             for t in range(PACK):
                 nc.tensor.transpose(turned[:, t * P : (t + 1) * P], a[j][:, t * P : (t + 1) * P], ident[:])
             return turned
 
-        def residual(j, scaled_chunk):
-            y_chunk = y_sb[:, :, j * CHUNK : (j + 1) * CHUNK]
-            nc.vector.tensor_tensor(q[j][:], scaled_chunk[:].rearrange("p (t i) -> p t i", t=PACK), y_chunk, SUB)
+        def residual(j, scaled):
+            y_halves = [y_sb[:, :, k * HALF : (k + 1) * HALF] for k in range(2)]
+            nc.vector.tensor_tensor(chunk_of(q, j), shaped(scaled, j), chunk_of(y_halves, j), SUB)
 
-        def square(j):
-            nc.scalar.activation(out=sq[j][:], in_=q[j][:], func=ACT.Square)
+        def inverse(k):
+            pair = (2 * k, 2 * k + 1)
+            for j in pair:
+                if j in VSQ:
+                    nc.vector.tensor_tensor(shaped(sq[j], j), chunk_of(q, j), chunk_of(q, j), MULT)
+                else:
+                    nc.scalar.activation(out=shaped(sq[j], j), in_=chunk_of(q, j), func=ACT.Square)
+            for j in pair:
+                nc.scalar.activation(out=root[j][:], in_=sq[j][:], func=ACT.Abs_reciprocal_sqrt, bias=ones[:])
+            for j in pair:
+                nc.scalar.activation(out=chunk_of(rec, j), in_=shaped(root[j], j), func=ACT.Square)
 
-        def inverse_root(j):
-            nc.scalar.activation(out=root[j][:], in_=sq[j][:], func=ACT.Abs_reciprocal_sqrt, bias=ones[:])
+        def numerator(k):
+            num = sb.tile([P, PACK, HALF], F32, name=f"num{k}", tag="num", align_bytes=64)
+            nc.vector.tensor_tensor(num[:], q[k][:], factor[:, :, k * HALF : (k + 1) * HALF], MULT)
+            return num
 
-        def inverse(j):
-            nc.scalar.activation(out=rec[j][:], in_=root[j][:], func=ACT.Square)
-
-        def numerator(j):
-            nc.vector.tensor_tensor(num[j][:], q[j][:], factor[:, :, j * CHUNK : (j + 1) * CHUNK], MULT)
-
-        def finish(j):
+        def finish(k, num):
             nc.vector.tensor_tensor(
-                h_bf[:, j * CHUNK * PACK : (j + 1) * CHUNK * PACK].rearrange("p (c e t) -> p c t e", e=2, t=PACK),
-                num[j][:].rearrange("p t (c e) -> p c t e", e=2),
-                rec[j][:].rearrange("p t (c e) -> p c t e", e=2),
+                h_bf[:, k * HALF * PACK : (k + 1) * HALF * PACK].rearrange("p (c e t) -> p c t e", e=2, t=PACK),
+                num[:].rearrange("p t (c e) -> p c t e", e=2),
+                rec[k][:].rearrange("p t (c e) -> p c t e", e=2),
                 MULT,
             )
 
-        def quantize_h(j):
-            quantize(h_q, h_bf, E5M2, j * CHUNK, (j + 1) * CHUNK)
-
-        scaled = [times_ts(j) for j in range(CHUNKS)]
-        for j in range(CHUNKS):
-            residual(j, scaled[j])
-        square(0)
-        square(1)
-        inverse_root(0)
-        inverse_root(1)
-        inverse(0)
-        square(2)
-        inverse(1)
-        square(3)
-        inverse_root(2)
-        inverse_root(3)
-        inverse(2)
-        inverse(3)
-        for j in range(CHUNKS):
-            numerator(j)
-        finish(0)
-        finish(1)
-        xm_block(0, nc.vector.tensor_copy, "a1")
-        quantize_h(0)
-        quantize_h(1)
-
-        dw = [tile(f"dw{m}", [P, N], F32) for m in range(D // P)]
-
-        def table_block(m, lo, hi, tag):
-            acc = bank(tag, f"dw_acc{m}_{lo}")
+        def table_product(m, tag, name):
+            acc = bank(tag, name)
             mx(acc[:], xm_q, E4M3, slice(m * P, (m + 1) * P), h_q, E5M2, slice(0, N))
-            nc.scalar.copy(out=dw[m][:, lo:hi], in_=acc[:, lo:hi])
+            return acc
 
-        def scatter(m, lo, hi):
-            nc.vector.tensor_copy(windows[m % WINDOWS][:].indirect(offsets[:, lo // 16 : hi // 16]), dw[m][:, lo:hi])
+        def to_sbuf(acc, lo, hi, name, tag):
+            dw = sb.tile([P, hi - lo], F32, name=name, tag=tag, align_bytes=64)
+            nc.scalar.copy(out=dw[:], in_=acc[:, lo:hi])
+            return dw
+
+        def scatter(m, dw, lo, hi):
+            nc.vector.tensor_copy(windows[m % WINDOWS][:].indirect(offsets[:, lo // 16 : hi // 16]), dw[:])
             if hi == N:
                 nc.sync.dma_start(out=out_0[m * P : (m + 1) * P, :], in_=windows[m % WINDOWS][:])
 
-        table_block(0, 0, HALF, "A0")
-        finish(2)
-        finish(3)
-        quantize_h(2)
-        quantize_h(3)
-        table_block(0, HALF, N, "A1")
-        scatter(0, 0, HALF)
-        xm_block(1, nc.scalar.copy, "rec2")
-        w_turn1 = bank("B0", "w_turn1")
+        scaled = [times_ts(j) for j in range(CHUNKS)]
+        residual(0, scaled[0])
+        residual(1, scaled[1])
+        inverse(0)
+        residual(2, scaled[2])
+        residual(3, scaled[3])
+        num0 = numerator(0)
+        xm_block(0, 2 * P, nc.scalar.copy, "sq0")
+        finish(0, num0)
+        quantize(h_q, h_bf, E5M2, 0, HALF)
+        early0 = table_product(0, "A0", "dw_early0")
+        dw_early0 = to_sbuf(early0, 0, HALF, "dw_early0", "dw_early0")
+        early1 = table_product(1, "A1", "dw_early1")
+        inverse(1)
+        num1 = numerator(1)
+        scatter(0, dw_early0, 0, HALF)
+        finish(1, num1)
+        dw_early1 = to_sbuf(early1, 0, HALF, "dw_early1", "num")
+        quantize(h_q, h_bf, E5M2, HALF, N)
+        scatter(1, dw_early1, 0, HALF)
+        for m in range(2):
+            late = table_product(m, f"A{m + 2}", f"dw_late{m}")
+            scatter(m, to_sbuf(late, HALF, N, f"dw_late{m}", f"dw_late{m}"), HALF, N)
+
+        xm_block(2 * P, D, nc.scalar.copy, "root2")
+        w_turn1 = bank("B1", "w_turn1")
         turn(w_bf, 1, w_turn1)
         slot_major_half(1, w_turn1, "root3")
-        scatter(0, HALF, N)
-        table_block(1, 0, N, "A2")
-        scatter(1, 0, N)
-        xm_block(2, nc.scalar.copy, "rec3")
 
         hi_bf = tile("hi_bf", [P, R * PACK], BF16)
         for u in range(2):
@@ -296,15 +295,14 @@ def tile_attend_gcau_wx_ts_kernel(tc, xT, wT, y, wt, ts, xm, offs, out_0, out_1)
             lay_out(hi_bf, u, h_turn)
         hi_q = operand("hi")
         quantize(hi_q, hi_bf, E5M2, 0, R)
-        xm_block(3, nc.scalar.copy, "dw0")
         for m in range(2, D // P):
-            table_block(m, 0, N, f"A{(m + 1) % 4}")
-            scatter(m, 0, N)
+            whole = table_product(m, ("C1", "A2")[m - 2], f"dw_acc{m}")
+            scatter(m, to_sbuf(whole, 0, N, f"dw{m}", f"dw{m}"), 0, N)
 
         gx = tile("gx", [P, R // P, D], F32)
         gx_rows = out_1[0].rearrange("(b p) d -> p b d", p=P)
         for b in range(R // P):
-            acc = bank(("B1", "B0", "C0", "C1")[b], f"gx_acc{b}")
+            acc = bank(("B0", "B1", "A0", "A1")[b], f"gx_acc{b}")
             mx(acc[:], hi_q, E5M2, slice(b * P, (b + 1) * P), wi_q, E4M3, slice(0, D))
             nc.scalar.copy(
                 out=gx[:, b, :].rearrange("r (p u e) -> r p u e", u=2, e=2),

@@ -145,6 +145,9 @@ def tile_attend_gcau_wx_ts_kernel(tc, xT, wT, y, wt, ts, xm, offs, out_0, out_1)
                 out=half_bf[:].rearrange("q (p e s) -> q p e s", e=2, s=PACK),
                 in_=src_bank[:].bitcast(BF16).rearrange("q (s p e) -> q p e s", s=PACK, e=2),
             )
+            return half_bf
+
+        def quantize_wi(u, half_bf):
             cols = slice(u * D // 2, (u + 1) * D // 2)
             nc.vector.quantize_mx(out=wi_q[0][:, cols].bitcast(E4M3), scales=wi_q[1][:, cols], in_=half_bf[:])
 
@@ -175,7 +178,7 @@ def tile_attend_gcau_wx_ts_kernel(tc, xT, wT, y, wt, ts, xm, offs, out_0, out_1)
                 mx(scores[j][:], w_q, E4M3, slots, x_q, E4M3, slice(0, R))
         w_turn0 = bank("C1", "w_turn0")
         turn(w_bf, 0, w_turn0)
-        slot_major_half(0, w_turn0, "x_raw")
+        wi_bf0 = slot_major_half(0, w_turn0, "x_raw")
 
         xm_q = operand("xm")
 
@@ -286,17 +289,18 @@ def tile_attend_gcau_wx_ts_kernel(tc, xT, wT, y, wt, ts, xm, offs, out_0, out_1)
         xm_block(2 * P, D, nc.scalar.copy, "root2")
         w_turn1 = bank("B1", "w_turn1")
         turn(w_bf, 1, w_turn1)
-        slot_major_half(1, w_turn1, "root3")
+        quantize_wi(0, wi_bf0)
+        quantize_wi(1, slot_major_half(1, w_turn1, "root3"))
 
         hi_bf = tile("hi_bf", [P, R * PACK], BF16)
         for u in range(2):
-            h_turn = bank(f"C{u}", f"h_turn{u}")
+            h_turn = bank(f"A{u + 2}", f"h_turn{u}")
             turn(h_bf, u, h_turn)
             lay_out(hi_bf, u, h_turn)
         hi_q = operand("hi")
         quantize(hi_q, hi_bf, E5M2, 0, R)
         for m in range(2, D // P):
-            whole = table_product(m, ("C1", "A2")[m - 2], f"dw_acc{m}")
+            whole = table_product(m, ("A2", "C0")[m - 2], f"dw_acc{m}")
             scatter(m, to_sbuf(whole, 0, N, f"dw{m}", f"dw{m}"), 0, N)
 
         gx = tile("gx", [P, R // P, D], F32)

@@ -269,47 +269,49 @@ def tile_attend_gcau_wx_ts_kernel(tc, xT, wT, y, wt, ts, xm, offs, out_0, out_1)
         residual(2, scaled[2])
         residual(3, scaled[3])
         num0 = numerator(0)
-        xm_block(0, 2 * P, nc.scalar.copy, "sq0")
+        xm_block(0, P, nc.vector.tensor_copy, "a1")
         finish(0, num0)
         quantize(h_q, h_bf, E5M2, 0, HALF)
-        early0 = table_product(0, "A0", "dw_early0")
-        dw_early0 = to_sbuf(early0, 0, HALF, "dw_early0", "dw_early0")
-        early1 = table_product(1, "A1", "dw_early1")
+        early = table_product(0, "A0", "dw_early")
         inverse(1)
-        num1 = numerator(1)
-        scatter(0, dw_early0, 0, HALF)
-        finish(1, num1)
-        dw_early1 = to_sbuf(early1, 0, HALF, "dw_early1", "num")
+        finish(1, numerator(1))
+        dw_early = to_sbuf(early, 0, HALF, "dw_early", "root3")
         quantize(h_q, h_bf, E5M2, HALF, N)
-        scatter(1, dw_early1, 0, HALF)
-        for m in range(2):
-            late = table_product(m, f"A{m + 2}", f"dw_late{m}")
-            scatter(m, to_sbuf(late, HALF, N, f"dw_late{m}", f"dw_late{m}"), HALF, N)
-
-        xm_block(2 * P, D, nc.scalar.copy, "root2")
+        scatter(0, dw_early, 0, HALF)
+        late = table_product(0, "A1", "dw_late")
+        scatter(0, to_sbuf(late, HALF, N, "dw_late", "dw_late"), HALF, N)
         w_turn1 = bank("B1", "w_turn1")
         turn(w_bf, 1, w_turn1)
         quantize_wi(0, wi_bf0)
-        quantize_wi(1, slot_major_half(1, w_turn1, "root3"))
+        quantize_wi(1, slot_major_half(1, w_turn1, "root2"))
 
         hi_bf = tile("hi_bf", [P, R * PACK], BF16)
         for u in range(2):
-            h_turn = bank(f"A{u + 2}", f"h_turn{u}")
+            h_turn = bank(("C0", "C1")[u], f"h_turn{u}")
             turn(h_bf, u, h_turn)
             lay_out(hi_bf, u, h_turn)
+        xm_block(P, 2 * P, nc.scalar.copy, "num")
+        xm_block(2 * P, D, nc.scalar.copy, "rec1")
         hi_q = operand("hi")
         quantize(hi_q, hi_bf, E5M2, 0, R)
-        for m in range(2, D // P):
-            whole = table_product(m, ("A2", "C0")[m - 2], f"dw_acc{m}")
-            scatter(m, to_sbuf(whole, 0, N, f"dw{m}", f"dw{m}"), 0, N)
 
         gx = tile("gx", [P, R // P, D], F32)
         gx_rows = out_1[0].rearrange("(b p) d -> p b d", p=P)
-        for b in range(R // P):
-            acc = bank(("B0", "B1", "A0", "A1")[b], f"gx_acc{b}")
+
+        def row_block(b, tag):
+            acc = bank(tag, f"gx_acc{b}")
             mx(acc[:], hi_q, E5M2, slice(b * P, (b + 1) * P), wi_q, E4M3, slice(0, D))
             nc.scalar.copy(
                 out=gx[:, b, :].rearrange("r (p u e) -> r p u e", u=2, e=2),
                 in_=acc[:].rearrange("r (u p e) -> r p u e", u=2, e=2),
             )
             nc.scalar.dma_start(out=gx_rows[:, b, :], in_=gx[:, b, :])
+
+        def whole_block(m, tag):
+            scatter(m, to_sbuf(table_product(m, tag, f"dw_acc{m}"), 0, N, f"dw{m}", f"dw{m}"), 0, N)
+
+        whole_block(1, "C0")
+        whole_block(2, "C1")
+        for b in range(R // P):
+            row_block(b, ("B0", "B1", "A2", "A3")[b])
+        whole_block(3, "B0")

@@ -20,13 +20,13 @@ ACT = mybir.ActivationFunctionType
 
 P = 128
 PACK = 4
-CHUNK = 128
-CHUNKS = N // CHUNK
 HALF = N // 2
+CHUNK = 128
+CHUNKS = 4
 DIRECT = 2
+SCORE_ORDER = (0, 1, 2, 3)
+VECTOR_SQUARES = (3,)
 WINDOWS = 3
-VSQ = (1,)
-X_SPLIT = 84
 VECTOR_MEMSETS = 2
 
 
@@ -36,8 +36,8 @@ def tile_attend_gcau_wx_ts_kernel(tc, xT, wT, y, wt, ts, xm, offs, out_0, out_1)
         sb = ctx.enter_context(tc.tile_pool(name="sb", bufs=1))
         ps = ctx.enter_context(tc.psum_pool(name="ps", bufs=1))
 
-        def tile(name, shape, dtype):
-            return sb.tile(shape, dtype, name=name, tag=name, align_bytes=64)
+        def tile(name, shape, dtype, buffer=None):
+            return sb.tile(shape, dtype, name=name, tag=buffer or name, align_bytes=64)
 
         def bank(tag, name):
             return ps.tile([P, 512], F32, name=name, tag=tag)
@@ -45,8 +45,8 @@ def tile_attend_gcau_wx_ts_kernel(tc, xT, wT, y, wt, ts, xm, offs, out_0, out_1)
         def operand(name):
             return tile(name + "_codes", [P, 512], U32), tile(name + "_scales", [P, 512], U8)
 
-        def quantize(op, src, fmt, lo, hi):
-            nc.vector.quantize_mx(out=op[0][:, lo:hi].bitcast(fmt), scales=op[1][:, lo:hi], in_=src[:, PACK * lo : PACK * hi])
+        def quantize(op, lo, hi, src, fmt):
+            nc.vector.quantize_mx(out=op[0][:, lo:hi].bitcast(fmt), scales=op[1][:, lo:hi], in_=src)
 
         def mx(out, lhs, lhs_fmt, lhs_cols, rhs, rhs_fmt, rhs_cols):
             nc.tensor.matmul_mx(
@@ -63,19 +63,13 @@ def tile_attend_gcau_wx_ts_kernel(tc, xT, wT, y, wt, ts, xm, offs, out_0, out_1)
         ts_cols = tile("ts_cols", [P, T // P], F32)
         nc.sync.dma_start(out=ts_cols[:], in_=ts[0].rearrange("(p c) -> p c", p=P))
         wt_sb = tile("wt_sb", [P, PACK], F32)
-        planes = [tile(f"plane{t}", [P, T], F32) for t in range(PACK)]
         w_rows = wT.rearrange("(p t) c -> p t c", t=PACK)
-        for t in range(PACK):
+        planes = {t: tile(f"plane{t}", [P, T], F32) for t in (2, 0, 1)}
+        nc.sync.dma_start(out=planes[2][:], in_=w_rows[:, 2, :])
+        nc.sync.dma_start(offsets[:], offs)
+        nc.sync.dma_start(out=wt_sb[:], in_=wt[0].rearrange("(p t) o -> p (t o)", t=PACK))
+        for t in range(2):
             nc.sync.dma_start(out=planes[t][:], in_=w_rows[:, t, :])
-            if t == 0:
-                nc.sync.dma_start(offsets[:], offs)
-                nc.sync.dma_start(out=wt_sb[:], in_=wt[0].rearrange("(p t) o -> p (t o)", t=PACK))
-        x_raw = tile("x_raw", [P, PACK, R], F32)
-        nc.sync.dma_start(out=x_raw[:], in_=xT[0].rearrange("(p j) r -> p j r", j=PACK))
-        y_sb = tile("y_sb", [P, PACK, N], F32)
-        nc.sync.dma_start(out=y_sb[:], in_=y[0].rearrange("(p t) i -> p t i", t=PACK))
-        xm_raw = tile("xm_raw", [P, PACK, D], F32)
-        nc.sync.dma_start(out=xm_raw[:], in_=xm[0].rearrange("(p t) d -> p t d", t=PACK))
 
         ones = tile("ones", [P, 1], F32)
         nc.vector.memset(ones[:], 1.0)
@@ -84,6 +78,9 @@ def tile_attend_gcau_wx_ts_kernel(tc, xT, wT, y, wt, ts, xm, offs, out_0, out_1)
         ident = tile("ident", [P, P], F32)
         make_identity(nc, ident[:])
 
+        h_q = operand("h")
+        nc.gpsimd.memset(h_q[0][:, HALF:N].bitcast(I32), 0)
+        nc.gpsimd.memset(h_q[1][:, HALF:N].bitcast(I32), 0)
         windows = [tile(f"window{m}", [P, T], F32) for m in range(WINDOWS)]
         for m in range(WINDOWS):
             engine = nc.vector if m < VECTOR_MEMSETS else nc.gpsimd
@@ -103,102 +100,97 @@ def tile_attend_gcau_wx_ts_kernel(tc, xT, wT, y, wt, ts, xm, offs, out_0, out_1)
         ts_slot = tile("ts_slot", [P, CHUNKS], F32)
         factor = tile("factor", [P, PACK, N], F32)
 
-        def gather_scales():
-            nc.vector.tensor_copy(ts_all[:], ts_win[:].indirect(offsets[:]))
-
-        def item_scales():
-            ts_turn = bank("C0", "ts_turn")
-            for j in range(DIRECT, CHUNKS):
-                nc.tensor.transpose(ts_turn[:, j * P : (j + 1) * P], ts_all[:, j * P : (j + 1) * P], ident[:])
-            nc.scalar.copy(out=ts_slot[:, DIRECT:CHUNKS], in_=ts_turn[:, DIRECT * P : N : P])
-
-        def row_factors():
-            for t in range(PACK):
-                nc.scalar.activation(out=factor[:, t, :], in_=ts_all[:], func=ACT.Copy, scale=wt_sb[:, t : t + 1])
-
         x_q = operand("x")
-
-        def x_part(x_bf, copy, lo, hi):
-            copy(
-                out=x_bf[:].rearrange("p (t m j) -> p m j t", t=PACK, j=PACK)[:, :, :, lo:hi],
-                in_=x_raw[:].rearrange("p j (m t) -> p m j t", t=PACK)[:, :, :, lo:hi],
-            )
-
-        w_bf = sb.tile([P, N * PACK], BF16, name="w_bf", tag="ts_win", align_bytes=64)
+        w_bf = tile("w_bf", [P, N * PACK], BF16)
         w_q = operand("w")
         wi_q = operand("wi")
+        nc.vector.tensor_copy(w_bf[:, 2 : N * PACK : PACK], planes[2][:].indirect(offsets[:]))
+        planes[3] = tile("plane3", [P, T], F32, "plane2")
+        nc.sync.dma_start(out=planes[3][:], in_=w_rows[:, 3, :])
+        nc.vector.tensor_copy(ts_all[:], ts_win[:].indirect(offsets[:]))
+        ts_turn = bank("C0", "ts_turn")
+        for j in range(DIRECT, CHUNKS):
+            nc.tensor.transpose(ts_turn[:, j * P : (j + 1) * P], ts_all[:, j * P : (j + 1) * P], ident[:])
+        for t in range(PACK):
+            nc.scalar.activation(out=factor[:, t, :], in_=ts_all[:], func=ACT.Copy, scale=wt_sb[:, t : t + 1])
+        nc.scalar.copy(out=ts_slot[:, DIRECT:CHUNKS], in_=ts_turn[:, DIRECT * P : N : P])
+        picked = tile("picked", [P, 2, N], BF16, "ts_win")
+        for t in range(2):
+            nc.vector.tensor_copy(picked[:, t, :], planes[t][:].indirect(offsets[:]))
+        nc.scalar.copy(out=w_bf[:].rearrange("p (i t) -> p i t", t=PACK)[:, :, 0:2], in_=picked[:].rearrange("p t i -> p i t"))
 
+        def quantize_wi(u, wi_bf):
+            quantize(wi_q, u * D // 2, (u + 1) * D // 2, wi_bf[:, 2 * u * D : 2 * (u + 1) * D], E4M3)
+
+        w_turn0 = bank("C1", "w_turn0")
+        for e in range(2):
+            slot_pairs = picked[:, e, :].bitcast(F32)
+            for v in range(2):
+                nc.tensor.transpose(w_turn0[:, (2 * e + v) * P : (2 * e + v + 1) * P], slot_pairs[:, v : N // 2 : 2], ident[:])
+        nc.vector.tensor_copy(w_bf[:, 3 : N * PACK : PACK], planes[3][:].indirect(offsets[:]))
+        x_raw = tile("x_raw", [P, PACK, R], F32, "plane0")
+        nc.sync.dma_start(out=x_raw[:], in_=xT[0].rearrange("(p j) r -> p j r", j=PACK))
+        y_sb = tile("y_sb", [P, PACK, N], F32, "plane1")
+        nc.sync.dma_start(out=y_sb[:], in_=y[0].rearrange("(p t) i -> p t i", t=PACK))
+        xm_raw = tile("xm_raw", [P, PACK, D], F32, "plane2")
+        nc.sync.dma_start(out=xm_raw[:], in_=xm[0].rearrange("(p t) d -> p t d", t=PACK))
+        scores = [bank(f"A{j}", f"scores{j}") for j in range(CHUNKS)]
+        quantize(w_q, 0, N, w_bf[:], E4M3)
+
+        x_bf = tile("x_bf", [P, R * PACK], BF16, "wt_sb")
+        for u, copy in enumerate((nc.vector.tensor_copy, nc.scalar.copy)):
+            copy(
+                out=x_bf[:].rearrange("p (t m j) -> p m j t", t=PACK, j=PACK)[:, :, :, 2 * u : 2 * u + 2],
+                in_=x_raw[:].rearrange("p j (m t) -> p m j t", t=PACK)[:, :, :, 2 * u : 2 * u + 2],
+            )
         def turn(src, u, dst_bank):
             words = src[:].bitcast(F32)
             for s in range(PACK):
                 nc.tensor.transpose(dst_bank[:, s * P : (s + 1) * P], words[:, 2 * s + u : 2 * N : 2 * PACK], ident[:])
 
-        def lay_out(dst, u, src_bank):
-            nc.scalar.copy(
-                out=dst[:].rearrange("q (p u e s) -> q u p e s", u=2, e=2, s=PACK)[:, u],
-                in_=src_bank[:].bitcast(BF16).rearrange("q (s p e) -> q p e s", s=PACK, e=2),
-            )
+        w_turn1 = bank("C0", "w_turn1")
+        turn(w_bf, 1, w_turn1)
+        for u in range(2):
+            quantize(x_q, u * R // 2, (u + 1) * R // 2, x_bf[:, u * R * 2 : (u + 1) * R * 2], E4M3)
+        wi_bf = tile("wi_bf", [P, D * PACK], BF16, "plane0")
+        nc.scalar.copy(
+            out=wi_bf[:, 0 : 2 * D].bitcast(F32).rearrange("g (p e v) -> g p e v", e=2, v=2),
+            in_=w_turn0[:].rearrange("g (e v p) -> g p e v", e=2, v=2),
+        )
+        nc.scalar.copy(
+            out=wi_bf[:, 2 * D : 4 * D].rearrange("g (p e s) -> g p e s", e=2, s=PACK),
+            in_=w_turn1[:].bitcast(BF16).rearrange("g (s p e) -> g p e s", s=PACK, e=2),
+        )
+        quantize_wi(0, wi_bf)
 
-        def slot_major_half(u, src_bank, tag):
-            half_bf = sb.tile([P, D * PACK // 2], BF16, name=f"wi_bf{u}", tag=tag, align_bytes=64)
-            nc.scalar.copy(
-                out=half_bf[:].rearrange("q (p e s) -> q p e s", e=2, s=PACK),
-                in_=src_bank[:].bitcast(BF16).rearrange("q (s p e) -> q p e s", s=PACK, e=2),
-            )
-            return half_bf
-
-        def quantize_wi(u, half_bf):
-            cols = slice(u * D // 2, (u + 1) * D // 2)
-            nc.vector.quantize_mx(out=wi_q[0][:, cols].bitcast(E4M3), scales=wi_q[1][:, cols], in_=half_bf[:])
-
-        picked = tile("picked", [P, 2, N], BF16)
-        for t in range(2):
-            nc.vector.tensor_copy(picked[:, t, :], planes[t][:].indirect(offsets[:]))
-        gather_scales()
-        nc.scalar.copy(out=w_bf[:].rearrange("p (i t) -> p i t", t=PACK)[:, :, 0:2], in_=picked[:].rearrange("p t i -> p i t"))
-        item_scales()
-        row_factors()
-        for t in range(2, PACK):
-            nc.vector.tensor_copy(w_bf[:, t : N * PACK : PACK], planes[t][:].indirect(offsets[:]))
-
-        scores = [bank(f"A{j}", f"scores{j}") for j in range(CHUNKS)]
-        quantize(w_q, w_bf, E4M3, 0, N)
-        x_bf = sb.tile([P, R * PACK], BF16, name="x_bf", tag="wt_sb", align_bytes=64)
-        x_part(x_bf, nc.vector.tensor_copy, 0, 2)
-        x_part(x_bf, nc.scalar.copy, 2, 4)
-        quantize(x_q, x_bf, E4M3, 0, R // 2)
-        quantize(x_q, x_bf, E4M3, R // 2, R)
-        for j in range(CHUNKS):
-            slots = slice(j * CHUNK, (j + 1) * CHUNK)
+        for j in SCORE_ORDER:
             if j < DIRECT:
                 for e in range(2):
                     t = 2 * j + e
                     mx(scores[j][:, e * HALF : (e + 1) * HALF], x_q, E4M3, slice(t * P, (t + 1) * P), w_q, E4M3, slice(0, HALF))
             else:
-                mx(scores[j][:], w_q, E4M3, slots, x_q, E4M3, slice(0, R))
-        w_turn0 = bank("C1", "w_turn0")
-        turn(w_bf, 0, w_turn0)
-        wi_bf0 = slot_major_half(0, w_turn0, "x_raw")
+                mx(scores[j][:], w_q, E4M3, slice(j * CHUNK, (j + 1) * CHUNK), x_q, E4M3, slice(0, R))
 
         xm_q = operand("xm")
 
-        def xm_block(lo, hi, copy, tag):
-            xm_bf = sb.tile([P, (hi - lo) * PACK], BF16, name=f"xm_bf{lo}", tag=tag, align_bytes=64)
+        def xm_block(lo, hi, copy, buffer):
+            xm_bf = tile(f"xm_bf{lo}", [P, (hi - lo) * PACK], BF16, buffer)
             copy(
                 out=xm_bf[:].rearrange("p (c e t) -> p c t e", e=PACK, t=PACK),
                 in_=xm_raw[:, :, lo:hi].rearrange("p t (c e) -> p c t e", e=PACK),
             )
-            nc.vector.quantize_mx(out=xm_q[0][:, lo:hi].bitcast(E4M3), scales=xm_q[1][:, lo:hi], in_=xm_bf[:])
+            return xm_bf
+
+        def quantize_xm(lo, hi, xm_bf):
+            quantize(xm_q, lo, hi, xm_bf[:], E4M3)
 
         h_bf = tile("h_bf", [P, N * PACK], BF16)
-        h_q = operand("h")
-        nc.gpsimd.memset(h_q[0][:, HALF:N].bitcast(I32), 0)
-        nc.gpsimd.memset(h_q[1][:, HALF:N].bitcast(I32), 0)
         a = [tile(f"a{j}", [P, R], F32) for j in range(CHUNKS)]
         q = [tile(f"q{k}", [P, PACK, HALF], F32) for k in range(2)]
         sq = [tile(f"sq{j}", [P, R], F32) for j in range(CHUNKS)]
         root = [tile(f"root{j}", [P, R], F32) for j in range(CHUNKS)]
         rec = [tile(f"rec{k}", [P, PACK, HALF], F32) for k in range(2)]
+        y_halves = [y_sb[:, :, k * HALF : (k + 1) * HALF] for k in range(2)]
 
         def chunk_of(halves, j):
             if j < DIRECT:
@@ -210,7 +202,8 @@ def tile_attend_gcau_wx_ts_kernel(tc, xT, wT, y, wt, ts, xm, offs, out_0, out_1)
 
         def times_ts(j):
             if j < DIRECT:
-                nc.vector.tensor_tensor(shaped(a[j], j), shaped(scores[j], j), ts_all[:, 0:HALF].unsqueeze(1).to_broadcast([P, 2, HALF]), MULT)
+                ts_half = ts_all[:, 0:HALF].unsqueeze(1).to_broadcast([P, 2, HALF])
+                nc.vector.tensor_tensor(shaped(a[j], j), shaped(scores[j], j), ts_half, MULT)
                 return a[j]
             nc.scalar.activation(out=a[j][:], in_=scores[j][:], func=ACT.Copy, scale=ts_slot[:, j : j + 1])
             turned = bank(f"B{j - DIRECT}", f"turned{j}")
@@ -218,24 +211,25 @@ def tile_attend_gcau_wx_ts_kernel(tc, xT, wT, y, wt, ts, xm, offs, out_0, out_1)
                 nc.tensor.transpose(turned[:, t * P : (t + 1) * P], a[j][:, t * P : (t + 1) * P], ident[:])
             return turned
 
-        def residual(j, scaled):
-            y_halves = [y_sb[:, :, k * HALF : (k + 1) * HALF] for k in range(2)]
-            nc.vector.tensor_tensor(chunk_of(q, j), shaped(scaled, j), chunk_of(y_halves, j), SUB)
+        def residual(j, scaled_chunk):
+            nc.vector.tensor_tensor(chunk_of(q, j), shaped(scaled_chunk, j), chunk_of(y_halves, j), SUB)
 
-        def inverse(k):
-            pair = (2 * k, 2 * k + 1)
-            for j in pair:
-                if j in VSQ:
-                    nc.vector.tensor_tensor(shaped(sq[j], j), chunk_of(q, j), chunk_of(q, j), MULT)
-                else:
-                    nc.scalar.activation(out=shaped(sq[j], j), in_=chunk_of(q, j), func=ACT.Square)
-            for j in pair:
+        def square(j):
+            if j in VECTOR_SQUARES:
+                nc.vector.tensor_tensor(shaped(sq[j], j), chunk_of(q, j), chunk_of(q, j), MULT)
+            else:
+                nc.scalar.activation(out=shaped(sq[j], j), in_=chunk_of(q, j), func=ACT.Square)
+
+        def roots(k):
+            for j in (2 * k, 2 * k + 1):
                 nc.scalar.activation(out=root[j][:], in_=sq[j][:], func=ACT.Abs_reciprocal_sqrt, bias=ones[:])
-            for j in pair:
+
+        def inverses(k):
+            for j in (2 * k, 2 * k + 1):
                 nc.scalar.activation(out=chunk_of(rec, j), in_=shaped(root[j], j), func=ACT.Square)
 
         def numerator(k):
-            num = sb.tile([P, PACK, HALF], F32, name=f"num{k}", tag="num", align_bytes=64)
+            num = tile(f"num{k}", [P, PACK, HALF], F32)
             nc.vector.tensor_tensor(num[:], q[k][:], factor[:, :, k * HALF : (k + 1) * HALF], MULT)
             return num
 
@@ -247,13 +241,16 @@ def tile_attend_gcau_wx_ts_kernel(tc, xT, wT, y, wt, ts, xm, offs, out_0, out_1)
                 MULT,
             )
 
+        def quantize_h(k):
+            quantize(h_q, k * HALF, (k + 1) * HALF, h_bf[:, k * HALF * PACK : (k + 1) * HALF * PACK], E5M2)
+
         def table_product(m, tag, name):
             acc = bank(tag, name)
             mx(acc[:], xm_q, E4M3, slice(m * P, (m + 1) * P), h_q, E5M2, slice(0, N))
             return acc
 
-        def to_sbuf(acc, lo, hi, name, tag):
-            dw = sb.tile([P, hi - lo], F32, name=name, tag=tag, align_bytes=64)
+        def to_sbuf(acc, lo, hi, name, buffer=None):
+            dw = tile(name, [P, hi - lo], F32, buffer)
             nc.scalar.copy(out=dw[:], in_=acc[:, lo:hi])
             return dw
 
@@ -262,38 +259,56 @@ def tile_attend_gcau_wx_ts_kernel(tc, xT, wT, y, wt, ts, xm, offs, out_0, out_1)
             if hi == N:
                 nc.sync.dma_start(out=out_0[m * P : (m + 1) * P, :], in_=windows[m % WINDOWS][:])
 
-        scaled = [times_ts(j) for j in range(CHUNKS)]
-        residual(0, scaled[0])
-        residual(1, scaled[1])
-        inverse(0)
-        residual(2, scaled[2])
-        residual(3, scaled[3])
+        s0 = times_ts(0)
+        s1 = times_ts(1)
+        s2 = times_ts(2)
+        s3 = times_ts(3)
+        residual(0, s0)
+        residual(1, s1)
+        quantize_wi(1, wi_bf)
+        square(0)
+        square(1)
+        roots(0)
         num0 = numerator(0)
-        xm_block(0, P, nc.vector.tensor_copy, "a1")
+        residual(2, s2)
+        residual(3, s3)
+        square(2)
+        inverses(0)
+        xm0 = xm_block(0, P, nc.vector.tensor_copy, "a1")
+        square(3)
+        num1 = numerator(1)
         finish(0, num0)
-        quantize(h_q, h_bf, E5M2, 0, HALF)
-        early = table_product(0, "A0", "dw_early")
-        inverse(1)
-        finish(1, numerator(1))
+        quantize_xm(0, P, xm0)
+        quantize_h(0)
+        early = table_product(0, "A0", "dw_acc_early")
+
+        roots(1)
+        inverses(1)
+        xm1 = xm_block(P, 3 * P, nc.scalar.copy, "root2")
         dw_early = to_sbuf(early, 0, HALF, "dw_early", "root3")
-        quantize(h_q, h_bf, E5M2, HALF, N)
+        finish(1, num1)
+        quantize_xm(P, 3 * P, xm1)
+        quantize_h(1)
+        xm2 = xm_block(3 * P, D, nc.scalar.copy, "rec1")
         scatter(0, dw_early, 0, HALF)
-        late = table_product(0, "A1", "dw_late")
-        scatter(0, to_sbuf(late, HALF, N, "dw_late", "dw_late"), HALF, N)
-        w_turn1 = bank("B1", "w_turn1")
-        turn(w_bf, 1, w_turn1)
-        quantize_wi(0, wi_bf0)
-        quantize_wi(1, slot_major_half(1, w_turn1, "root2"))
+        late = table_product(0, "A1", "dw_acc_late")
+        acc1 = table_product(1, "A2", "dw_acc1")
+        dw_late = to_sbuf(late, HALF, N, "dw_late")
+        dw1 = to_sbuf(acc1, 0, N, "dw1")
+        quantize_xm(3 * P, D, xm2)
+        scatter(0, dw_late, HALF, N)
 
         hi_bf = tile("hi_bf", [P, R * PACK], BF16)
         for u in range(2):
-            h_turn = bank(("C0", "C1")[u], f"h_turn{u}")
+            h_turn = bank(("A1", "A2")[u], f"h_turn{u}")
             turn(h_bf, u, h_turn)
-            lay_out(hi_bf, u, h_turn)
-        xm_block(P, 2 * P, nc.scalar.copy, "num")
-        xm_block(2 * P, D, nc.scalar.copy, "rec1")
+            nc.scalar.copy(
+                out=hi_bf[:].rearrange("g (p u e s) -> g u p e s", u=2, e=2, s=PACK)[:, u],
+                in_=h_turn[:].bitcast(BF16).rearrange("g (s p e) -> g p e s", s=PACK, e=2),
+            )
         hi_q = operand("hi")
-        quantize(hi_q, hi_bf, E5M2, 0, R)
+        scatter(1, dw1, 0, N)
+        quantize(hi_q, 0, R, hi_bf[:], E5M2)
 
         gx = tile("gx", [P, R // P, D], F32)
         gx_rows = out_1[0].rearrange("(b p) d -> p b d", p=P)
@@ -308,10 +323,9 @@ def tile_attend_gcau_wx_ts_kernel(tc, xT, wT, y, wt, ts, xm, offs, out_0, out_1)
             nc.scalar.dma_start(out=gx_rows[:, b, :], in_=gx[:, b, :])
 
         def whole_block(m, tag):
-            scatter(m, to_sbuf(table_product(m, tag, f"dw_acc{m}"), 0, N, f"dw{m}", f"dw{m}"), 0, N)
+            scatter(m, to_sbuf(table_product(m, tag, f"dw_acc{m}"), 0, N, f"dw{m}"), 0, N)
 
-        whole_block(1, "C0")
-        whole_block(2, "C1")
+        whole_block(2, "A1")
+        whole_block(3, "A2")
         for b in range(R // P):
-            row_block(b, ("B0", "B1", "A2", "A3")[b])
-        whole_block(3, "B0")
+            row_block(b, ("B0", "B1", "C0", "C1")[b])

@@ -42,8 +42,8 @@ def tile_attend_gcau_wx_ts_kernel(tc, xT, wT, y, wt, ts, xm, offs, out_0, out_1)
         def bank(tag, name):
             return ps.tile([P, 512], F32, name=name, tag=tag)
 
-        def operand(name):
-            return tile(name + "_codes", [P, 512], U32), tile(name + "_scales", [P, 512], U8)
+        def operand(name, columns=512, buffer=None):
+            return tile(name + "_codes", [P, columns], U32, buffer), tile(name + "_scales", [P, columns], U8)
 
         def quantize(op, lo, hi, src, fmt):
             nc.vector.quantize_mx(out=op[0][:, lo:hi].bitcast(fmt), scales=op[1][:, lo:hi], in_=src)
@@ -102,8 +102,6 @@ def tile_attend_gcau_wx_ts_kernel(tc, xT, wT, y, wt, ts, xm, offs, out_0, out_1)
 
         x_q = operand("x")
         w_bf = tile("w_bf", [P, N * PACK], BF16)
-        w_q = operand("w")
-        wi_q = operand("wi")
         nc.vector.tensor_copy(w_bf[:, 2 : N * PACK : PACK], planes[2][:].indirect(offsets[:]))
         planes[3] = tile("plane3", [P, T], F32, "plane2")
         nc.sync.dma_start(out=planes[3][:], in_=w_rows[:, 3, :])
@@ -119,15 +117,20 @@ def tile_attend_gcau_wx_ts_kernel(tc, xT, wT, y, wt, ts, xm, offs, out_0, out_1)
             nc.vector.tensor_copy(picked[:, t, :], planes[t][:].indirect(offsets[:]))
         nc.scalar.copy(out=w_bf[:].rearrange("p (i t) -> p i t", t=PACK)[:, :, 0:2], in_=picked[:].rearrange("p t i -> p i t"))
 
-        def quantize_wi(u, wi_bf):
-            quantize(wi_q, u * D // 2, (u + 1) * D // 2, wi_bf[:, 2 * u * D : 2 * (u + 1) * D], E4M3)
-
         w_turn0 = bank("C1", "w_turn0")
         for e in range(2):
             slot_pairs = picked[:, e, :].bitcast(F32)
             for v in range(2):
                 nc.tensor.transpose(w_turn0[:, (2 * e + v) * P : (2 * e + v + 1) * P], slot_pairs[:, v : N // 2 : 2], ident[:])
-        nc.vector.tensor_copy(w_bf[:, 3 : N * PACK : PACK], planes[3][:].indirect(offsets[:]))
+        wi_bf = [tile("wi_bf0", [P, D * PACK // 2], BF16)]
+        nc.scalar.copy(
+            out=wi_bf[0][:].bitcast(F32).rearrange("g (p e v) -> g p e v", e=2, v=2),
+            in_=w_turn0[:].rearrange("g (e v p) -> g p e v", e=2, v=2),
+        )
+        for lo in (0, HALF):
+            nc.vector.tensor_copy(
+                w_bf[:, lo * PACK + 3 : (lo + HALF) * PACK : PACK], planes[3][:].indirect(offsets[:, lo // 16 : (lo + HALF) // 16])
+            )
         x_raw = tile("x_raw", [P, PACK, R], F32, "plane0")
         nc.sync.dma_start(out=x_raw[:], in_=xT[0].rearrange("(p j) r -> p j r", j=PACK))
         y_sb = tile("y_sb", [P, PACK, N], F32, "plane1")
@@ -135,12 +138,13 @@ def tile_attend_gcau_wx_ts_kernel(tc, xT, wT, y, wt, ts, xm, offs, out_0, out_1)
         xm_raw = tile("xm_raw", [P, PACK, D], F32, "plane2")
         nc.sync.dma_start(out=xm_raw[:], in_=xm[0].rearrange("(p t) d -> p t d", t=PACK))
         scores = [bank(f"A{j}", f"scores{j}") for j in range(CHUNKS)]
-        quantize(w_q, 0, N, w_bf[:], E4M3)
+        w_q = [operand("w0", HALF)]
+        quantize(w_q[0], 0, HALF, w_bf[:, 0 : HALF * PACK], E4M3)
 
-        x_bf = tile("x_bf", [P, R * PACK], BF16, "wt_sb")
+        x_bf = [tile(f"x_bf{u}", [P, R * 2], BF16, ("x_bf0", "wt_sb")[u]) for u in range(2)]
         for u, copy in enumerate((nc.vector.tensor_copy, nc.scalar.copy)):
             copy(
-                out=x_bf[:].rearrange("p (t m j) -> p m j t", t=PACK, j=PACK)[:, :, :, 2 * u : 2 * u + 2],
+                out=x_bf[u][:].rearrange("p (t m j) -> p m j t", t=2, j=PACK),
                 in_=x_raw[:].rearrange("p j (m t) -> p m j t", t=PACK)[:, :, :, 2 * u : 2 * u + 2],
             )
         def turn(src, u, dst_bank):
@@ -151,25 +155,28 @@ def tile_attend_gcau_wx_ts_kernel(tc, xT, wT, y, wt, ts, xm, offs, out_0, out_1)
         w_turn1 = bank("C0", "w_turn1")
         turn(w_bf, 1, w_turn1)
         for u in range(2):
-            quantize(x_q, u * R // 2, (u + 1) * R // 2, x_bf[:, u * R * 2 : (u + 1) * R * 2], E4M3)
-        wi_bf = tile("wi_bf", [P, D * PACK], BF16, "plane0")
+            quantize(x_q, u * R // 2, (u + 1) * R // 2, x_bf[u][:], E4M3)
+        w_q.append(operand("w1", HALF, "x_bf0"))
+        quantize(w_q[1], 0, HALF, w_bf[:, HALF * PACK : N * PACK], E4M3)
+        wi_q = operand("wi", D, "wt_sb")
+        wi_bf.append(tile("wi_bf1", [P, D * PACK // 2], BF16, "plane0"))
         nc.scalar.copy(
-            out=wi_bf[:, 0 : 2 * D].bitcast(F32).rearrange("g (p e v) -> g p e v", e=2, v=2),
-            in_=w_turn0[:].rearrange("g (e v p) -> g p e v", e=2, v=2),
-        )
-        nc.scalar.copy(
-            out=wi_bf[:, 2 * D : 4 * D].rearrange("g (p e s) -> g p e s", e=2, s=PACK),
+            out=wi_bf[1][:].rearrange("g (p e s) -> g p e s", e=2, s=PACK),
             in_=w_turn1[:].bitcast(BF16).rearrange("g (s p e) -> g p e s", s=PACK, e=2),
         )
-        quantize_wi(0, wi_bf)
+
+        def quantize_wi(u):
+            quantize(wi_q, u * D // 2, (u + 1) * D // 2, wi_bf[u][:], E4M3)
+
+        quantize_wi(0)
 
         for j in SCORE_ORDER:
             if j < DIRECT:
                 for e in range(2):
                     t = 2 * j + e
-                    mx(scores[j][:, e * HALF : (e + 1) * HALF], x_q, E4M3, slice(t * P, (t + 1) * P), w_q, E4M3, slice(0, HALF))
+                    mx(scores[j][:, e * HALF : (e + 1) * HALF], x_q, E4M3, slice(t * P, (t + 1) * P), w_q[0], E4M3, slice(0, HALF))
             else:
-                mx(scores[j][:], w_q, E4M3, slice(j * CHUNK, (j + 1) * CHUNK), x_q, E4M3, slice(0, R))
+                mx(scores[j][:], w_q[1], E4M3, slice((j - DIRECT) * CHUNK, (j - DIRECT + 1) * CHUNK), x_q, E4M3, slice(0, R))
 
         xm_q = operand("xm")
 
@@ -265,7 +272,7 @@ def tile_attend_gcau_wx_ts_kernel(tc, xT, wT, y, wt, ts, xm, offs, out_0, out_1)
         s3 = times_ts(3)
         residual(0, s0)
         residual(1, s1)
-        quantize_wi(1, wi_bf)
+        quantize_wi(1)
         square(0)
         square(1)
         roots(0)
@@ -284,18 +291,20 @@ def tile_attend_gcau_wx_ts_kernel(tc, xT, wT, y, wt, ts, xm, offs, out_0, out_1)
 
         roots(1)
         inverses(1)
-        xm1 = xm_block(P, 3 * P, nc.scalar.copy, "root2")
+        xm1 = xm_block(P, 2 * P, nc.scalar.copy, "root2")
+        xm2 = xm_block(2 * P, 3 * P, nc.scalar.copy, "sq3")
         dw_early = to_sbuf(early, 0, HALF, "dw_early", "root3")
         finish(1, num1)
-        quantize_xm(P, 3 * P, xm1)
+        quantize_xm(P, 2 * P, xm1)
         quantize_h(1)
-        xm2 = xm_block(3 * P, D, nc.scalar.copy, "rec1")
+        quantize_xm(2 * P, 3 * P, xm2)
+        xm3 = xm_block(3 * P, D, nc.scalar.copy, "rec1")
         scatter(0, dw_early, 0, HALF)
         late = table_product(0, "A1", "dw_acc_late")
         acc1 = table_product(1, "A2", "dw_acc1")
         dw_late = to_sbuf(late, HALF, N, "dw_late")
         dw1 = to_sbuf(acc1, 0, N, "dw1")
-        quantize_xm(3 * P, D, xm2)
+        quantize_xm(3 * P, D, xm3)
         scatter(0, dw_late, HALF, N)
 
         hi_bf = tile("hi_bf", [P, R * PACK], BF16)

@@ -301,40 +301,47 @@ def tile_attend_gcau_wx_ts_kernel(tc, xT, wT, y, wt, ts, xm, offs, out_0, out_1)
         xm3 = xm_block(3 * P, D, nc.scalar.copy, "rec1")
         scatter(0, dw_early, 0, HALF)
         late = table_product(0, "A1", "dw_acc_late")
-        acc1 = table_product(1, "A2", "dw_acc1")
         dw_late = to_sbuf(late, HALF, N, "dw_late")
-        dw1 = to_sbuf(acc1, 0, N, "dw1")
         quantize_xm(3 * P, D, xm3)
         scatter(0, dw_late, HALF, N)
 
-        hi_bf = tile("hi_bf", [P, R * PACK], BF16)
-        for u in range(2):
-            h_turn = bank(("A1", "A2")[u], f"h_turn{u}")
-            turn(h_bf, u, h_turn)
-            nc.scalar.copy(
-                out=hi_bf[:].rearrange("g (p u e s) -> g u p e s", u=2, e=2, s=PACK)[:, u],
-                in_=h_turn[:].bitcast(BF16).rearrange("g (s p e) -> g p e s", s=PACK, e=2),
-            )
         hi_q = operand("hi")
-        scatter(1, dw1, 0, N)
-        quantize(hi_q, 0, R, hi_bf[:], E5M2)
+        gx = tile("gx", [P, PACK, D], F32)
+        gx_rows = out_1[0].rearrange("(p t) d -> p t d", t=PACK)
 
-        gx = tile("gx", [P, R // P, D], F32)
-        gx_rows = out_1[0].rearrange("(b p) d -> p b d", p=P)
-
-        def row_block(b, tag):
-            acc = bank(tag, f"gx_acc{b}")
-            mx(acc[:], hi_q, E5M2, slice(b * P, (b + 1) * P), wi_q, E4M3, slice(0, D))
+        def h_by_slots(u, tag):
+            h_turn = bank(tag, f"h_turn{u}")
+            turn(h_bf, u, h_turn)
+            hi_bf = tile(f"hi_bf{u}", [P, R * 2], BF16)
             nc.scalar.copy(
-                out=gx[:, b, :].rearrange("r (p u e) -> r p u e", u=2, e=2),
+                out=hi_bf[:].rearrange("g (e p s) -> g e p s", e=2, s=PACK),
+                in_=h_turn[:].bitcast(BF16).rearrange("g (s p e) -> g e p s", s=PACK, e=2),
+            )
+            return hi_bf
+
+        def quantize_hi(u, hi_bf):
+            quantize(hi_q, u * R // 2, (u + 1) * R // 2, hi_bf[:], E5M2)
+
+        def row_block(t, tag):
+            acc = bank(tag, f"gx_acc{t}")
+            mx(acc[:], hi_q, E5M2, slice(t * P, (t + 1) * P), wi_q, E4M3, slice(0, D))
+            nc.scalar.copy(
+                out=gx[:, t, :].rearrange("r (p u e) -> r p u e", u=2, e=2),
                 in_=acc[:].rearrange("r (u p e) -> r p u e", u=2, e=2),
             )
-            nc.scalar.dma_start(out=gx_rows[:, b, :], in_=gx[:, b, :])
+            nc.scalar.dma_start(out=gx_rows[:, t, :], in_=gx[:, t, :])
 
-        def whole_block(m, tag):
-            scatter(m, to_sbuf(table_product(m, tag, f"dw_acc{m}"), 0, N, f"dw{m}"), 0, N)
+        def block_in_sbuf(m, tag):
+            return to_sbuf(table_product(m, tag, f"dw_acc{m}"), 0, N, f"dw{m}")
 
-        whole_block(2, "A1")
-        whole_block(3, "A2")
-        for b in range(R // P):
-            row_block(b, ("B0", "B1", "C0", "C1")[b])
+        quantize_hi(0, h_by_slots(0, "B0"))
+        dw1 = block_in_sbuf(1, "A2")
+        hi_bf1 = h_by_slots(1, "A1")
+        scatter(1, dw1, 0, N)
+        row_block(0, "C0")
+        row_block(1, "C1")
+        quantize_hi(1, hi_bf1)
+        scatter(2, block_in_sbuf(2, "A1"), 0, N)
+        row_block(2, "B1")
+        row_block(3, "B0")
+        scatter(3, block_in_sbuf(3, "C0"), 0, N)

@@ -329,7 +329,8 @@ def tile_attend_gcau_wx_ts_kernel(tc, xT, wT, y, wt, ts, xm, offs, out_0, out_1)
                 out=gx[:, t, :].rearrange("r (p u e) -> r p u e", u=2, e=2),
                 in_=acc[:].rearrange("r (u p e) -> r p u e", u=2, e=2),
             )
-            nc.scalar.dma_start(out=gx_rows[:, t, :], in_=gx[:, t, :])
+            if t % 2 == 1:
+                nc.scalar.dma_start(out=gx_rows[:, t - 1 : t + 1, :], in_=gx[:, t - 1 : t + 1, :])
 
         def block_in_sbuf(m, tag):
             return to_sbuf(table_product(m, tag, f"dw_acc{m}"), 0, N, f"dw{m}")

@@ -24,6 +24,7 @@ HALF = N // 2
 CHUNK = 128
 CHUNKS = 4
 DIRECT = 2
+X_SPLIT = 32
 SCORE_ORDER = (0, 1, 2, 3)
 VECTOR_SQUARES = (3,)
 WINDOWS = 3
@@ -142,11 +143,16 @@ def tile_attend_gcau_wx_ts_kernel(tc, xT, wT, y, wt, ts, xm, offs, out_0, out_1)
         quantize(w_q[0], 0, HALF, w_bf[:, 0 : HALF * PACK], E4M3)
 
         x_bf = [tile(f"x_bf{u}", [P, R * 2], BF16, ("x_bf0", "wt_sb")[u]) for u in range(2)]
-        for u, copy in enumerate((nc.vector.tensor_copy, nc.scalar.copy)):
+        for copy, u, lo, hi in (
+            (nc.vector.tensor_copy, 0, 0, P),
+            (nc.scalar.copy, 1, X_SPLIT, P),
+            (nc.vector.tensor_copy, 1, 0, X_SPLIT),
+        ):
             copy(
-                out=x_bf[u][:].rearrange("p (t m j) -> p m j t", t=2, j=PACK),
-                in_=x_raw[:].rearrange("p j (m t) -> p m j t", t=PACK)[:, :, :, 2 * u : 2 * u + 2],
+                out=x_bf[u][:].rearrange("p (t m j) -> p m j t", t=2, j=PACK)[:, lo:hi],
+                in_=x_raw[:].rearrange("p j (m t) -> p m j t", t=PACK)[:, lo:hi, :, 2 * u : 2 * u + 2],
             )
+
         def turn(src, u, dst_bank):
             words = src[:].bitcast(F32)
             for s in range(PACK):

@@ -23,10 +23,10 @@ PACK = 4
 HALF = N // 2
 CHUNK = 128
 CHUNKS = 4
-DIRECT = 2
+DIRECT = (0, 3)
 X_SPLIT = 32
 SCORE_ORDER = (0, 1, 2, 3)
-VECTOR_SQUARES = (3,)
+VECTOR_SQUARES = ()
 WINDOWS = 3
 VECTOR_MEMSETS = 2
 
@@ -79,9 +79,9 @@ def tile_attend_gcau_wx_ts_kernel(tc, xT, wT, y, wt, ts, xm, offs, out_0, out_1)
         ident = tile("ident", [P, P], F32)
         make_identity(nc, ident[:])
 
-        h_q = operand("h")
-        nc.gpsimd.memset(h_q[0][:, HALF:N].bitcast(I32), 0)
-        nc.gpsimd.memset(h_q[1][:, HALF:N].bitcast(I32), 0)
+        h_q = operand("h", HALF + N)
+        nc.gpsimd.memset(h_q[0][:, 0:HALF].bitcast(I32), 0)
+        nc.gpsimd.memset(h_q[1][:, 0:HALF].bitcast(I32), 0)
         windows = [tile(f"window{m}", [P, T], F32) for m in range(WINDOWS)]
         for m in range(WINDOWS):
             engine = nc.vector if m < VECTOR_MEMSETS else nc.gpsimd
@@ -108,11 +108,11 @@ def tile_attend_gcau_wx_ts_kernel(tc, xT, wT, y, wt, ts, xm, offs, out_0, out_1)
         nc.sync.dma_start(out=planes[3][:], in_=w_rows[:, 3, :])
         nc.vector.tensor_copy(ts_all[:], ts_win[:].indirect(offsets[:]))
         ts_turn = bank("C0", "ts_turn")
-        for j in range(DIRECT, CHUNKS):
+        for j in (1, 2):
             nc.tensor.transpose(ts_turn[:, j * P : (j + 1) * P], ts_all[:, j * P : (j + 1) * P], ident[:])
         for t in range(PACK):
             nc.scalar.activation(out=factor[:, t, :], in_=ts_all[:], func=ACT.Copy, scale=wt_sb[:, t : t + 1])
-        nc.scalar.copy(out=ts_slot[:, DIRECT:CHUNKS], in_=ts_turn[:, DIRECT * P : N : P])
+        nc.scalar.copy(out=ts_slot[:, 1:3], in_=ts_turn[:, P : 3 * P : P])
         picked = tile("picked", [P, 2, N], BF16, "ts_win")
         for t in range(2):
             nc.vector.tensor_copy(picked[:, t, :], planes[t][:].indirect(offsets[:]))
@@ -177,12 +177,12 @@ def tile_attend_gcau_wx_ts_kernel(tc, xT, wT, y, wt, ts, xm, offs, out_0, out_1)
         quantize_wi(0)
 
         for j in SCORE_ORDER:
-            if j < DIRECT:
-                for e in range(2):
-                    t = 2 * j + e
-                    mx(scores[j][:, e * HALF : (e + 1) * HALF], x_q, E4M3, slice(t * P, (t + 1) * P), w_q[0], E4M3, slice(0, HALF))
+            w_cols = slice(j % 2 * CHUNK, (j % 2 + 1) * CHUNK)
+            if j in DIRECT:
+                for t in range(PACK):
+                    mx(scores[j][:, t * P : (t + 1) * P], x_q, E4M3, slice(t * P, (t + 1) * P), w_q[j // 2], E4M3, w_cols)
             else:
-                mx(scores[j][:], w_q[1], E4M3, slice((j - DIRECT) * CHUNK, (j - DIRECT + 1) * CHUNK), x_q, E4M3, slice(0, R))
+                mx(scores[j][:], w_q[j // 2], E4M3, w_cols, x_q, E4M3, slice(0, R))
 
         xm_q = operand("xm")
 
@@ -198,68 +198,58 @@ def tile_attend_gcau_wx_ts_kernel(tc, xT, wT, y, wt, ts, xm, offs, out_0, out_1)
             quantize(xm_q, lo, hi, xm_bf[:], E4M3)
 
         h_bf = tile("h_bf", [P, N * PACK], BF16)
-        a = [tile(f"a{j}", [P, R], F32) for j in range(CHUNKS)]
-        q = [tile(f"q{k}", [P, PACK, HALF], F32) for k in range(2)]
-        sq = [tile(f"sq{j}", [P, R], F32) for j in range(CHUNKS)]
-        root = [tile(f"root{j}", [P, R], F32) for j in range(CHUNKS)]
-        rec = [tile(f"rec{k}", [P, PACK, HALF], F32) for k in range(2)]
-        y_halves = [y_sb[:, :, k * HALF : (k + 1) * HALF] for k in range(2)]
+        q, sq, root, rec, num = ([tile(f"{kind}{j}", [P, R], F32) for j in range(CHUNKS)] for kind in ("q", "sq", "root", "rec", "num"))
+        a = [tile(f"a{j}", [P, R], F32, ("a0", "a1", "a2", "a1")[j]) for j in range(CHUNKS)]
 
-        def chunk_of(halves, j):
-            if j < DIRECT:
-                return halves[0][:, 2 * j : 2 * j + 2, :]
-            return halves[1][:, :, (j - DIRECT) * CHUNK : (j - DIRECT + 1) * CHUNK]
+        def planes_of(flat):
+            return flat[:].rearrange("p (t i) -> p t i", t=PACK)
 
-        def shaped(flat, j):
-            return flat[:].rearrange("p (t i) -> p t i", t=2 if j < DIRECT else PACK)
+        def slots(j):
+            return slice(j * CHUNK, (j + 1) * CHUNK)
 
         def times_ts(j):
-            if j < DIRECT:
-                ts_half = ts_all[:, 0:HALF].unsqueeze(1).to_broadcast([P, 2, HALF])
-                nc.vector.tensor_tensor(shaped(a[j], j), shaped(scores[j], j), ts_half, MULT)
+            if j in DIRECT:
+                ts_chunk = ts_all[:, slots(j)].unsqueeze(1).to_broadcast([P, PACK, CHUNK])
+                nc.vector.tensor_tensor(planes_of(a[j]), planes_of(scores[j]), ts_chunk, MULT)
                 return a[j]
             nc.scalar.activation(out=a[j][:], in_=scores[j][:], func=ACT.Copy, scale=ts_slot[:, j : j + 1])
-            turned = bank(f"B{j - DIRECT}", f"turned{j}")
+            turned = bank(f"B{j - 1}", f"turned{j}")
             for t in range(PACK):
                 nc.tensor.transpose(turned[:, t * P : (t + 1) * P], a[j][:, t * P : (t + 1) * P], ident[:])
             return turned
 
         def residual(j, scaled_chunk):
-            nc.vector.tensor_tensor(chunk_of(q, j), shaped(scaled_chunk, j), chunk_of(y_halves, j), SUB)
+            nc.vector.tensor_tensor(planes_of(q[j]), planes_of(scaled_chunk), y_sb[:, :, slots(j)], SUB)
 
         def square(j):
             if j in VECTOR_SQUARES:
-                nc.vector.tensor_tensor(shaped(sq[j], j), chunk_of(q, j), chunk_of(q, j), MULT)
+                nc.vector.tensor_tensor(sq[j][:], q[j][:], q[j][:], MULT)
             else:
-                nc.scalar.activation(out=shaped(sq[j], j), in_=chunk_of(q, j), func=ACT.Square)
+                nc.scalar.activation(out=sq[j][:], in_=q[j][:], func=ACT.Square)
 
-        def roots(k):
-            for j in (2 * k, 2 * k + 1):
-                nc.scalar.activation(out=root[j][:], in_=sq[j][:], func=ACT.Abs_reciprocal_sqrt, bias=ones[:])
+        def roots(j):
+            nc.scalar.activation(out=root[j][:], in_=sq[j][:], func=ACT.Abs_reciprocal_sqrt, bias=ones[:])
 
-        def inverses(k):
-            for j in (2 * k, 2 * k + 1):
-                nc.scalar.activation(out=chunk_of(rec, j), in_=shaped(root[j], j), func=ACT.Square)
+        def inverses(j):
+            nc.scalar.activation(out=rec[j][:], in_=root[j][:], func=ACT.Square)
 
-        def numerator(k):
-            num = tile(f"num{k}", [P, PACK, HALF], F32)
-            nc.vector.tensor_tensor(num[:], q[k][:], factor[:, :, k * HALF : (k + 1) * HALF], MULT)
-            return num
+        def numerator(j, engine=nc.vector):
+            engine.tensor_tensor(planes_of(num[j]), planes_of(q[j]), factor[:, :, slots(j)], MULT)
 
-        def finish(k, num):
+        def finish(j):
             nc.vector.tensor_tensor(
-                h_bf[:, k * HALF * PACK : (k + 1) * HALF * PACK].rearrange("p (c e t) -> p c t e", e=2, t=PACK),
-                num[:].rearrange("p t (c e) -> p c t e", e=2),
-                rec[k][:].rearrange("p t (c e) -> p c t e", e=2),
+                h_bf[:, j * CHUNK * PACK : (j + 1) * CHUNK * PACK].rearrange("p (c e t) -> p c t e", e=2, t=PACK),
+                num[j][:].rearrange("p (t c e) -> p c t e", t=PACK, e=2),
+                rec[j][:].rearrange("p (t c e) -> p c t e", t=PACK, e=2),
                 MULT,
             )
 
-        def quantize_h(k):
-            quantize(h_q, k * HALF, (k + 1) * HALF, h_bf[:, k * HALF * PACK : (k + 1) * HALF * PACK], E5M2)
+        def quantize_h(lo, hi):
+            quantize(h_q, HALF + lo, HALF + hi, h_bf[:, lo * PACK : hi * PACK], E5M2)
 
-        def table_product(m, tag, name):
+        def table_product(m, tag, name, start=HALF):
             acc = bank(tag, name)
-            mx(acc[:], xm_q, E4M3, slice(m * P, (m + 1) * P), h_q, E5M2, slice(0, N))
+            mx(acc[:], xm_q, E4M3, slice(m * P, (m + 1) * P), h_q, E5M2, slice(start, start + N))
             return acc
 
         def to_sbuf(acc, lo, hi, name, buffer=None):
@@ -268,46 +258,56 @@ def tile_attend_gcau_wx_ts_kernel(tc, xT, wT, y, wt, ts, xm, offs, out_0, out_1)
             return dw
 
         def scatter(m, dw, lo, hi):
-            nc.vector.tensor_copy(windows[m % WINDOWS][:].indirect(offsets[:, lo // 16 : hi // 16]), dw[:])
+            target = windows[m % WINDOWS][:].indirect(offsets[:, lo // 16 : hi // 16])
+            nc.vector.tensor_copy(target, dw[:])
             if hi == N:
                 nc.sync.dma_start(out=out_0[m * P : (m + 1) * P, :], in_=windows[m % WINDOWS][:])
 
         s0 = times_ts(0)
         s1 = times_ts(1)
         s2 = times_ts(2)
-        s3 = times_ts(3)
-        residual(0, s0)
-        residual(1, s1)
         quantize_wi(1)
+        residual(0, s0)
         square(0)
-        square(1)
+        numerator(0)
+        residual(1, s1)
         roots(0)
-        num0 = numerator(0)
+        square(1)
+        s3 = times_ts(3)
         residual(2, s2)
-        residual(3, s3)
-        square(2)
         inverses(0)
-        xm0 = xm_block(0, P, nc.vector.tensor_copy, "a1")
-        square(3)
-        num1 = numerator(1)
-        finish(0, num0)
-        quantize_xm(0, P, xm0)
-        quantize_h(0)
-        early = table_product(0, "A0", "dw_acc_early")
-
+        residual(3, s3)
         roots(1)
+        square(2)
+        numerator(1)
         inverses(1)
+        finish(0)
+        xm0 = xm_block(0, P, nc.vector.tensor_copy, "num0")
+        square(3)
+        numerator(2)
+        quantize_xm(0, P, xm0)
+        finish(1)
+        roots(2)
+        roots(3)
+        numerator(3)
+        quantize_h(0, HALF)
+        early = table_product(0, "A0", "dw_acc_early", 0)
+        inverses(2)
+        inverses(3)
+        finish(2)
+        dw_early = tile("dw_early", [P, HALF], F32, "root3")
+        nc.scalar.copy(out=dw_early[:], in_=early[:, HALF:N])
         xm1 = xm_block(P, 2 * P, nc.scalar.copy, "root2")
-        xm2 = xm_block(2 * P, 3 * P, nc.scalar.copy, "sq3")
-        dw_early = to_sbuf(early, 0, HALF, "dw_early", "root3")
-        finish(1, num1)
+        finish(3)
+        quantize_h(HALF, HALF + CHUNK)
+        quantize_h(HALF + CHUNK, N)
         quantize_xm(P, 2 * P, xm1)
-        quantize_h(1)
-        quantize_xm(2 * P, 3 * P, xm2)
-        xm3 = xm_block(3 * P, D, nc.scalar.copy, "rec1")
+        xm2 = xm_block(2 * P, 3 * P, nc.scalar.copy, "root2")
+        xm3 = xm_block(3 * P, D, nc.scalar.copy, "rec3")
         scatter(0, dw_early, 0, HALF)
         late = table_product(0, "A1", "dw_acc_late")
         dw_late = to_sbuf(late, HALF, N, "dw_late")
+        quantize_xm(2 * P, 3 * P, xm2)
         quantize_xm(3 * P, D, xm3)
         scatter(0, dw_late, HALF, N)
 
@@ -318,7 +318,7 @@ def tile_attend_gcau_wx_ts_kernel(tc, xT, wT, y, wt, ts, xm, offs, out_0, out_1)
         def h_by_slots(u, tag):
             h_turn = bank(tag, f"h_turn{u}")
             turn(h_bf, u, h_turn)
-            hi_bf = tile(f"hi_bf{u}", [P, R * 2], BF16)
+            hi_bf = tile(f"hi_bf{u}", [P, R * 2], BF16, ("rec3", "hi_bf1")[u])
             nc.scalar.copy(
                 out=hi_bf[:].rearrange("g (e p s) -> g e p s", e=2, s=PACK),
                 in_=h_turn[:].bitcast(BF16).rearrange("g (s p e) -> g e p s", s=PACK, e=2),
@@ -341,14 +341,16 @@ def tile_attend_gcau_wx_ts_kernel(tc, xT, wT, y, wt, ts, xm, offs, out_0, out_1)
         def block_in_sbuf(m, tag):
             return to_sbuf(table_product(m, tag, f"dw_acc{m}"), 0, N, f"dw{m}")
 
-        quantize_hi(0, h_by_slots(0, "B0"))
+        hi_bf0 = h_by_slots(0, "B0")
         dw1 = block_in_sbuf(1, "A2")
         hi_bf1 = h_by_slots(1, "A1")
+        quantize_hi(0, hi_bf0)
         scatter(1, dw1, 0, N)
         row_block(0, "C0")
         row_block(1, "C1")
+        dw2 = block_in_sbuf(2, "A1")
         quantize_hi(1, hi_bf1)
-        scatter(2, block_in_sbuf(2, "A1"), 0, N)
+        scatter(2, dw2, 0, N)
         row_block(2, "B1")
         row_block(3, "B0")
         scatter(3, block_in_sbuf(3, "C0"), 0, N)

@@ -28,16 +28,19 @@ X_SPLIT = 32
 SCORE_ORDER = (0, 1, 2, 3)
 VECTOR_SQUARES = ()
 WINDOWS = 3
-VECTOR_MEMSETS = 2
+VECTOR_MEMSETS = 1
 
 
 def tile_attend_gcau_wx_ts_kernel(tc, xT, wT, y, wt, ts, xm, offs, out_0, out_1):
     nc = tc.nc
     with ExitStack() as ctx:
         sb = ctx.enter_context(tc.tile_pool(name="sb", bufs=1))
+        placed = ctx.enter_context(tc.tile_pool(name="placed", bufs=1))
         ps = ctx.enter_context(tc.psum_pool(name="ps", bufs=1))
 
         def tile(name, shape, dtype, buffer=None):
+            if isinstance(buffer, int):
+                return placed.tile(shape, dtype, name=name, offset=buffer * 1024, align_bytes=64)
             return sb.tile(shape, dtype, name=name, tag=buffer or name, align_bytes=64)
 
         def bank(tag, name):
@@ -61,11 +64,13 @@ def tile_attend_gcau_wx_ts_kernel(tc, xT, wT, y, wt, ts, xm, offs, out_0, out_1)
             )
 
         offsets = sb.tile([P, N // 16], U16, name="offsets")
-        ts_cols = tile("ts_cols", [P, T // P], F32)
+        ts_span = tile("ts_span", [P, 2 * T + 512], F32, 7)
+        ts_cols = ts_span[:, 0 : T // P]
         nc.sync.dma_start(out=ts_cols[:], in_=ts[0].rearrange("(p c) -> p c", p=P))
         wt_sb = tile("wt_sb", [P, PACK], F32)
         w_rows = wT.rearrange("(p t) c -> p t c", t=PACK)
-        planes = {t: tile(f"plane{t}", [P, T], F32) for t in (2, 0, 1)}
+        planes = {t: tile(f"plane{t}", [P, T], F32) for t in (0, 1)}
+        planes[2] = tile("plane2", [P, T], F32)
         nc.sync.dma_start(out=planes[2][:], in_=w_rows[:, 2, :])
         nc.sync.dma_start(offsets[:], offs)
         nc.sync.dma_start(out=wt_sb[:], in_=wt[0].rearrange("(p t) o -> p (t o)", t=PACK))
@@ -74,20 +79,22 @@ def tile_attend_gcau_wx_ts_kernel(tc, xT, wT, y, wt, ts, xm, offs, out_0, out_1)
 
         ones = tile("ones", [P, 1], F32)
         nc.vector.memset(ones[:], 1.0)
+        seed = tile("seed", [P, 1], F32, 38)
+        nc.vector.memset(seed[:, 0:1], 1.0)
         warm = tile("warm", [P, 1], F32)
-        nc.scalar.activation(out=warm[:], in_=ones[:], func=ACT.Abs_reciprocal_sqrt, bias=ones[:])
+        nc.scalar.activation(out=warm[:], in_=seed[:, 0:1], func=ACT.Abs_reciprocal_sqrt, bias=ones[:])
         ident = tile("ident", [P, P], F32)
         make_identity(nc, ident[:])
 
         h_q = operand("h", HALF + N)
         nc.gpsimd.memset(h_q[0][:, 0:HALF].bitcast(I32), 0)
         nc.gpsimd.memset(h_q[1][:, 0:HALF].bitcast(I32), 0)
-        windows = [tile(f"window{m}", [P, T], F32) for m in range(WINDOWS)]
+        windows = [tile(f"window{m}", [P, T], F32, (38, 16, 24)[m]) for m in range(WINDOWS)]
         for m in range(WINDOWS):
             engine = nc.vector if m < VECTOR_MEMSETS else nc.gpsimd
             engine.memset(windows[m][:].bitcast(I32), 0)
 
-        ts_win = tile("ts_win", [P, T], F32)
+        ts_win = tile("ts_win", [P, T], F32, 47)
         for g in range(PACK):
             spread = bank(f"A{g}", f"spread{g}")
             for e in range(PACK):
@@ -104,7 +111,7 @@ def tile_attend_gcau_wx_ts_kernel(tc, xT, wT, y, wt, ts, xm, offs, out_0, out_1)
         x_q = operand("x")
         w_bf = tile("w_bf", [P, N * PACK], BF16)
         nc.vector.tensor_copy(w_bf[:, 2 : N * PACK : PACK], planes[2][:].indirect(offsets[:]))
-        planes[3] = tile("plane3", [P, T], F32, "plane2")
+        planes[3] = tile("plane3", [P, T], F32, 8)
         nc.sync.dma_start(out=planes[3][:], in_=w_rows[:, 3, :])
         nc.vector.tensor_copy(ts_all[:], ts_win[:].indirect(offsets[:]))
         ts_turn = bank("C0", "ts_turn")
@@ -113,7 +120,7 @@ def tile_attend_gcau_wx_ts_kernel(tc, xT, wT, y, wt, ts, xm, offs, out_0, out_1)
         for t in range(PACK):
             nc.scalar.activation(out=factor[:, t, :], in_=ts_all[:], func=ACT.Copy, scale=wt_sb[:, t : t + 1])
         nc.scalar.copy(out=ts_slot[:, 1:3], in_=ts_turn[:, P : 3 * P : P])
-        picked = tile("picked", [P, 2, N], BF16, "ts_win")
+        picked = tile("picked", [P, 2, N], BF16, 47)
         for t in range(2):
             nc.vector.tensor_copy(picked[:, t, :], planes[t][:].indirect(offsets[:]))
         nc.scalar.copy(out=w_bf[:].rearrange("p (i t) -> p i t", t=PACK)[:, :, 0:2], in_=picked[:].rearrange("p t i -> p i t"))
@@ -132,17 +139,17 @@ def tile_attend_gcau_wx_ts_kernel(tc, xT, wT, y, wt, ts, xm, offs, out_0, out_1)
             nc.vector.tensor_copy(
                 w_bf[:, lo * PACK + 3 : (lo + HALF) * PACK : PACK], planes[3][:].indirect(offsets[:, lo // 16 : (lo + HALF) // 16])
             )
-        x_raw = tile("x_raw", [P, PACK, R], F32, "plane0")
+        x_raw = tile("x_raw", [P, PACK, R], F32, 0)
         nc.sync.dma_start(out=x_raw[:], in_=xT[0].rearrange("(p j) r -> p j r", j=PACK))
-        y_sb = tile("y_sb", [P, PACK, N], F32, "plane1")
+        y_sb = tile("y_sb", [P, PACK, N], F32, "plane0")
         nc.sync.dma_start(out=y_sb[:], in_=y[0].rearrange("(p t) i -> p t i", t=PACK))
-        xm_raw = tile("xm_raw", [P, PACK, D], F32, "plane2")
+        xm_raw = tile("xm_raw", [P, PACK, D], F32, "plane1")
         nc.sync.dma_start(out=xm_raw[:], in_=xm[0].rearrange("(p t) d -> p t d", t=PACK))
         scores = [bank(f"A{j}", f"scores{j}") for j in range(CHUNKS)]
         w_q = [operand("w0", HALF)]
         quantize(w_q[0], 0, HALF, w_bf[:, 0 : HALF * PACK], E4M3)
 
-        x_bf = [tile(f"x_bf{u}", [P, R * 2], BF16, ("x_bf0", "wt_sb")[u]) for u in range(2)]
+        x_bf = [tile(f"x_bf{u}", [P, R * 2], BF16, (46, 48)[u]) for u in range(2)]
         for copy, u, lo, hi in (
             (nc.vector.tensor_copy, 0, 0, P),
             (nc.scalar.copy, 1, X_SPLIT, P),
@@ -162,10 +169,10 @@ def tile_attend_gcau_wx_ts_kernel(tc, xT, wT, y, wt, ts, xm, offs, out_0, out_1)
         turn(w_bf, 1, w_turn1)
         for u in range(2):
             quantize(x_q, u * R // 2, (u + 1) * R // 2, x_bf[u][:], E4M3)
-        w_q.append(operand("w1", HALF, "x_bf0"))
+        w_q.append(operand("w1", HALF, 46))
         quantize(w_q[1], 0, HALF, w_bf[:, HALF * PACK : N * PACK], E4M3)
-        wi_q = operand("wi", D, "wt_sb")
-        wi_bf.append(tile("wi_bf1", [P, D * PACK // 2], BF16, "plane0"))
+        wi_q = operand("wi", D, 48)
+        wi_bf.append(tile("wi_bf1", [P, D * PACK // 2], BF16, 0))
         nc.scalar.copy(
             out=wi_bf[1][:].rearrange("g (p e s) -> g p e s", e=2, s=PACK),
             in_=w_turn1[:].bitcast(BF16).rearrange("g (s p e) -> g p e s", s=PACK, e=2),

@@ -351,13 +351,14 @@ def tile_attend_gcau_wx_ts_kernel(tc, xT, wT, y, wt, ts, xm, offs, out_0, out_1)
         hi_bf0 = h_by_slots(0, "B0")
         dw1 = block_in_sbuf(1, "A2")
         hi_bf1 = h_by_slots(1, "A1")
+        dw2 = block_in_sbuf(2, "B0")
         quantize_hi(0, hi_bf0)
         scatter(1, dw1, 0, N)
         row_block(0, "C0")
         row_block(1, "C1")
-        dw2 = block_in_sbuf(2, "A1")
+        dw3 = block_in_sbuf(3, "A2")
         quantize_hi(1, hi_bf1)
         scatter(2, dw2, 0, N)
         row_block(2, "B1")
-        row_block(3, "B0")
-        scatter(3, block_in_sbuf(3, "C0"), 0, N)
+        row_block(3, "A3")
+        scatter(3, dw3, 0, N)

@@ -26,7 +26,7 @@ CHUNKS = 4
 DIRECT = (0, 3)
 X_SPLIT = 32
 SCORE_ORDER = (0, 1, 2, 3)
-VECTOR_SQUARES = ()
+VECTOR_SQUARE = 512
 WINDOWS = 3
 VECTOR_MEMSETS = 1
 
@@ -205,8 +205,8 @@ def tile_attend_gcau_wx_ts_kernel(tc, xT, wT, y, wt, ts, xm, offs, out_0, out_1)
             quantize(xm_q, lo, hi, xm_bf[:], E4M3)
 
         h_bf = tile("h_bf", [P, N * PACK], BF16)
-        q, sq, root, rec, num = ([tile(f"{kind}{j}", [P, R], F32) for j in range(CHUNKS)] for kind in ("q", "sq", "root", "rec", "num"))
-        a = [tile(f"a{j}", [P, R], F32, ("a0", "a1", "a2", "a1")[j]) for j in range(CHUNKS)]
+        a = [tile(f"a{j}", [P, R], F32, ("a0", "a1", "a2", "a3")[j]) for j in range(CHUNKS)]
+        q, sq, root, rec, num = ([tile(f"{kind}{j}", [P, R], F32, "a1" if (kind, j) == ("q", 3) else None) for j in range(CHUNKS)] for kind in ("q", "sq", "root", "rec", "num"))
 
         def planes_of(flat):
             return flat[:].rearrange("p (t i) -> p t i", t=PACK)
@@ -225,14 +225,15 @@ def tile_attend_gcau_wx_ts_kernel(tc, xT, wT, y, wt, ts, xm, offs, out_0, out_1)
                 nc.tensor.transpose(turned[:, t * P : (t + 1) * P], a[j][:, t * P : (t + 1) * P], ident[:])
             return turned
 
-        def residual(j, scaled_chunk):
-            nc.vector.tensor_tensor(planes_of(q[j]), planes_of(scaled_chunk), y_sb[:, :, slots(j)], SUB)
+        def residual(j, scaled_chunk, engine=nc.vector):
+            engine.tensor_tensor(planes_of(q[j]), planes_of(scaled_chunk), y_sb[:, :, slots(j)], SUB)
 
         def square(j):
-            if j in VECTOR_SQUARES:
-                nc.vector.tensor_tensor(sq[j][:], q[j][:], q[j][:], MULT)
-            else:
-                nc.scalar.activation(out=sq[j][:], in_=q[j][:], func=ACT.Square)
+            lo = VECTOR_SQUARE if j == CHUNKS - 1 else 0
+            if lo:
+                nc.vector.tensor_tensor(sq[j][:, 0:lo], q[j][:, 0:lo], q[j][:, 0:lo], MULT)
+            if lo < R:
+                nc.scalar.activation(out=sq[j][:, lo:R], in_=q[j][:, lo:R], func=ACT.Square)
 
         def roots(j):
             nc.scalar.activation(out=root[j][:], in_=sq[j][:], func=ACT.Abs_reciprocal_sqrt, bias=ones[:])
@@ -276,14 +277,14 @@ def tile_attend_gcau_wx_ts_kernel(tc, xT, wT, y, wt, ts, xm, offs, out_0, out_1)
         quantize_wi(1)
         residual(0, s0)
         square(0)
-        numerator(0)
+        numerator(0, nc.gpsimd)
+        s3 = times_ts(3)
         residual(1, s1)
         roots(0)
         square(1)
-        s3 = times_ts(3)
         residual(2, s2)
-        inverses(0)
         residual(3, s3)
+        inverses(0)
         roots(1)
         square(2)
         numerator(1)

@@ -22,25 +22,22 @@ P = 128
 PACK = 4
 HALF = N // 2
 CHUNK = 128
-CHUNKS = 4
-DIRECT = (0, 3)
+CHUNKS = N // CHUNK
+TURNED = (1, 2)
+VECTOR_SQUARE = CHUNKS - 1
+GPSIMD_NUMERATOR = 0
 X_SPLIT = 32
-SCORE_ORDER = (0, 1, 2, 3)
-VECTOR_SQUARE = 512
 WINDOWS = 3
-VECTOR_MEMSETS = 1
+VECTOR_MEMSETS = 2
 
 
 def tile_attend_gcau_wx_ts_kernel(tc, xT, wT, y, wt, ts, xm, offs, out_0, out_1):
     nc = tc.nc
     with ExitStack() as ctx:
         sb = ctx.enter_context(tc.tile_pool(name="sb", bufs=1))
-        placed = ctx.enter_context(tc.tile_pool(name="placed", bufs=1))
         ps = ctx.enter_context(tc.psum_pool(name="ps", bufs=1))
 
         def tile(name, shape, dtype, buffer=None):
-            if isinstance(buffer, int):
-                return placed.tile(shape, dtype, name=name, offset=buffer * 1024, align_bytes=64)
             return sb.tile(shape, dtype, name=name, tag=buffer or name, align_bytes=64)
 
         def bank(tag, name):
@@ -64,37 +61,35 @@ def tile_attend_gcau_wx_ts_kernel(tc, xT, wT, y, wt, ts, xm, offs, out_0, out_1)
             )
 
         offsets = sb.tile([P, N // 16], U16, name="offsets")
-        ts_span = tile("ts_span", [P, 2 * T + 512], F32, 7)
-        ts_cols = ts_span[:, 0 : T // P]
+        ts_cols = tile("ts_cols", [P, T // P], F32)
         nc.sync.dma_start(out=ts_cols[:], in_=ts[0].rearrange("(p c) -> p c", p=P))
         wt_sb = tile("wt_sb", [P, PACK], F32)
         w_rows = wT.rearrange("(p t) c -> p t c", t=PACK)
-        planes = {t: tile(f"plane{t}", [P, T], F32) for t in (0, 1)}
-        planes[2] = tile("plane2", [P, T], F32)
+        planes = {t: tile(f"plane{t}", [P, T], F32) for t in (2, 0, 1)}
         nc.sync.dma_start(out=planes[2][:], in_=w_rows[:, 2, :])
         nc.sync.dma_start(offsets[:], offs)
         nc.sync.dma_start(out=wt_sb[:], in_=wt[0].rearrange("(p t) o -> p (t o)", t=PACK))
         for t in range(2):
             nc.sync.dma_start(out=planes[t][:], in_=w_rows[:, t, :])
 
-        ones = tile("ones", [P, 1], F32)
-        nc.vector.memset(ones[:], 1.0)
-        seed = tile("seed", [P, 1], F32, 38)
-        nc.vector.memset(seed[:, 0:1], 1.0)
-        warm = tile("warm", [P, 1], F32)
-        nc.scalar.activation(out=warm[:], in_=seed[:, 0:1], func=ACT.Abs_reciprocal_sqrt, bias=ones[:])
+        zero = tile("zero", [P, 1], F32)
+        nc.vector.memset(zero[:], 0.0)
+        one = tile("one", [P, 1], F32)
+        nc.vector.memset(one[:], 1.0)
+        root_bias = tile("root_bias", [P, 1], F32)
+        nc.scalar.activation(out=root_bias[:], in_=zero[:], func=ACT.Abs_reciprocal_sqrt, bias=one[:])
         ident = tile("ident", [P, P], F32)
         make_identity(nc, ident[:])
 
         h_q = operand("h", HALF + N)
         nc.gpsimd.memset(h_q[0][:, 0:HALF].bitcast(I32), 0)
         nc.gpsimd.memset(h_q[1][:, 0:HALF].bitcast(I32), 0)
-        windows = [tile(f"window{m}", [P, T], F32, (38, 16, 24)[m]) for m in range(WINDOWS)]
+        windows = [tile(f"window{m}", [P, T], F32) for m in range(WINDOWS)]
         for m in range(WINDOWS):
             engine = nc.vector if m < VECTOR_MEMSETS else nc.gpsimd
             engine.memset(windows[m][:].bitcast(I32), 0)
 
-        ts_win = tile("ts_win", [P, T], F32, 47)
+        ts_win = tile("ts_win", [P, T], F32)
         for g in range(PACK):
             spread = bank(f"A{g}", f"spread{g}")
             for e in range(PACK):
@@ -111,16 +106,16 @@ def tile_attend_gcau_wx_ts_kernel(tc, xT, wT, y, wt, ts, xm, offs, out_0, out_1)
         x_q = operand("x")
         w_bf = tile("w_bf", [P, N * PACK], BF16)
         nc.vector.tensor_copy(w_bf[:, 2 : N * PACK : PACK], planes[2][:].indirect(offsets[:]))
-        planes[3] = tile("plane3", [P, T], F32, 8)
+        planes[3] = tile("plane3", [P, T], F32, "plane2")
         nc.sync.dma_start(out=planes[3][:], in_=w_rows[:, 3, :])
         nc.vector.tensor_copy(ts_all[:], ts_win[:].indirect(offsets[:]))
         ts_turn = bank("C0", "ts_turn")
-        for j in (1, 2):
+        for j in TURNED:
             nc.tensor.transpose(ts_turn[:, j * P : (j + 1) * P], ts_all[:, j * P : (j + 1) * P], ident[:])
         for t in range(PACK):
             nc.scalar.activation(out=factor[:, t, :], in_=ts_all[:], func=ACT.Copy, scale=wt_sb[:, t : t + 1])
-        nc.scalar.copy(out=ts_slot[:, 1:3], in_=ts_turn[:, P : 3 * P : P])
-        picked = tile("picked", [P, 2, N], BF16, 47)
+        nc.scalar.copy(out=ts_slot[:, TURNED[0] : TURNED[-1] + 1], in_=ts_turn[:, TURNED[0] * P : (TURNED[-1] + 1) * P : P])
+        picked = tile("picked", [P, 2, N], BF16, "ts_win")
         for t in range(2):
             nc.vector.tensor_copy(picked[:, t, :], planes[t][:].indirect(offsets[:]))
         nc.scalar.copy(out=w_bf[:].rearrange("p (i t) -> p i t", t=PACK)[:, :, 0:2], in_=picked[:].rearrange("p t i -> p i t"))
@@ -139,17 +134,17 @@ def tile_attend_gcau_wx_ts_kernel(tc, xT, wT, y, wt, ts, xm, offs, out_0, out_1)
             nc.vector.tensor_copy(
                 w_bf[:, lo * PACK + 3 : (lo + HALF) * PACK : PACK], planes[3][:].indirect(offsets[:, lo // 16 : (lo + HALF) // 16])
             )
-        x_raw = tile("x_raw", [P, PACK, R], F32, 0)
+        x_raw = tile("x_raw", [P, PACK, R], F32, "plane0")
         nc.sync.dma_start(out=x_raw[:], in_=xT[0].rearrange("(p j) r -> p j r", j=PACK))
-        y_sb = tile("y_sb", [P, PACK, N], F32, "plane0")
+        y_sb = tile("y_sb", [P, PACK, N], F32, "plane1")
         nc.sync.dma_start(out=y_sb[:], in_=y[0].rearrange("(p t) i -> p t i", t=PACK))
-        xm_raw = tile("xm_raw", [P, PACK, D], F32, "plane1")
+        xm_raw = tile("xm_raw", [P, PACK, D], F32, "plane2")
         nc.sync.dma_start(out=xm_raw[:], in_=xm[0].rearrange("(p t) d -> p t d", t=PACK))
         scores = [bank(f"A{j}", f"scores{j}") for j in range(CHUNKS)]
         w_q = [operand("w0", HALF)]
         quantize(w_q[0], 0, HALF, w_bf[:, 0 : HALF * PACK], E4M3)
 
-        x_bf = [tile(f"x_bf{u}", [P, R * 2], BF16, (46, 48)[u]) for u in range(2)]
+        x_bf = [tile(f"x_bf{u}", [P, R * 2], BF16, ("x_bf0", "wt_sb")[u]) for u in range(2)]
         for copy, u, lo, hi in (
             (nc.vector.tensor_copy, 0, 0, P),
             (nc.scalar.copy, 1, X_SPLIT, P),
@@ -169,10 +164,10 @@ def tile_attend_gcau_wx_ts_kernel(tc, xT, wT, y, wt, ts, xm, offs, out_0, out_1)
         turn(w_bf, 1, w_turn1)
         for u in range(2):
             quantize(x_q, u * R // 2, (u + 1) * R // 2, x_bf[u][:], E4M3)
-        w_q.append(operand("w1", HALF, 46))
+        w_q.append(operand("w1", HALF, "x_bf0"))
         quantize(w_q[1], 0, HALF, w_bf[:, HALF * PACK : N * PACK], E4M3)
-        wi_q = operand("wi", D, 48)
-        wi_bf.append(tile("wi_bf1", [P, D * PACK // 2], BF16, 0))
+        wi_q = operand("wi", D, "wt_sb")
+        wi_bf.append(tile("wi_bf1", [P, D * PACK // 2], BF16, "plane0"))
         nc.scalar.copy(
             out=wi_bf[1][:].rearrange("g (p e s) -> g p e s", e=2, s=PACK),
             in_=w_turn1[:].bitcast(BF16).rearrange("g (s p e) -> g p e s", s=PACK, e=2),
@@ -183,13 +178,13 @@ def tile_attend_gcau_wx_ts_kernel(tc, xT, wT, y, wt, ts, xm, offs, out_0, out_1)
 
         quantize_wi(0)
 
-        for j in SCORE_ORDER:
-            w_cols = slice(j % 2 * CHUNK, (j % 2 + 1) * CHUNK)
-            if j in DIRECT:
-                for t in range(PACK):
-                    mx(scores[j][:, t * P : (t + 1) * P], x_q, E4M3, slice(t * P, (t + 1) * P), w_q[j // 2], E4M3, w_cols)
+        for j in range(CHUNKS):
+            w_half, w_cols = w_q[j * CHUNK // HALF], slice(j * CHUNK % HALF, j * CHUNK % HALF + CHUNK)
+            if j in TURNED:
+                mx(scores[j][:], w_half, E4M3, w_cols, x_q, E4M3, slice(0, R))
             else:
-                mx(scores[j][:], w_q[j // 2], E4M3, w_cols, x_q, E4M3, slice(0, R))
+                for t in range(PACK):
+                    mx(scores[j][:, t * P : (t + 1) * P], x_q, E4M3, slice(t * P, (t + 1) * P), w_half, E4M3, w_cols)
 
         xm_q = operand("xm")
 
@@ -205,8 +200,9 @@ def tile_attend_gcau_wx_ts_kernel(tc, xT, wT, y, wt, ts, xm, offs, out_0, out_1)
             quantize(xm_q, lo, hi, xm_bf[:], E4M3)
 
         h_bf = tile("h_bf", [P, N * PACK], BF16)
-        a = [tile(f"a{j}", [P, R], F32, ("a0", "a1", "a2", "a3")[j]) for j in range(CHUNKS)]
-        q, sq, root, rec, num = ([tile(f"{kind}{j}", [P, R], F32, "a1" if (kind, j) == ("q", 3) else None) for j in range(CHUNKS)] for kind in ("q", "sq", "root", "rec", "num"))
+        a = [tile(f"a{j}", [P, R], F32) for j in range(CHUNKS)]
+        q = [tile(f"q{j}", [P, R], F32, "a1" if j == CHUNKS - 1 else None) for j in range(CHUNKS)]
+        sq, root, rec, num = ([tile(f"{kind}{j}", [P, R], F32) for j in range(CHUNKS)] for kind in ("sq", "root", "rec", "num"))
 
         def planes_of(flat):
             return flat[:].rearrange("p (t i) -> p t i", t=PACK)
@@ -215,33 +211,33 @@ def tile_attend_gcau_wx_ts_kernel(tc, xT, wT, y, wt, ts, xm, offs, out_0, out_1)
             return slice(j * CHUNK, (j + 1) * CHUNK)
 
         def times_ts(j):
-            if j in DIRECT:
+            if j not in TURNED:
                 ts_chunk = ts_all[:, slots(j)].unsqueeze(1).to_broadcast([P, PACK, CHUNK])
                 nc.vector.tensor_tensor(planes_of(a[j]), planes_of(scores[j]), ts_chunk, MULT)
                 return a[j]
             nc.scalar.activation(out=a[j][:], in_=scores[j][:], func=ACT.Copy, scale=ts_slot[:, j : j + 1])
-            turned = bank(f"B{j - 1}", f"turned{j}")
+            turned = bank(f"B{TURNED.index(j)}", f"turned{j}")
             for t in range(PACK):
                 nc.tensor.transpose(turned[:, t * P : (t + 1) * P], a[j][:, t * P : (t + 1) * P], ident[:])
             return turned
 
-        def residual(j, scaled_chunk, engine=nc.vector):
-            engine.tensor_tensor(planes_of(q[j]), planes_of(scaled_chunk), y_sb[:, :, slots(j)], SUB)
+        def residual(j, scaled_chunk):
+            nc.vector.tensor_tensor(planes_of(q[j]), planes_of(scaled_chunk), y_sb[:, :, slots(j)], SUB)
 
         def square(j):
-            lo = VECTOR_SQUARE if j == CHUNKS - 1 else 0
-            if lo:
-                nc.vector.tensor_tensor(sq[j][:, 0:lo], q[j][:, 0:lo], q[j][:, 0:lo], MULT)
-            if lo < R:
-                nc.scalar.activation(out=sq[j][:, lo:R], in_=q[j][:, lo:R], func=ACT.Square)
+            if j == VECTOR_SQUARE:
+                nc.vector.tensor_tensor(sq[j][:], q[j][:], q[j][:], MULT)
+            else:
+                nc.scalar.activation(out=sq[j][:], in_=q[j][:], func=ACT.Square)
 
-        def roots(j):
-            nc.scalar.activation(out=root[j][:], in_=sq[j][:], func=ACT.Abs_reciprocal_sqrt, bias=ones[:])
+        def inverse_root(j):
+            nc.scalar.activation(out=root[j][:], in_=sq[j][:], func=ACT.Abs_reciprocal_sqrt, bias=root_bias[:])
 
-        def inverses(j):
+        def inverse(j):
             nc.scalar.activation(out=rec[j][:], in_=root[j][:], func=ACT.Square)
 
-        def numerator(j, engine=nc.vector):
+        def numerator(j):
+            engine = nc.gpsimd if j == GPSIMD_NUMERATOR else nc.vector
             engine.tensor_tensor(planes_of(num[j]), planes_of(q[j]), factor[:, :, slots(j)], MULT)
 
         def finish(j):
@@ -266,8 +262,7 @@ def tile_attend_gcau_wx_ts_kernel(tc, xT, wT, y, wt, ts, xm, offs, out_0, out_1)
             return dw
 
         def scatter(m, dw, lo, hi):
-            target = windows[m % WINDOWS][:].indirect(offsets[:, lo // 16 : hi // 16])
-            nc.vector.tensor_copy(target, dw[:])
+            nc.vector.tensor_copy(windows[m % WINDOWS][:].indirect(offsets[:, lo // 16 : hi // 16]), dw[:])
             if hi == N:
                 nc.sync.dma_start(out=out_0[m * P : (m + 1) * P, :], in_=windows[m % WINDOWS][:])
 
@@ -277,34 +272,33 @@ def tile_attend_gcau_wx_ts_kernel(tc, xT, wT, y, wt, ts, xm, offs, out_0, out_1)
         quantize_wi(1)
         residual(0, s0)
         square(0)
-        numerator(0, nc.gpsimd)
+        numerator(0)
         s3 = times_ts(3)
         residual(1, s1)
-        roots(0)
+        inverse_root(0)
         square(1)
         residual(2, s2)
         residual(3, s3)
-        inverses(0)
-        roots(1)
+        inverse(0)
+        inverse_root(1)
         square(2)
         numerator(1)
-        inverses(1)
+        inverse(1)
         finish(0)
         xm0 = xm_block(0, P, nc.vector.tensor_copy, "num0")
         square(3)
         numerator(2)
         quantize_xm(0, P, xm0)
         finish(1)
-        roots(2)
-        roots(3)
+        inverse_root(2)
+        inverse_root(3)
         numerator(3)
         quantize_h(0, HALF)
         early = table_product(0, "A0", "dw_acc_early", 0)
-        inverses(2)
-        inverses(3)
+        inverse(2)
+        inverse(3)
         finish(2)
-        dw_early = tile("dw_early", [P, HALF], F32, "root3")
-        nc.scalar.copy(out=dw_early[:], in_=early[:, HALF:N])
+        dw_early = to_sbuf(early, HALF, N, "dw_early", "root3")
         xm1 = xm_block(P, 2 * P, nc.scalar.copy, "root2")
         finish(3)
         quantize_h(HALF, HALF + CHUNK)
@@ -326,7 +320,7 @@ def tile_attend_gcau_wx_ts_kernel(tc, xT, wT, y, wt, ts, xm, offs, out_0, out_1)
         def h_by_slots(u, tag):
             h_turn = bank(tag, f"h_turn{u}")
             turn(h_bf, u, h_turn)
-            hi_bf = tile(f"hi_bf{u}", [P, R * 2], BF16, ("rec3", "hi_bf1")[u])
+            hi_bf = tile(f"hi_bf{u}", [P, R * 2], BF16, "rec3" if u == 0 else None)
             nc.scalar.copy(
                 out=hi_bf[:].rearrange("g (e p s) -> g e p s", e=2, s=PACK),
                 in_=h_turn[:].bitcast(BF16).rearrange("g (s p e) -> g e p s", s=PACK, e=2),

@@ -65,12 +65,18 @@ def tile_attend_gcau_wx_ts_kernel(tc, xT, wT, y, wt, ts, xm, offs, out_0, out_1)
         nc.sync.dma_start(out=ts_cols[:], in_=ts[0].rearrange("(p c) -> p c", p=P))
         wt_sb = tile("wt_sb", [P, PACK], F32)
         w_rows = wT.rearrange("(p t) c -> p t c", t=PACK)
-        planes = {t: tile(f"plane{t}", [P, T], F32) for t in (2, 0, 1)}
+        planes = [tile(f"plane{t}", [P, T], F32) for t in range(PACK)]
         nc.sync.dma_start(out=planes[2][:], in_=w_rows[:, 2, :])
         nc.sync.dma_start(offsets[:], offs)
         nc.sync.dma_start(out=wt_sb[:], in_=wt[0].rearrange("(p t) o -> p (t o)", t=PACK))
-        for t in range(2):
+        for t in (0, 1, 3):
             nc.sync.dma_start(out=planes[t][:], in_=w_rows[:, t, :])
+        x_raw = tile("x_raw", [P, PACK, R], F32)
+        nc.sync.dma_start(out=x_raw[:], in_=xT[0].rearrange("(p j) r -> p j r", j=PACK))
+        y_sb = tile("y_sb", [P, PACK, N], F32)
+        nc.sync.dma_start(out=y_sb[:], in_=y[0].rearrange("(p t) i -> p t i", t=PACK))
+        xm_raw = tile("xm_raw", [P, PACK, D], F32)
+        nc.sync.dma_start(out=xm_raw[:], in_=xm[0].rearrange("(p t) d -> p t d", t=PACK))
 
         zero = tile("zero", [P, 1], F32)
         nc.vector.memset(zero[:], 0.0)
@@ -106,8 +112,6 @@ def tile_attend_gcau_wx_ts_kernel(tc, xT, wT, y, wt, ts, xm, offs, out_0, out_1)
         x_q = operand("x")
         w_bf = tile("w_bf", [P, N * PACK], BF16)
         nc.vector.tensor_copy(w_bf[:, 2 : N * PACK : PACK], planes[2][:].indirect(offsets[:]))
-        planes[3] = tile("plane3", [P, T], F32, "plane2")
-        nc.sync.dma_start(out=planes[3][:], in_=w_rows[:, 3, :])
         nc.vector.tensor_copy(ts_all[:], ts_win[:].indirect(offsets[:]))
         ts_turn = bank("C0", "ts_turn")
         for j in TURNED:
@@ -134,12 +138,6 @@ def tile_attend_gcau_wx_ts_kernel(tc, xT, wT, y, wt, ts, xm, offs, out_0, out_1)
             nc.vector.tensor_copy(
                 w_bf[:, lo * PACK + 3 : (lo + HALF) * PACK : PACK], planes[3][:].indirect(offsets[:, lo // 16 : (lo + HALF) // 16])
             )
-        x_raw = tile("x_raw", [P, PACK, R], F32, "plane0")
-        nc.sync.dma_start(out=x_raw[:], in_=xT[0].rearrange("(p j) r -> p j r", j=PACK))
-        y_sb = tile("y_sb", [P, PACK, N], F32, "plane1")
-        nc.sync.dma_start(out=y_sb[:], in_=y[0].rearrange("(p t) i -> p t i", t=PACK))
-        xm_raw = tile("xm_raw", [P, PACK, D], F32, "plane2")
-        nc.sync.dma_start(out=xm_raw[:], in_=xm[0].rearrange("(p t) d -> p t d", t=PACK))
         scores = [bank(f"A{j}", f"scores{j}") for j in range(CHUNKS)]
         w_q = [operand("w0", HALF)]
         quantize(w_q[0], 0, HALF, w_bf[:, 0 : HALF * PACK], E4M3)
@@ -167,10 +165,10 @@ def tile_attend_gcau_wx_ts_kernel(tc, xT, wT, y, wt, ts, xm, offs, out_0, out_1)
         w_q.append(operand("w1", HALF, "x_bf0"))
         quantize(w_q[1], 0, HALF, w_bf[:, HALF * PACK : N * PACK], E4M3)
         wi_q = operand("wi", D, "wt_sb")
-        wi_bf.append(tile("wi_bf1", [P, D * PACK // 2], BF16, "plane0"))
+        wi_bf.append(tile("wi_bf1", [P, D * PACK // 2], BF16, "x_raw"))
         nc.scalar.copy(
-            out=wi_bf[1][:].rearrange("g (p e s) -> g p e s", e=2, s=PACK),
-            in_=w_turn1[:].bitcast(BF16).rearrange("g (s p e) -> g p e s", s=PACK, e=2),
+            out=wi_bf[1][:].rearrange("g (p e s) -> g p s e", e=2, s=PACK),
+            in_=w_turn1[:].bitcast(BF16).rearrange("g (s p e) -> g p s e", s=PACK, e=2),
         )
 
         def quantize_wi(u):
@@ -322,8 +320,8 @@ def tile_attend_gcau_wx_ts_kernel(tc, xT, wT, y, wt, ts, xm, offs, out_0, out_1)
             turn(h_bf, u, h_turn)
             hi_bf = tile(f"hi_bf{u}", [P, R * 2], BF16, "rec3" if u == 0 else None)
             nc.scalar.copy(
-                out=hi_bf[:].rearrange("g (e p s) -> g e p s", e=2, s=PACK),
-                in_=h_turn[:].bitcast(BF16).rearrange("g (s p e) -> g e p s", s=PACK, e=2),
+                out=hi_bf[:].rearrange("g (e p s) -> g p s e", e=2, s=PACK),
+                in_=h_turn[:].bitcast(BF16).rearrange("g (s p e) -> g p s e", s=PACK, e=2),
             )
             return hi_bf
 

@@ -73,10 +73,15 @@ def tile_attend_gcau_wx_ts_kernel(tc, xT, wT, y, wt, ts, xm, offs, out_0, out_1)
             nc.sync.dma_start(out=planes[t][:], in_=w_rows[:, t, :])
         x_raw = tile("x_raw", [P, PACK, R], F32)
         nc.sync.dma_start(out=x_raw[:], in_=xT[0].rearrange("(p j) r -> p j r", j=PACK))
-        y_sb = tile("y_sb", [P, PACK, N], F32)
-        nc.sync.dma_start(out=y_sb[:], in_=y[0].rearrange("(p t) i -> p t i", t=PACK))
-        xm_raw = tile("xm_raw", [P, PACK, D], F32)
-        nc.sync.dma_start(out=xm_raw[:], in_=xm[0].rearrange("(p t) d -> p t d", t=PACK))
+        y_rows = y[0].rearrange("(p t) i -> p t i", t=PACK)
+        xm_rows = xm[0].rearrange("(p t) d -> p t d", t=PACK)
+        y_sb = [tile(f"y_sb{u}", [P, PACK, HALF], F32) for u in range(2)]
+        xm_first = tile("xm_first", [P, PACK, P], F32)
+        xm_rest = tile("xm_rest", [P, PACK, D - P], F32)
+        nc.sync.dma_start(out=xm_first[:], in_=xm_rows[:, :, 0:P])
+        nc.sync.dma_start(out=y_sb[0][:], in_=y_rows[:, :, 0:HALF])
+        nc.sync.dma_start(out=y_sb[1][:], in_=y_rows[:, :, HALF:N])
+        nc.sync.dma_start(out=xm_rest[:], in_=xm_rows[:, :, P:D])
 
         zero = tile("zero", [P, 1], F32)
         nc.vector.memset(zero[:], 0.0)
@@ -190,7 +195,7 @@ def tile_attend_gcau_wx_ts_kernel(tc, xT, wT, y, wt, ts, xm, offs, out_0, out_1)
             xm_bf = tile(f"xm_bf{lo}", [P, (hi - lo) * PACK], BF16, buffer)
             copy(
                 out=xm_bf[:].rearrange("p (c e t) -> p c t e", e=PACK, t=PACK),
-                in_=xm_raw[:, :, lo:hi].rearrange("p t (c e) -> p c t e", e=PACK),
+                in_=(xm_first[:] if lo == 0 else xm_rest[:, :, lo - P : hi - P]).rearrange("p t (c e) -> p c t e", e=PACK),
             )
             return xm_bf
 
@@ -220,19 +225,19 @@ def tile_attend_gcau_wx_ts_kernel(tc, xT, wT, y, wt, ts, xm, offs, out_0, out_1)
             return turned
 
         def residual(j, scaled_chunk):
-            nc.vector.tensor_tensor(planes_of(q[j]), planes_of(scaled_chunk), y_sb[:, :, slots(j)], SUB)
+            nc.vector.tensor_tensor(planes_of(q[j]), planes_of(scaled_chunk), y_sb[j // 2][:, :, slots(j % 2)], SUB)
 
-        def square(j):
+        def square(j, cols=slice(0, R)):
             if j == VECTOR_SQUARE:
                 nc.vector.tensor_tensor(sq[j][:], q[j][:], q[j][:], MULT)
             else:
-                nc.scalar.activation(out=sq[j][:], in_=q[j][:], func=ACT.Square)
+                nc.scalar.activation(out=sq[j][:, cols], in_=q[j][:, cols], func=ACT.Square)
 
-        def inverse_root(j):
-            nc.scalar.activation(out=root[j][:], in_=sq[j][:], func=ACT.Abs_reciprocal_sqrt, bias=root_bias[:])
+        def inverse_root(j, cols=slice(0, R)):
+            nc.scalar.activation(out=root[j][:, cols], in_=sq[j][:, cols], func=ACT.Abs_reciprocal_sqrt, bias=root_bias[:])
 
-        def inverse(j):
-            nc.scalar.activation(out=rec[j][:], in_=root[j][:], func=ACT.Square)
+        def inverse(j, cols=slice(0, R)):
+            nc.scalar.activation(out=rec[j][:, cols], in_=root[j][:, cols], func=ACT.Square)
 
         def numerator(j):
             engine = nc.gpsimd if j == GPSIMD_NUMERATOR else nc.vector
@@ -264,46 +269,50 @@ def tile_attend_gcau_wx_ts_kernel(tc, xT, wT, y, wt, ts, xm, offs, out_0, out_1)
             if hi == N:
                 nc.sync.dma_start(out=out_0[m * P : (m + 1) * P, :], in_=windows[m % WINDOWS][:])
 
+        quantize_xm(0, P, xm_block(0, P, nc.scalar.copy, None))
         s0 = times_ts(0)
         s1 = times_ts(1)
         s2 = times_ts(2)
         quantize_wi(1)
         residual(0, s0)
-        square(0)
+        halves = (slice(0, R // 2), slice(R // 2, R))
+        for cols in halves:
+            square(0, cols)
         numerator(0)
         s3 = times_ts(3)
         residual(1, s1)
-        inverse_root(0)
+        for cols in halves:
+            inverse_root(0, cols)
+        inverse(0, halves[0])
         square(1)
         residual(2, s2)
         residual(3, s3)
-        inverse(0)
+        inverse(0, halves[1])
         inverse_root(1)
-        square(2)
+        square(2, halves[0])
         numerator(1)
-        inverse(1)
-        finish(0)
-        xm0 = xm_block(0, P, nc.vector.tensor_copy, "num0")
         square(3)
-        numerator(2)
-        quantize_xm(0, P, xm0)
-        finish(1)
-        inverse_root(2)
-        inverse_root(3)
+        inverse(1)
+        square(2, halves[1])
+        finish(0)
         numerator(3)
+        finish(1)
+        inverse_root(3)
+        inverse_root(2)
+        numerator(2)
         quantize_h(0, HALF)
         early = table_product(0, "A0", "dw_acc_early", 0)
-        inverse(2)
         inverse(3)
-        finish(2)
-        dw_early = to_sbuf(early, HALF, N, "dw_early", "root3")
-        xm1 = xm_block(P, 2 * P, nc.scalar.copy, "root2")
+        inverse(2)
         finish(3)
-        quantize_h(HALF, HALF + CHUNK)
+        xm1 = xm_block(P, 2 * P, nc.scalar.copy, "rec1")
+        dw_early = to_sbuf(early, HALF, N, "dw_early")
+        finish(2)
         quantize_h(HALF + CHUNK, N)
+        quantize_h(HALF, HALF + CHUNK)
         quantize_xm(P, 2 * P, xm1)
-        xm2 = xm_block(2 * P, 3 * P, nc.scalar.copy, "root2")
-        xm3 = xm_block(3 * P, D, nc.scalar.copy, "rec3")
+        xm2 = xm_block(2 * P, 3 * P, nc.scalar.copy, "rec1")
+        xm3 = xm_block(3 * P, D, nc.scalar.copy, "rec2")
         scatter(0, dw_early, 0, HALF)
         late = table_product(0, "A1", "dw_acc_late")
         dw_late = to_sbuf(late, HALF, N, "dw_late")
@@ -318,7 +327,7 @@ def tile_attend_gcau_wx_ts_kernel(tc, xT, wT, y, wt, ts, xm, offs, out_0, out_1)
         def h_by_slots(u, tag):
             h_turn = bank(tag, f"h_turn{u}")
             turn(h_bf, u, h_turn)
-            hi_bf = tile(f"hi_bf{u}", [P, R * 2], BF16, "rec3" if u == 0 else None)
+            hi_bf = tile(f"hi_bf{u}", [P, R * 2], BF16, "rec2" if u == 0 else None)
             nc.scalar.copy(
                 out=hi_bf[:].rearrange("g (e p s) -> g p s e", e=2, s=PACK),
                 in_=h_turn[:].bitcast(BF16).rearrange("g (s p e) -> g p s e", s=PACK, e=2),

@@ -78,10 +78,12 @@ def tile_attend_gcau_wx_ts_kernel(tc, xT, wT, y, wt, ts, xm, offs, out_0, out_1)
         y_sb = [tile(f"y_sb{u}", [P, PACK, HALF], F32) for u in range(2)]
         xm_first = tile("xm_first", [P, PACK, P], F32)
         xm_rest = tile("xm_rest", [P, PACK, D - P], F32)
-        nc.sync.dma_start(out=xm_first[:], in_=xm_rows[:, :, 0:P])
         nc.sync.dma_start(out=y_sb[0][:], in_=y_rows[:, :, 0:HALF])
-        nc.sync.dma_start(out=y_sb[1][:], in_=y_rows[:, :, HALF:N])
-        nc.sync.dma_start(out=xm_rest[:], in_=xm_rows[:, :, P:D])
+        nc.sync.dma_start(out=xm_first[:], in_=xm_rows[:, :, 0:P])
+        for t in range(PACK):
+            nc.sync.dma_start(out=y_sb[1][:, t, :], in_=y_rows[:, t, HALF:N])
+        for t in range(PACK):
+            nc.sync.dma_start(out=xm_rest[:, t, :], in_=xm_rows[:, t, P:D])
 
         zero = tile("zero", [P, 1], F32)
         nc.vector.memset(zero[:], 0.0)
@@ -269,12 +271,13 @@ def tile_attend_gcau_wx_ts_kernel(tc, xT, wT, y, wt, ts, xm, offs, out_0, out_1)
             if hi == N:
                 nc.sync.dma_start(out=out_0[m * P : (m + 1) * P, :], in_=windows[m % WINDOWS][:])
 
-        quantize_xm(0, P, xm_block(0, P, nc.scalar.copy, None))
+        xm0 = xm_block(0, P, nc.scalar.copy, None)
         s0 = times_ts(0)
         s1 = times_ts(1)
         s2 = times_ts(2)
         quantize_wi(1)
         residual(0, s0)
+        quantize_xm(0, P, xm0)
         halves = (slice(0, R // 2), slice(R // 2, R))
         for cols in halves:
             square(0, cols)

@@ -27,7 +27,7 @@ TURNED = (1, 2)
 VECTOR_SQUARE = CHUNKS - 1
 GPSIMD_NUMERATOR = 0
 X_SPLIT = 32
-WINDOWS = 3
+WINDOWS = 4
 VECTOR_MEMSETS = 2
 
 
@@ -36,8 +36,11 @@ def tile_attend_gcau_wx_ts_kernel(tc, xT, wT, y, wt, ts, xm, offs, out_0, out_1)
     with ExitStack() as ctx:
         sb = ctx.enter_context(tc.tile_pool(name="sb", bufs=1))
         ps = ctx.enter_context(tc.psum_pool(name="ps", bufs=1))
+        shared = ctx.enter_context(tc.tile_pool(name="shared", bufs=1))
 
         def tile(name, shape, dtype, buffer=None):
+            if isinstance(buffer, int):
+                return shared.tile(shape, dtype, name=name, align_bytes=64, offset=buffer)
             return sb.tile(shape, dtype, name=name, tag=buffer or name, align_bytes=64)
 
         def bank(tag, name):
@@ -76,14 +79,13 @@ def tile_attend_gcau_wx_ts_kernel(tc, xT, wT, y, wt, ts, xm, offs, out_0, out_1)
         y_rows = y[0].rearrange("(p t) i -> p t i", t=PACK)
         xm_rows = xm[0].rearrange("(p t) d -> p t d", t=PACK)
         y_sb = [tile(f"y_sb{u}", [P, PACK, HALF], F32) for u in range(2)]
-        xm_first = tile("xm_first", [P, PACK, P], F32)
-        xm_rest = tile("xm_rest", [P, PACK, D - P], F32)
-        nc.sync.dma_start(out=y_sb[0][:], in_=y_rows[:, :, 0:HALF])
-        nc.sync.dma_start(out=xm_first[:], in_=xm_rows[:, :, 0:P])
-        for t in range(PACK):
-            nc.sync.dma_start(out=y_sb[1][:, t, :], in_=y_rows[:, t, HALF:N])
-        for t in range(PACK):
-            nc.sync.dma_start(out=xm_rest[:, t, :], in_=xm_rows[:, t, P:D])
+        xm_sb = [tile(f"xm_sb{u}", [P, PACK, D // 2], F32) for u in range(2)]
+        for u in range(2):
+            if u == 0:
+                nc.sync.dma_start(out=xm_sb[u][:], in_=xm_rows[:, :, u * D // 2 : (u + 1) * D // 2])
+            nc.sync.dma_start(out=y_sb[u][:], in_=y_rows[:, :, u * HALF : (u + 1) * HALF])
+            if u == 1:
+                nc.sync.dma_start(out=xm_sb[u][:], in_=xm_rows[:, :, u * D // 2 : (u + 1) * D // 2])
 
         zero = tile("zero", [P, 1], F32)
         nc.vector.memset(zero[:], 0.0)
@@ -94,13 +96,10 @@ def tile_attend_gcau_wx_ts_kernel(tc, xT, wT, y, wt, ts, xm, offs, out_0, out_1)
         ident = tile("ident", [P, P], F32)
         make_identity(nc, ident[:])
 
-        h_q = operand("h", HALF + N)
-        nc.gpsimd.memset(h_q[0][:, 0:HALF].bitcast(I32), 0)
-        nc.gpsimd.memset(h_q[1][:, 0:HALF].bitcast(I32), 0)
-        windows = [tile(f"window{m}", [P, T], F32) for m in range(WINDOWS)]
-        for m in range(WINDOWS):
-            engine = nc.vector if m < VECTOR_MEMSETS else nc.gpsimd
-            engine.memset(windows[m][:].bitcast(I32), 0)
+        h_q = operand("h")
+        windows = [tile(f"window{m}", [P, T], F32) for m in range(VECTOR_MEMSETS)]
+        for window in windows:
+            nc.vector.memset(window[:].bitcast(I32), 0)
 
         ts_win = tile("ts_win", [P, T], F32)
         for g in range(PACK):
@@ -129,6 +128,9 @@ def tile_attend_gcau_wx_ts_kernel(tc, xT, wT, y, wt, ts, xm, offs, out_0, out_1)
         picked = tile("picked", [P, 2, N], BF16, "ts_win")
         for t in range(2):
             nc.vector.tensor_copy(picked[:, t, :], planes[t][:].indirect(offsets[:]))
+        for m, plane in ((2, "plane2"), (3, "plane0")):
+            windows.append(tile(f"window{m}", [P, T], F32, plane))
+            nc.gpsimd.memset(windows[m][:].bitcast(I32), 0)
         nc.scalar.copy(out=w_bf[:].rearrange("p (i t) -> p i t", t=PACK)[:, :, 0:2], in_=picked[:].rearrange("p t i -> p i t"))
 
         w_turn0 = bank("C1", "w_turn0")
@@ -172,11 +174,6 @@ def tile_attend_gcau_wx_ts_kernel(tc, xT, wT, y, wt, ts, xm, offs, out_0, out_1)
         w_q.append(operand("w1", HALF, "x_bf0"))
         quantize(w_q[1], 0, HALF, w_bf[:, HALF * PACK : N * PACK], E4M3)
         wi_q = operand("wi", D, "wt_sb")
-        wi_bf.append(tile("wi_bf1", [P, D * PACK // 2], BF16, "x_raw"))
-        nc.scalar.copy(
-            out=wi_bf[1][:].rearrange("g (p e s) -> g p s e", e=2, s=PACK),
-            in_=w_turn1[:].bitcast(BF16).rearrange("g (s p e) -> g p s e", s=PACK, e=2),
-        )
 
         def quantize_wi(u):
             quantize(wi_q, u * D // 2, (u + 1) * D // 2, wi_bf[u][:], E4M3)
@@ -197,7 +194,7 @@ def tile_attend_gcau_wx_ts_kernel(tc, xT, wT, y, wt, ts, xm, offs, out_0, out_1)
             xm_bf = tile(f"xm_bf{lo}", [P, (hi - lo) * PACK], BF16, buffer)
             copy(
                 out=xm_bf[:].rearrange("p (c e t) -> p c t e", e=PACK, t=PACK),
-                in_=(xm_first[:] if lo == 0 else xm_rest[:, :, lo - P : hi - P]).rearrange("p t (c e) -> p c t e", e=PACK),
+                in_=xm_sb[lo // 256][:, :, lo % 256 : lo % 256 + hi - lo].rearrange("p t (c e) -> p c t e", e=PACK),
             )
             return xm_bf
 
@@ -207,7 +204,8 @@ def tile_attend_gcau_wx_ts_kernel(tc, xT, wT, y, wt, ts, xm, offs, out_0, out_1)
         h_bf = tile("h_bf", [P, N * PACK], BF16)
         a = [tile(f"a{j}", [P, R], F32) for j in range(CHUNKS)]
         q = [tile(f"q{j}", [P, R], F32, "a1" if j == CHUNKS - 1 else None) for j in range(CHUNKS)]
-        sq, root, rec, num = ([tile(f"{kind}{j}", [P, R], F32) for j in range(CHUNKS)] for kind in ("sq", "root", "rec", "num"))
+        sq, root, rec = ([tile(f"{kind}{j}", [P, R], F32) for j in range(CHUNKS)] for kind in ("sq", "root", "rec"))
+        num = [tile(f"num{j}", [P, R], F32, 1024 if j == 2 else None) for j in range(CHUNKS)]
 
         def planes_of(flat):
             return flat[:].rearrange("p (t i) -> p t i", t=PACK)
@@ -254,30 +252,38 @@ def tile_attend_gcau_wx_ts_kernel(tc, xT, wT, y, wt, ts, xm, offs, out_0, out_1)
             )
 
         def quantize_h(lo, hi):
-            quantize(h_q, HALF + lo, HALF + hi, h_bf[:, lo * PACK : hi * PACK], E5M2)
+            quantize(h_q, lo, hi, h_bf[:, lo * PACK : hi * PACK], E5M2)
 
-        def table_product(m, tag, name, start=HALF):
+        def table_product(m, tag, name, lo=0, hi=N):
             acc = bank(tag, name)
-            mx(acc[:], xm_q, E4M3, slice(m * P, (m + 1) * P), h_q, E5M2, slice(start, start + N))
+            mx(acc[:, 0 : hi - lo], xm_q, E4M3, slice(m * P, (m + 1) * P), h_q, E5M2, slice(lo, hi))
             return acc
 
-        def to_sbuf(acc, lo, hi, name, buffer=None):
-            dw = tile(name, [P, hi - lo], F32, buffer)
-            nc.scalar.copy(out=dw[:], in_=acc[:, lo:hi])
+        def to_sbuf(copy, acc, width, name, buffer=None):
+            dw = tile(name, [P, width], F32, buffer)
+            copy(out=dw[:], in_=acc[:, 0:width])
             return dw
 
-        def scatter(m, dw, lo, hi):
-            nc.vector.tensor_copy(windows[m % WINDOWS][:].indirect(offsets[:, lo // 16 : hi // 16]), dw[:])
-            if hi == N:
-                nc.sync.dma_start(out=out_0[m * P : (m + 1) * P, :], in_=windows[m % WINDOWS][:])
+        def store(m):
+            nc.sync.dma_start(out=out_0[m * P : (m + 1) * P, :], in_=windows[m][:])
 
-        xm0 = xm_block(0, P, nc.scalar.copy, None)
+        def vector_scatter(m, dw, lo, hi):
+            nc.vector.tensor_copy(windows[m][:].indirect(offsets[:, lo // 16 : hi // 16]), dw[:])
+
+        def scalar_scatter(m, dw, lo, hi):
+            for part in range(lo, hi, HALF):
+                nc.scalar.activation(
+                    out=windows[m][:].indirect(offsets[:, part // 16 : (part + HALF) // 16]),
+                    in_=dw[:, part - lo : part - lo + HALF],
+                    func=ACT.Copy,
+                )
+
+        xm01 = xm_block(0, 2 * P, nc.scalar.copy, "x_raw")
         s0 = times_ts(0)
         s1 = times_ts(1)
         s2 = times_ts(2)
-        quantize_wi(1)
+        quantize_xm(0, 2 * P, xm01)
         residual(0, s0)
-        quantize_xm(0, P, xm0)
         halves = (slice(0, R // 2), slice(R // 2, R))
         for cols in halves:
             square(0, cols)
@@ -304,34 +310,64 @@ def tile_attend_gcau_wx_ts_kernel(tc, xT, wT, y, wt, ts, xm, offs, out_0, out_1)
         inverse_root(2)
         numerator(2)
         quantize_h(0, HALF)
-        early = table_product(0, "A0", "dw_acc_early", 0)
+        FIRST, SECOND = (0, HALF), (HALF, N)
+        first = {0: table_product(0, "A0", "first0", *FIRST)}
+        first[1] = table_product(1, "C1", "first1", *FIRST)
         inverse(3)
         inverse(2)
         finish(3)
-        xm1 = xm_block(P, 2 * P, nc.scalar.copy, "rec1")
-        dw_early = to_sbuf(early, HALF, N, "dw_early")
         finish(2)
+
+        def first_copy(m, buffer=None):
+            return to_sbuf(nc.scalar.copy, first[m], HALF, f"dw_first{m}", buffer)
+
+        def second_copy(m, buffer=None):
+            return to_sbuf(nc.vector.tensor_copy, second[m], HALF, f"dw_second{m}", buffer)
+
+        f0 = first_copy(0, "root3")
+        f1 = first_copy(1, "root2")
+        scalar_scatter(0, f0, *FIRST)
         quantize_h(HALF + CHUNK, N)
+        xm2 = xm_block(2 * P, 3 * P, nc.vector.tensor_copy, 1024)
         quantize_h(HALF, HALF + CHUNK)
-        quantize_xm(P, 2 * P, xm1)
-        xm2 = xm_block(2 * P, 3 * P, nc.scalar.copy, "rec1")
-        xm3 = xm_block(3 * P, D, nc.scalar.copy, "rec2")
-        scatter(0, dw_early, 0, HALF)
-        late = table_product(0, "A1", "dw_acc_late")
-        dw_late = to_sbuf(late, HALF, N, "dw_late")
+        second = {0: table_product(0, "A1", "second0", *SECOND)}
+        second[1] = table_product(1, "A2", "second1", *SECOND)
+        xm3 = xm_block(3 * P, D, nc.vector.tensor_copy, 2048)
         quantize_xm(2 * P, 3 * P, xm2)
         quantize_xm(3 * P, D, xm3)
-        scatter(0, dw_late, HALF, N)
+        first[2] = table_product(2, "A3", "first2", *FIRST)
+        second[2] = table_product(2, "B0", "second2", *SECOND)
+        first[3] = table_product(3, "B1", "first3", *FIRST)
+        second[3] = table_product(3, "A0", "second3", *SECOND)
+        l01 = tile("dw_second01", [P, 2, HALF], F32, 512)
+        l0, l1 = l01[:, 0, :], l01[:, 1, :]
+        nc.vector.tensor_copy(l0, second[0][:, 0:HALF])
+        nc.vector.tensor_copy(l1, second[1][:, 0:HALF])
+        vector_scatter(0, l0, *SECOND)
+        store(0)
+        f2 = first_copy(2, 6144)
+        scalar_scatter(1, f1, *FIRST)
+        l2 = second_copy(2)
+        vector_scatter(1, l1, *SECOND)
+        store(1)
+        f3 = first_copy(3)
+        scalar_scatter(2, f2, *FIRST)
+        l3 = second_copy(3)
+        vector_scatter(2, l2, *SECOND)
+        store(2)
+        scalar_scatter(3, f3, *FIRST)
+        vector_scatter(3, l3, *SECOND)
+        store(3)
 
         hi_q = operand("hi")
-        gx = tile("gx", [P, PACK, D], F32)
+        gx = [tile(f"gx{u}", [P, 2, D], F32) for u in range(2)]
         gx_rows = out_1[0].rearrange("(p t) d -> p t d", t=PACK)
 
-        def h_by_slots(u, tag):
+        def h_by_slots(u, tag, copy, buffer):
             h_turn = bank(tag, f"h_turn{u}")
             turn(h_bf, u, h_turn)
-            hi_bf = tile(f"hi_bf{u}", [P, R * 2], BF16, "rec2" if u == 0 else None)
-            nc.scalar.copy(
+            hi_bf = tile(f"hi_bf{u}", [P, R * 2], BF16, buffer)
+            copy(
                 out=hi_bf[:].rearrange("g (e p s) -> g p s e", e=2, s=PACK),
                 in_=h_turn[:].bitcast(BF16).rearrange("g (s p e) -> g p s e", s=PACK, e=2),
             )
@@ -340,30 +376,30 @@ def tile_attend_gcau_wx_ts_kernel(tc, xT, wT, y, wt, ts, xm, offs, out_0, out_1)
         def quantize_hi(u, hi_bf):
             quantize(hi_q, u * R // 2, (u + 1) * R // 2, hi_bf[:], E5M2)
 
-        def row_block(t, tag):
+        def row_block(t, tag, copy):
             acc = bank(tag, f"gx_acc{t}")
             mx(acc[:], hi_q, E5M2, slice(t * P, (t + 1) * P), wi_q, E4M3, slice(0, D))
-            nc.scalar.copy(
-                out=gx[:, t, :].rearrange("r (p u e) -> r p u e", u=2, e=2),
+            copy(
+                out=gx[t // 2][:, t % 2, :].rearrange("r (p u e) -> r p u e", u=2, e=2),
                 in_=acc[:].rearrange("r (u p e) -> r p u e", u=2, e=2),
             )
-            if t % 2 == 1:
-                nc.scalar.dma_start(out=gx_rows[:, t - 1 : t + 1, :], in_=gx[:, t - 1 : t + 1, :])
 
-        def block_in_sbuf(m, tag):
-            return to_sbuf(table_product(m, tag, f"dw_acc{m}"), 0, N, f"dw{m}")
+        def store_rows(u):
+            nc.sync.dma_start(out=gx_rows[:, 2 * u : 2 * u + 2, :], in_=gx[u][:])
 
-        hi_bf0 = h_by_slots(0, "B0")
-        dw1 = block_in_sbuf(1, "A2")
-        hi_bf1 = h_by_slots(1, "A1")
-        dw2 = block_in_sbuf(2, "B0")
+        wi_bf.append(tile("wi_bf1", [P, D * PACK // 2], BF16, 4608))
+        nc.scalar.copy(
+            out=wi_bf[1][:].rearrange("g (p e s) -> g p s e", e=2, s=PACK),
+            in_=w_turn1[:].bitcast(BF16).rearrange("g (s p e) -> g p s e", s=PACK, e=2),
+        )
+        hi_bf0 = h_by_slots(0, "A1", nc.scalar.copy, 6656)
+        hi_bf1 = h_by_slots(1, "A2", nc.scalar.copy, "dw_first3")
+        quantize_wi(1)
         quantize_hi(0, hi_bf0)
-        scatter(1, dw1, 0, N)
-        row_block(0, "C0")
-        row_block(1, "C1")
-        dw3 = block_in_sbuf(3, "A2")
+        row_block(0, "C1", nc.vector.tensor_copy)
+        row_block(1, "A3", nc.vector.tensor_copy)
+        store_rows(0)
         quantize_hi(1, hi_bf1)
-        scatter(2, dw2, 0, N)
-        row_block(2, "B1")
-        row_block(3, "A3")
-        scatter(3, dw3, 0, N)
+        row_block(2, "B0", nc.scalar.copy)
+        row_block(3, "B1", nc.vector.tensor_copy)
+        store_rows(1)

@@ -26,6 +26,7 @@ CHUNKS = N // CHUNK
 TURNED = (1, 2)
 VECTOR_SQUARE = CHUNKS - 1
 GPSIMD_NUMERATOR = 0
+WEAVE_SPLIT = 352
 X_SPLIT = 32
 WINDOWS = 4
 VECTOR_MEMSETS = 2
@@ -66,15 +67,16 @@ def tile_attend_gcau_wx_ts_kernel(tc, xT, wT, y, wt, ts, xm, offs, out_0, out_1)
         offsets = sb.tile([P, N // 16], U16, name="offsets")
         ts_cols = tile("ts_cols", [P, T // P], F32)
         nc.sync.dma_start(out=ts_cols[:], in_=ts[0].rearrange("(p c) -> p c", p=P))
-        wt_sb = tile("wt_sb", [P, PACK], F32)
+        picked = tile("picked", [P, 5 * N], BF16, 10240)
+        wt_sb = picked[:, 4 * N : 4 * N + 2 * PACK].bitcast(F32)
         w_rows = wT.rearrange("(p t) c -> p t c", t=PACK)
         planes = [tile(f"plane{t}", [P, T], F32) for t in range(PACK)]
-        nc.sync.dma_start(out=planes[2][:], in_=w_rows[:, 2, :])
+        nc.sync.dma_start(out=planes[0][:], in_=w_rows[:, 0, :])
         nc.sync.dma_start(offsets[:], offs)
-        nc.sync.dma_start(out=wt_sb[:], in_=wt[0].rearrange("(p t) o -> p (t o)", t=PACK))
-        for t in (0, 1, 3):
+        nc.sync.dma_start(out=wt_sb, in_=wt[0].rearrange("(p t) o -> p (t o)", t=PACK))
+        for t in (1, 2, 3):
             nc.sync.dma_start(out=planes[t][:], in_=w_rows[:, t, :])
-        x_raw = tile("x_raw", [P, PACK, R], F32)
+        x_raw = tile("x_raw", [P, PACK, R], F32, 16384)
         nc.sync.dma_start(out=x_raw[:], in_=xT[0].rearrange("(p j) r -> p j r", j=PACK))
         y_rows = y[0].rearrange("(p t) i -> p t i", t=PACK)
         xm_rows = xm[0].rearrange("(p t) d -> p t d", t=PACK)
@@ -117,41 +119,57 @@ def tile_attend_gcau_wx_ts_kernel(tc, xT, wT, y, wt, ts, xm, offs, out_0, out_1)
 
         x_q = operand("x")
         w_bf = tile("w_bf", [P, N * PACK], BF16)
-        nc.vector.tensor_copy(w_bf[:, 2 : N * PACK : PACK], planes[2][:].indirect(offsets[:]))
-        nc.vector.tensor_copy(ts_all[:], ts_win[:].indirect(offsets[:]))
+        wi_q = operand("wi", D)
+
+        def plane_of(t, lo=0, hi=N):
+            return picked[:, t * N + lo : t * N + hi]
+
+        def turn_pair(u, tag):
+            dst = bank(tag, f"w_turn{u}")
+            for e in range(2):
+                slot_pairs = plane_of(2 * u + e).bitcast(F32)
+                for v in range(2):
+                    nc.tensor.transpose(dst[:, (2 * e + v) * P : (2 * e + v + 1) * P], slot_pairs[:, v : N // 2 : 2], ident[:])
+            return dst
+
+        def pair_to_sbuf(copy, turned_pair, dst):
+            copy(
+                out=dst.bitcast(F32).rearrange("g (p e v) -> g p e v", e=2, v=2),
+                in_=turned_pair[:].rearrange("g (e v p) -> g p e v", e=2, v=2),
+            )
+
+        def weave(copy, lo, hi):
+            copy(
+                out=w_bf[:, lo * PACK : hi * PACK].rearrange("p (c e t) -> p c t e", e=PACK, t=PACK),
+                in_=picked[:, 0 : PACK * N].rearrange("p (t i) -> p t i", t=PACK)[:, :, lo:hi].rearrange("p t (c e) -> p c t e", e=PACK),
+            )
+
+        nc.scalar.activation(out=ts_all[:], in_=ts_win[:].indirect(offsets[:]), func=ACT.Copy)
         ts_turn = bank("C0", "ts_turn")
         for j in TURNED:
             nc.tensor.transpose(ts_turn[:, j * P : (j + 1) * P], ts_all[:, j * P : (j + 1) * P], ident[:])
         for t in range(PACK):
             nc.scalar.activation(out=factor[:, t, :], in_=ts_all[:], func=ACT.Copy, scale=wt_sb[:, t : t + 1])
         nc.scalar.copy(out=ts_slot[:, TURNED[0] : TURNED[-1] + 1], in_=ts_turn[:, TURNED[0] * P : (TURNED[-1] + 1) * P : P])
-        picked = tile("picked", [P, 2, N], BF16, "ts_win")
-        for t in range(2):
-            nc.vector.tensor_copy(picked[:, t, :], planes[t][:].indirect(offsets[:]))
-        for m, plane in ((2, "plane2"), (3, "plane0")):
+        for t in range(3):
+            nc.vector.tensor_copy(plane_of(t), planes[t][:].indirect(offsets[:]))
+        for m, plane in ((2, "plane0"), (3, "plane1")):
             windows.append(tile(f"window{m}", [P, T], F32, plane))
             nc.gpsimd.memset(windows[m][:].bitcast(I32), 0)
-        nc.scalar.copy(out=w_bf[:].rearrange("p (i t) -> p i t", t=PACK)[:, :, 0:2], in_=picked[:].rearrange("p t i -> p i t"))
-
-        w_turn0 = bank("C1", "w_turn0")
-        for e in range(2):
-            slot_pairs = picked[:, e, :].bitcast(F32)
-            for v in range(2):
-                nc.tensor.transpose(w_turn0[:, (2 * e + v) * P : (2 * e + v + 1) * P], slot_pairs[:, v : N // 2 : 2], ident[:])
-        wi_bf = [tile("wi_bf0", [P, D * PACK // 2], BF16)]
-        nc.scalar.copy(
-            out=wi_bf[0][:].bitcast(F32).rearrange("g (p e v) -> g p e v", e=2, v=2),
-            in_=w_turn0[:].rearrange("g (e v p) -> g p e v", e=2, v=2),
-        )
-        for lo in (0, HALF):
-            nc.vector.tensor_copy(
-                w_bf[:, lo * PACK + 3 : (lo + HALF) * PACK : PACK], planes[3][:].indirect(offsets[:, lo // 16 : (lo + HALF) // 16])
-            )
+        wi_bf0 = picked[:, 3 * N : 5 * N]
+        pair_to_sbuf(nc.scalar.copy, turn_pair(0, "C1"), wi_bf0)
+        quantize(wi_q, 0, D // 2, wi_bf0, E4M3)
+        nc.vector.tensor_copy(plane_of(3, 0, HALF), planes[3][:].indirect(offsets[:, 0 : HALF // 16]))
+        nc.scalar.activation(out=plane_of(3, HALF, N), in_=planes[3][:].indirect(offsets[:, HALF // 16 : N // 16]), func=ACT.Copy)
+        weave(nc.vector.tensor_copy, 0, HALF)
+        weave(nc.scalar.copy, WEAVE_SPLIT, N)
+        weave(nc.vector.tensor_copy, HALF, WEAVE_SPLIT)
+        w_turn1 = turn_pair(1, "C0")
         scores = [bank(f"A{j}", f"scores{j}") for j in range(CHUNKS)]
         w_q = [operand("w0", HALF)]
         quantize(w_q[0], 0, HALF, w_bf[:, 0 : HALF * PACK], E4M3)
 
-        x_bf = [tile(f"x_bf{u}", [P, R * 2], BF16, ("x_bf0", "wt_sb")[u]) for u in range(2)]
+        x_bf = [tile(f"x_bf{u}", [P, R * 2], BF16, 10240 + 2048 * u) for u in range(2)]
         for copy, u, lo, hi in (
             (nc.vector.tensor_copy, 0, 0, P),
             (nc.scalar.copy, 1, X_SPLIT, P),
@@ -167,18 +185,12 @@ def tile_attend_gcau_wx_ts_kernel(tc, xT, wT, y, wt, ts, xm, offs, out_0, out_1)
             for s in range(PACK):
                 nc.tensor.transpose(dst_bank[:, s * P : (s + 1) * P], words[:, 2 * s + u : 2 * N : 2 * PACK], ident[:])
 
-        w_turn1 = bank("C0", "w_turn1")
-        turn(w_bf, 1, w_turn1)
         for u in range(2):
             quantize(x_q, u * R // 2, (u + 1) * R // 2, x_bf[u][:], E4M3)
-        w_q.append(operand("w1", HALF, "x_bf0"))
+        w_q.append(operand("w1", HALF, 10240))
         quantize(w_q[1], 0, HALF, w_bf[:, HALF * PACK : N * PACK], E4M3)
-        wi_q = operand("wi", D, "wt_sb")
-
-        def quantize_wi(u):
-            quantize(wi_q, u * D // 2, (u + 1) * D // 2, wi_bf[u][:], E4M3)
-
-        quantize_wi(0)
+        wi_bf1 = tile("wi_bf1", [P, D * PACK // 2], BF16, 12288)
+        pair_to_sbuf(nc.vector.tensor_copy, w_turn1, wi_bf1[:])
 
         for j in range(CHUNKS):
             w_half, w_cols = w_q[j * CHUNK // HALF], slice(j * CHUNK % HALF, j * CHUNK % HALF + CHUNK)
@@ -202,7 +214,7 @@ def tile_attend_gcau_wx_ts_kernel(tc, xT, wT, y, wt, ts, xm, offs, out_0, out_1)
             quantize(xm_q, lo, hi, xm_bf[:], E4M3)
 
         h_bf = tile("h_bf", [P, N * PACK], BF16)
-        a = [tile(f"a{j}", [P, R], F32) for j in range(CHUNKS)]
+        a = [tile(f"a{j}", [P, R], F32, {0: 26624, 3: 25600}.get(j)) for j in range(CHUNKS)]
         q = [tile(f"q{j}", [P, R], F32, "a1" if j == CHUNKS - 1 else None) for j in range(CHUNKS)]
         sq, root, rec = ([tile(f"{kind}{j}", [P, R], F32) for j in range(CHUNKS)] for kind in ("sq", "root", "rec"))
         num = [tile(f"num{j}", [P, R], F32, 1024 if j == 2 else None) for j in range(CHUNKS)]
@@ -278,12 +290,13 @@ def tile_attend_gcau_wx_ts_kernel(tc, xT, wT, y, wt, ts, xm, offs, out_0, out_1)
                     func=ACT.Copy,
                 )
 
-        xm01 = xm_block(0, 2 * P, nc.scalar.copy, "x_raw")
+        xm01 = xm_block(0, 2 * P, nc.scalar.copy, 18432)
         s0 = times_ts(0)
         s1 = times_ts(1)
         s2 = times_ts(2)
-        quantize_xm(0, 2 * P, xm01)
+        quantize(wi_q, D // 2, D, wi_bf1[:], E4M3)
         residual(0, s0)
+        quantize_xm(0, 2 * P, xm01)
         halves = (slice(0, R // 2), slice(R // 2, R))
         for cols in halves:
             square(0, cols)
@@ -387,19 +400,13 @@ def tile_attend_gcau_wx_ts_kernel(tc, xT, wT, y, wt, ts, xm, offs, out_0, out_1)
         def store_rows(u):
             nc.sync.dma_start(out=gx_rows[:, 2 * u : 2 * u + 2, :], in_=gx[u][:])
 
-        wi_bf.append(tile("wi_bf1", [P, D * PACK // 2], BF16, 4608))
-        nc.scalar.copy(
-            out=wi_bf[1][:].rearrange("g (p e s) -> g p s e", e=2, s=PACK),
-            in_=w_turn1[:].bitcast(BF16).rearrange("g (s p e) -> g p s e", s=PACK, e=2),
-        )
         hi_bf0 = h_by_slots(0, "A1", nc.scalar.copy, 6656)
-        hi_bf1 = h_by_slots(1, "A2", nc.scalar.copy, "dw_first3")
-        quantize_wi(1)
+        hi_bf1 = h_by_slots(1, "A2", nc.scalar.copy, 4608)
         quantize_hi(0, hi_bf0)
         row_block(0, "C1", nc.vector.tensor_copy)
-        row_block(1, "A3", nc.vector.tensor_copy)
+        row_block(1, "A3", nc.scalar.copy)
         store_rows(0)
         quantize_hi(1, hi_bf1)
-        row_block(2, "B0", nc.scalar.copy)
-        row_block(3, "B1", nc.vector.tensor_copy)
+        row_block(2, "B0", nc.vector.tensor_copy)
+        row_block(3, "B1", nc.scalar.copy)
         store_rows(1)

@@ -81,13 +81,12 @@ def tile_attend_gcau_wx_ts_kernel(tc, xT, wT, y, wt, ts, xm, offs, out_0, out_1)
         y_rows = y[0].rearrange("(p t) i -> p t i", t=PACK)
         xm_rows = xm[0].rearrange("(p t) d -> p t d", t=PACK)
         y_sb = [tile(f"y_sb{u}", [P, PACK, HALF], F32) for u in range(2)]
-        xm_sb = [tile(f"xm_sb{u}", [P, PACK, D // 2], F32) for u in range(2)]
-        for u in range(2):
-            if u == 0:
-                nc.sync.dma_start(out=xm_sb[u][:], in_=xm_rows[:, :, u * D // 2 : (u + 1) * D // 2])
-            nc.sync.dma_start(out=y_sb[u][:], in_=y_rows[:, :, u * HALF : (u + 1) * HALF])
-            if u == 1:
-                nc.sync.dma_start(out=xm_sb[u][:], in_=xm_rows[:, :, u * D // 2 : (u + 1) * D // 2])
+        xm_first = tile("xm_first", [P, PACK, P], F32)
+        xm_rest = tile("xm_rest", [P, PACK, D - P], F32, 30720)
+        nc.sync.dma_start(out=y_sb[0][:], in_=y_rows[:, :, 0:HALF])
+        nc.sync.dma_start(out=xm_first[:], in_=xm_rows[:, :, 0:P])
+        nc.sync.dma_start(out=y_sb[1][:], in_=y_rows[:, :, HALF:N])
+        nc.sync.dma_start(out=xm_rest[:], in_=xm_rows[:, :, P:D])
 
         zero = tile("zero", [P, 1], F32)
         nc.vector.memset(zero[:], 0.0)
@@ -189,8 +188,8 @@ def tile_attend_gcau_wx_ts_kernel(tc, xT, wT, y, wt, ts, xm, offs, out_0, out_1)
             quantize(x_q, u * R // 2, (u + 1) * R // 2, x_bf[u][:], E4M3)
         w_q.append(operand("w1", HALF, 10240))
         quantize(w_q[1], 0, HALF, w_bf[:, HALF * PACK : N * PACK], E4M3)
-        wi_bf1 = tile("wi_bf1", [P, D * PACK // 2], BF16, 12288)
-        pair_to_sbuf(nc.vector.tensor_copy, w_turn1, wi_bf1[:])
+        wi_bf1 = tile("wi_bf1", [P, D * PACK // 2], BF16, 16384)
+        pair_to_sbuf(nc.scalar.copy, w_turn1, wi_bf1[:])
 
         for j in range(CHUNKS):
             w_half, w_cols = w_q[j * CHUNK // HALF], slice(j * CHUNK % HALF, j * CHUNK % HALF + CHUNK)
@@ -206,7 +205,7 @@ def tile_attend_gcau_wx_ts_kernel(tc, xT, wT, y, wt, ts, xm, offs, out_0, out_1)
             xm_bf = tile(f"xm_bf{lo}", [P, (hi - lo) * PACK], BF16, buffer)
             copy(
                 out=xm_bf[:].rearrange("p (c e t) -> p c t e", e=PACK, t=PACK),
-                in_=xm_sb[lo // 256][:, :, lo % 256 : lo % 256 + hi - lo].rearrange("p t (c e) -> p c t e", e=PACK),
+                in_=(xm_first[:] if lo == 0 else xm_rest[:, :, lo - P : hi - P]).rearrange("p t (c e) -> p c t e", e=PACK),
             )
             return xm_bf
 
@@ -290,13 +289,13 @@ def tile_attend_gcau_wx_ts_kernel(tc, xT, wT, y, wt, ts, xm, offs, out_0, out_1)
                     func=ACT.Copy,
                 )
 
-        xm01 = xm_block(0, 2 * P, nc.scalar.copy, 18432)
+        xm0 = xm_block(0, P, nc.scalar.copy, 18432)
         s0 = times_ts(0)
         s1 = times_ts(1)
         s2 = times_ts(2)
         quantize(wi_q, D // 2, D, wi_bf1[:], E4M3)
         residual(0, s0)
-        quantize_xm(0, 2 * P, xm01)
+        quantize_xm(0, P, xm0)
         halves = (slice(0, R // 2), slice(R // 2, R))
         for cols in halves:
             square(0, cols)
@@ -325,7 +324,6 @@ def tile_attend_gcau_wx_ts_kernel(tc, xT, wT, y, wt, ts, xm, offs, out_0, out_1)
         quantize_h(0, HALF)
         FIRST, SECOND = (0, HALF), (HALF, N)
         first = {0: table_product(0, "A0", "first0", *FIRST)}
-        first[1] = table_product(1, "C1", "first1", *FIRST)
         inverse(3)
         inverse(2)
         finish(3)
@@ -338,26 +336,27 @@ def tile_attend_gcau_wx_ts_kernel(tc, xT, wT, y, wt, ts, xm, offs, out_0, out_1)
             return to_sbuf(nc.vector.tensor_copy, second[m], HALF, f"dw_second{m}", buffer)
 
         f0 = first_copy(0, "root3")
-        f1 = first_copy(1, "root2")
+        xm2 = xm_block(2 * P, 3 * P, nc.scalar.copy, "root2")
         scalar_scatter(0, f0, *FIRST)
         quantize_h(HALF + CHUNK, N)
-        xm2 = xm_block(2 * P, 3 * P, nc.vector.tensor_copy, 1024)
+        xm1 = xm_block(P, 2 * P, nc.vector.tensor_copy, 1024)
         quantize_h(HALF, HALF + CHUNK)
         second = {0: table_product(0, "A1", "second0", *SECOND)}
+        quantize_xm(P, 2 * P, xm1)
+        first[1] = table_product(1, "C1", "first1", *FIRST)
         second[1] = table_product(1, "A2", "second1", *SECOND)
         xm3 = xm_block(3 * P, D, nc.vector.tensor_copy, 2048)
         quantize_xm(2 * P, 3 * P, xm2)
-        quantize_xm(3 * P, D, xm3)
         first[2] = table_product(2, "A3", "first2", *FIRST)
         second[2] = table_product(2, "B0", "second2", *SECOND)
+        l0 = second_copy(0, 30720)
+        quantize_xm(3 * P, D, xm3)
         first[3] = table_product(3, "B1", "first3", *FIRST)
         second[3] = table_product(3, "A0", "second3", *SECOND)
-        l01 = tile("dw_second01", [P, 2, HALF], F32, 512)
-        l0, l1 = l01[:, 0, :], l01[:, 1, :]
-        nc.vector.tensor_copy(l0, second[0][:, 0:HALF])
-        nc.vector.tensor_copy(l1, second[1][:, 0:HALF])
         vector_scatter(0, l0, *SECOND)
         store(0)
+        f1 = first_copy(1)
+        l1 = second_copy(1)
         f2 = first_copy(2, 6144)
         scalar_scatter(1, f1, *FIRST)
         l2 = second_copy(2)

@@ -16,6 +16,7 @@ E4M3 = mybir.dt.float8_e4m3fn_x4
 E5M2 = mybir.dt.float8_e5m2_x4
 MULT = mybir.AluOpType.mult
 SUB = mybir.AluOpType.subtract
+ADD = mybir.AluOpType.add
 ACT = mybir.ActivationFunctionType
 
 P = 128
@@ -199,7 +200,7 @@ def tile_attend_gcau_wx_ts_kernel(tc, xT, wT, y, wt, ts, xm, offs, out_0, out_1)
                 for t in range(PACK):
                     mx(scores[j][:, t * P : (t + 1) * P], x_q, E4M3, slice(t * P, (t + 1) * P), w_half, E4M3, w_cols)
 
-        xm_q = operand("xm")
+        xm_q = [operand(f"xm{m}", P) for m in range(PACK)]
 
         def xm_block(lo, hi, copy, buffer):
             xm_bf = tile(f"xm_bf{lo}", [P, (hi - lo) * PACK], BF16, buffer)
@@ -209,8 +210,20 @@ def tile_attend_gcau_wx_ts_kernel(tc, xT, wT, y, wt, ts, xm, offs, out_0, out_1)
             )
             return xm_bf
 
+        def xm_block_gpsimd(lo, hi, buffer):
+            xm_bf = tile(f"xm_bf{lo}", [P, (hi - lo) * PACK], BF16, buffer)
+            nc.gpsimd.tensor_scalar(
+                out=xm_bf[:].rearrange("p (c t) -> p c t", t=PACK),
+                in0=xm_rest[:, :, lo - P : hi - P].rearrange("p t c -> p c t"),
+                scalar1=1.0,
+                scalar2=0.0,
+                op0=MULT,
+                op1=ADD,
+            )
+            return xm_bf
+
         def quantize_xm(lo, hi, xm_bf):
-            quantize(xm_q, lo, hi, xm_bf[:], E4M3)
+            quantize(xm_q[lo // P], 0, P, xm_bf[:], E4M3)
 
         h_bf = tile("h_bf", [P, N * PACK], BF16)
         a = [tile(f"a{j}", [P, R], F32, {0: 26624, 3: 25600}.get(j)) for j in range(CHUNKS)]
@@ -267,7 +280,7 @@ def tile_attend_gcau_wx_ts_kernel(tc, xT, wT, y, wt, ts, xm, offs, out_0, out_1)
 
         def table_product(m, tag, name, lo=0, hi=N):
             acc = bank(tag, name)
-            mx(acc[:, 0 : hi - lo], xm_q, E4M3, slice(m * P, (m + 1) * P), h_q, E5M2, slice(lo, hi))
+            mx(acc[:, 0 : hi - lo], xm_q[m], E4M3, slice(0, P), h_q, E5M2, slice(lo, hi))
             return acc
 
         def to_sbuf(copy, acc, width, name, buffer=None):
@@ -279,7 +292,7 @@ def tile_attend_gcau_wx_ts_kernel(tc, xT, wT, y, wt, ts, xm, offs, out_0, out_1)
             nc.sync.dma_start(out=out_0[m * P : (m + 1) * P, :], in_=windows[m][:])
 
         def vector_scatter(m, dw, lo, hi):
-            nc.vector.tensor_copy(windows[m][:].indirect(offsets[:, lo // 16 : hi // 16]), dw[:])
+            nc.vector.tensor_copy(windows[m][:].indirect(offsets[:, lo // 16 : hi // 16]), dw)
 
         def scalar_scatter(m, dw, lo, hi):
             for part in range(lo, hi, HALF):
@@ -300,6 +313,7 @@ def tile_attend_gcau_wx_ts_kernel(tc, xT, wT, y, wt, ts, xm, offs, out_0, out_1)
         for cols in halves:
             square(0, cols)
         numerator(0)
+        xm1 = xm_block_gpsimd(P, 2 * P, 27648)
         s3 = times_ts(3)
         residual(1, s1)
         for cols in halves:
@@ -336,39 +350,41 @@ def tile_attend_gcau_wx_ts_kernel(tc, xT, wT, y, wt, ts, xm, offs, out_0, out_1)
             return to_sbuf(nc.vector.tensor_copy, second[m], HALF, f"dw_second{m}", buffer)
 
         f0 = first_copy(0, "root3")
-        xm2 = xm_block(2 * P, 3 * P, nc.scalar.copy, "root2")
-        scalar_scatter(0, f0, *FIRST)
-        quantize_h(HALF + CHUNK, N)
-        xm1 = xm_block(P, 2 * P, nc.vector.tensor_copy, 1024)
-        quantize_h(HALF, HALF + CHUNK)
-        second = {0: table_product(0, "A1", "second0", *SECOND)}
         quantize_xm(P, 2 * P, xm1)
         first[1] = table_product(1, "C1", "first1", *FIRST)
-        second[1] = table_product(1, "A2", "second1", *SECOND)
+        scalar_scatter(0, f0, *FIRST)
+        quantize_h(HALF + CHUNK, N)
+        part3 = table_product(0, "A1", "part3", HALF + CHUNK, N)
+        xm2 = xm_block(2 * P, 3 * P, nc.vector.tensor_copy, 1024)
+        quantize_h(HALF, HALF + CHUNK)
+        part2 = table_product(0, "A2", "part2", HALF, HALF + CHUNK)
+        second = {1: table_product(1, "B0", "second1", *SECOND)}
         xm3 = xm_block(3 * P, D, nc.vector.tensor_copy, 2048)
         quantize_xm(2 * P, 3 * P, xm2)
         first[2] = table_product(2, "A3", "first2", *FIRST)
-        second[2] = table_product(2, "B0", "second2", *SECOND)
-        l0 = second_copy(0, 30720)
+        second[2] = table_product(2, "B1", "second2", *SECOND)
         quantize_xm(3 * P, D, xm3)
-        first[3] = table_product(3, "B1", "first3", *FIRST)
+        first[3] = table_product(3, "C0", "first3", *FIRST)
         second[3] = table_product(3, "A0", "second3", *SECOND)
-        vector_scatter(0, l0, *SECOND)
+        l0 = tile("dw_second0", [P, HALF], F32)
+        nc.vector.tensor_copy(l0[:, CHUNK:HALF], part3[:, 0:CHUNK])
+        nc.vector.tensor_copy(l0[:, 0:CHUNK], part2[:, 0:CHUNK])
+        l1 = second_copy(1)
+        vector_scatter(0, l0[:], *SECOND)
         store(0)
         f1 = first_copy(1)
-        l1 = second_copy(1)
-        f2 = first_copy(2, 6144)
         scalar_scatter(1, f1, *FIRST)
         l2 = second_copy(2)
-        vector_scatter(1, l1, *SECOND)
+        vector_scatter(1, l1[:], *SECOND)
         store(1)
-        f3 = first_copy(3)
+        f2 = first_copy(2)
+        f3 = first_copy(3, 6144)
         scalar_scatter(2, f2, *FIRST)
         l3 = second_copy(3)
-        vector_scatter(2, l2, *SECOND)
+        vector_scatter(2, l2[:], *SECOND)
         store(2)
         scalar_scatter(3, f3, *FIRST)
-        vector_scatter(3, l3, *SECOND)
+        vector_scatter(3, l3[:], *SECOND)
         store(3)
 
         hi_q = operand("hi")
@@ -399,13 +415,13 @@ def tile_attend_gcau_wx_ts_kernel(tc, xT, wT, y, wt, ts, xm, offs, out_0, out_1)
         def store_rows(u):
             nc.sync.dma_start(out=gx_rows[:, 2 * u : 2 * u + 2, :], in_=gx[u][:])
 
-        hi_bf0 = h_by_slots(0, "A1", nc.scalar.copy, 6656)
-        hi_bf1 = h_by_slots(1, "A2", nc.scalar.copy, 4608)
+        hi_bf0 = h_by_slots(0, "B1", nc.scalar.copy, 6656)
+        hi_bf1 = h_by_slots(1, "A0", nc.scalar.copy, 4608)
         quantize_hi(0, hi_bf0)
-        row_block(0, "C1", nc.vector.tensor_copy)
-        row_block(1, "A3", nc.scalar.copy)
+        row_block(0, "A1", nc.vector.tensor_copy)
+        row_block(1, "A2", nc.scalar.copy)
         store_rows(0)
         quantize_hi(1, hi_bf1)
-        row_block(2, "B0", nc.vector.tensor_copy)
-        row_block(3, "B1", nc.scalar.copy)
+        row_block(2, "A3", nc.vector.tensor_copy)
+        row_block(3, "C1", nc.scalar.copy)
         store_rows(1)

@@ -191,8 +191,19 @@ def tile_attend_gcau_wx_ts_kernel(tc, xT, wT, y, wt, ts, xm, offs, out_0, out_1)
         quantize(w_q[1], 0, HALF, w_bf[:, HALF * PACK : N * PACK], E4M3)
         wi_bf1 = tile("wi_bf1", [P, D * PACK // 2], BF16, 16384)
         pair_to_sbuf(nc.scalar.copy, w_turn1, wi_bf1[:])
+        quantize(wi_q, D // 2, D, wi_bf1[:], E4M3)
 
-        for j in range(CHUNKS):
+        first_scores = [bank("C1", "first_scores"), scores[0]]
+
+        def score_first(u):
+            for e in range(2):
+                t = 2 * u + e
+                mx(first_scores[u][:, e * P : (e + 1) * P], x_q, E4M3, slice(t * P, (t + 1) * P), w_q[0], E4M3, slice(0, CHUNK))
+
+        score_first(0)
+        for j in range(1, CHUNKS):
+            if j == 1:
+                score_first(1)
             w_half, w_cols = w_q[j * CHUNK // HALF], slice(j * CHUNK % HALF, j * CHUNK % HALF + CHUNK)
             if j in TURNED:
                 mx(scores[j][:], w_half, E4M3, w_cols, x_q, E4M3, slice(0, R))
@@ -303,11 +314,15 @@ def tile_attend_gcau_wx_ts_kernel(tc, xT, wT, y, wt, ts, xm, offs, out_0, out_1)
                 )
 
         xm0 = xm_block(0, P, nc.scalar.copy, 18432)
-        s0 = times_ts(0)
+        ts_first = ts_all[:, slots(0)].unsqueeze(1).to_broadcast([P, 2, CHUNK])
+        for u in range(2):
+            nc.vector.tensor_tensor(planes_of(a[0])[:, 2 * u : 2 * u + 2], planes_of(first_scores[u])[:, 0:2], ts_first, MULT)
         s1 = times_ts(1)
         s2 = times_ts(2)
-        quantize(wi_q, D // 2, D, wi_bf1[:], E4M3)
-        residual(0, s0)
+        for u in range(2):
+            nc.vector.tensor_tensor(
+                planes_of(q[0])[:, 2 * u : 2 * u + 2], planes_of(a[0])[:, 2 * u : 2 * u + 2], y_sb[0][:, 2 * u : 2 * u + 2, slots(0)], SUB
+            )
         quantize_xm(0, P, xm0)
         halves = (slice(0, R // 2), slice(R // 2, R))
         for cols in halves:

from contextlib import ExitStack

import concourse.mybir as mybir
from concourse.masks import make_identity

N, T, D, R = 512, 2048, 512, 512
FLOPS = 3 * 2 * N * D * R

F32 = mybir.dt.float32
BF16 = mybir.dt.bfloat16
U32 = mybir.dt.uint32
I32 = mybir.dt.int32
U16 = mybir.dt.uint16
U8 = mybir.dt.uint8
E4M3 = mybir.dt.float8_e4m3fn_x4
E5M2 = mybir.dt.float8_e5m2_x4
MULT = mybir.AluOpType.mult
SUB = mybir.AluOpType.subtract
ADD = mybir.AluOpType.add
ACT = mybir.ActivationFunctionType

P = 128
PACK = 4
HALF = N // 2
CHUNK = 128
CHUNKS = N // CHUNK
TURNED = (1, 2)
VECTOR_SQUARE = CHUNKS - 1
GPSIMD_NUMERATOR = 0
WEAVE_SPLIT = 352
X_SPLIT = 32
WINDOWS = 4
VECTOR_MEMSETS = 2


def tile_attend_gcau_wx_ts_kernel(tc, xT, wT, y, wt, ts, xm, offs, out_0, out_1):
    nc = tc.nc
    with ExitStack() as ctx:
        sb = ctx.enter_context(tc.tile_pool(name="sb", bufs=1))
        ps = ctx.enter_context(tc.psum_pool(name="ps", bufs=1))
        shared = ctx.enter_context(tc.tile_pool(name="shared", bufs=1))

        def tile(name, shape, dtype, buffer=None):
            if isinstance(buffer, int):
                return shared.tile(shape, dtype, name=name, align_bytes=64, offset=buffer)
            return sb.tile(shape, dtype, name=name, tag=buffer or name, align_bytes=64)

        def bank(tag, name):
            return ps.tile([P, 512], F32, name=name, tag=tag)

        def operand(name, columns=512, buffer=None):
            return tile(name + "_codes", [P, columns], U32, buffer), tile(name + "_scales", [P, columns], U8)

        def quantize(op, lo, hi, src, fmt):
            nc.vector.quantize_mx(out=op[0][:, lo:hi].bitcast(fmt), scales=op[1][:, lo:hi], in_=src)

        def mx(out, lhs, lhs_fmt, lhs_cols, rhs, rhs_fmt, rhs_cols):
            nc.tensor.matmul_mx(
                out=out,
                lhsT=lhs[0][:, lhs_cols].bitcast(lhs_fmt),
                lhsT_scale=lhs[1][:, lhs_cols],
                rhs=rhs[0][:, rhs_cols].bitcast(rhs_fmt),
                rhs_scale=rhs[1][:, rhs_cols],
                start=True,
                stop=True,
            )

        offsets = sb.tile([P, N // 16], U16, name="offsets")
        ts_cols = tile("ts_cols", [P, T // P], F32)
        nc.sync.dma_start(out=ts_cols[:], in_=ts[0].rearrange("(p c) -> p c", p=P))
        picked = tile("picked", [P, 5 * N], BF16, 10240)
        wt_sb = picked[:, 4 * N : 4 * N + 2 * PACK].bitcast(F32)
        w_rows = wT.rearrange("(p t) c -> p t c", t=PACK)
        planes = [tile(f"plane{t}", [P, T], F32) for t in range(PACK)]
        nc.sync.dma_start(out=planes[0][:], in_=w_rows[:, 0, :])
        nc.sync.dma_start(offsets[:], offs)
        nc.sync.dma_start(out=wt_sb, in_=wt[0].rearrange("(p t) o -> p (t o)", t=PACK))
        for t in (1, 2, 3):
            nc.sync.dma_start(out=planes[t][:], in_=w_rows[:, t, :])
        x_raw = tile("x_raw", [P, PACK, R], F32, 16384)
        nc.sync.dma_start(out=x_raw[:], in_=xT[0].rearrange("(p j) r -> p j r", j=PACK))
        y_rows = y[0].rearrange("(p t) i -> p t i", t=PACK)
        xm_rows = xm[0].rearrange("(p t) d -> p t d", t=PACK)
        y_sb = [tile(f"y_sb{u}", [P, PACK, HALF], F32) for u in range(2)]
        xm_first = tile("xm_first", [P, PACK, P], F32)
        xm_rest = tile("xm_rest", [P, PACK, D - P], F32, 30720)
        nc.sync.dma_start(out=y_sb[0][:], in_=y_rows[:, :, 0:HALF])
        nc.sync.dma_start(out=xm_first[:], in_=xm_rows[:, :, 0:P])
        nc.sync.dma_start(out=y_sb[1][:], in_=y_rows[:, :, HALF:N])
        nc.sync.dma_start(out=xm_rest[:], in_=xm_rows[:, :, P:D])

        zero = tile("zero", [P, 1], F32)
        nc.vector.memset(zero[:], 0.0)
        one = tile("one", [P, 1], F32)
        nc.vector.memset(one[:], 1.0)
        root_bias = tile("root_bias", [P, 1], F32)
        nc.scalar.activation(out=root_bias[:], in_=zero[:], func=ACT.Abs_reciprocal_sqrt, bias=one[:])
        ident = tile("ident", [P, P], F32)
        make_identity(nc, ident[:])

        h_q = operand("h")
        windows = [tile(f"window{m}", [P, T], F32) for m in range(VECTOR_MEMSETS)]
        for window in windows:
            nc.vector.memset(window[:].bitcast(I32), 0)

        ts_win = tile("ts_win", [P, T], F32)
        for g in range(PACK):
            spread = bank(f"A{g}", f"spread{g}")
            for e in range(PACK):
                c = PACK * g + e
                nc.tensor.transpose(spread[:, e * P : (e + 1) * P], ts_cols[:, c : c + 1].to_broadcast([P, P]), ident[:])
            nc.scalar.copy(
                out=ts_win[:].rearrange("m (p g e) -> m g p e", g=PACK, e=PACK)[:, g],
                in_=spread[:].rearrange("m (e p) -> m p e", e=PACK),
            )
        ts_all = tile("ts_all", [P, N], F32)
        ts_slot = tile("ts_slot", [P, CHUNKS], F32)
        factor = tile("factor", [P, PACK, N], F32)

        x_q = operand("x")
        w_bf = tile("w_bf", [P, N * PACK], BF16)
        wi_q = operand("wi", D)

        def plane_of(t, lo=0, hi=N):
            return picked[:, t * N + lo : t * N + hi]

        def turn_pair(u, tag):
            dst = bank(tag, f"w_turn{u}")
            for e in range(2):
                slot_pairs = plane_of(2 * u + e).bitcast(F32)
                for v in range(2):
                    nc.tensor.transpose(dst[:, (2 * e + v) * P : (2 * e + v + 1) * P], slot_pairs[:, v : N // 2 : 2], ident[:])
            return dst

        def pair_to_sbuf(copy, turned_pair, dst):
            copy(
                out=dst.bitcast(F32).rearrange("g (p e v) -> g p e v", e=2, v=2),
                in_=turned_pair[:].rearrange("g (e v p) -> g p e v", e=2, v=2),
            )

        def weave(copy, lo, hi):
            copy(
                out=w_bf[:, lo * PACK : hi * PACK].rearrange("p (c e t) -> p c t e", e=PACK, t=PACK),
                in_=picked[:, 0 : PACK * N].rearrange("p (t i) -> p t i", t=PACK)[:, :, lo:hi].rearrange("p t (c e) -> p c t e", e=PACK),
            )

        nc.scalar.activation(out=ts_all[:], in_=ts_win[:].indirect(offsets[:]), func=ACT.Copy)
        ts_turn = bank("C0", "ts_turn")
        for j in TURNED:
            nc.tensor.transpose(ts_turn[:, j * P : (j + 1) * P], ts_all[:, j * P : (j + 1) * P], ident[:])
        for t in range(PACK):
            nc.scalar.activation(out=factor[:, t, :], in_=ts_all[:], func=ACT.Copy, scale=wt_sb[:, t : t + 1])
        nc.scalar.copy(out=ts_slot[:, TURNED[0] : TURNED[-1] + 1], in_=ts_turn[:, TURNED[0] * P : (TURNED[-1] + 1) * P : P])
        for t in range(3):
            nc.vector.tensor_copy(plane_of(t), planes[t][:].indirect(offsets[:]))
        for m, plane in ((2, "plane0"), (3, "plane1")):
            windows.append(tile(f"window{m}", [P, T], F32, plane))
            nc.gpsimd.memset(windows[m][:].bitcast(I32), 0)
        wi_bf0 = picked[:, 3 * N : 5 * N]
        pair_to_sbuf(nc.scalar.copy, turn_pair(0, "C1"), wi_bf0)
        quantize(wi_q, 0, D // 2, wi_bf0, E4M3)
        nc.vector.tensor_copy(plane_of(3, 0, HALF), planes[3][:].indirect(offsets[:, 0 : HALF // 16]))
        nc.scalar.activation(out=plane_of(3, HALF, N), in_=planes[3][:].indirect(offsets[:, HALF // 16 : N // 16]), func=ACT.Copy)
        weave(nc.vector.tensor_copy, 0, HALF)
        weave(nc.scalar.copy, WEAVE_SPLIT, N)
        weave(nc.vector.tensor_copy, HALF, WEAVE_SPLIT)
        w_turn1 = turn_pair(1, "C0")
        scores = [bank(f"A{j}", f"scores{j}") for j in range(CHUNKS)]
        w_q = [operand("w0", HALF)]
        quantize(w_q[0], 0, HALF, w_bf[:, 0 : HALF * PACK], E4M3)

        x_bf = [tile(f"x_bf{u}", [P, R * 2], BF16, 10240 + 2048 * u) for u in range(2)]
        for copy, u, lo, hi in (
            (nc.vector.tensor_copy, 0, 0, P),
            (nc.scalar.copy, 1, X_SPLIT, P),
            (nc.vector.tensor_copy, 1, 0, X_SPLIT),
        ):
            copy(
                out=x_bf[u][:].rearrange("p (t m j) -> p m j t", t=2, j=PACK)[:, lo:hi],
                in_=x_raw[:].rearrange("p j (m t) -> p m j t", t=PACK)[:, lo:hi, :, 2 * u : 2 * u + 2],
            )

        def turn(src, u, dst_bank):
            words = src[:].bitcast(F32)
            for s in range(PACK):
                nc.tensor.transpose(dst_bank[:, s * P : (s + 1) * P], words[:, 2 * s + u : 2 * N : 2 * PACK], ident[:])

        for u in range(2):
            quantize(x_q, u * R // 2, (u + 1) * R // 2, x_bf[u][:], E4M3)
        w_q.append(operand("w1", HALF, 10240))
        quantize(w_q[1], 0, HALF, w_bf[:, HALF * PACK : N * PACK], E4M3)
        wi_bf1 = tile("wi_bf1", [P, D * PACK // 2], BF16, 16384)
        pair_to_sbuf(nc.scalar.copy, w_turn1, wi_bf1[:])
        quantize(wi_q, D // 2, D, wi_bf1[:], E4M3)

        first_scores = [bank("C1", "first_scores"), scores[0]]

        def score_first(u):
            for e in range(2):
                t = 2 * u + e
                mx(first_scores[u][:, e * P : (e + 1) * P], x_q, E4M3, slice(t * P, (t + 1) * P), w_q[0], E4M3, slice(0, CHUNK))

        score_first(0)
        for j in range(1, CHUNKS):
            if j == 1:
                score_first(1)
            w_half, w_cols = w_q[j * CHUNK // HALF], slice(j * CHUNK % HALF, j * CHUNK % HALF + CHUNK)
            if j in TURNED:
                mx(scores[j][:], w_half, E4M3, w_cols, x_q, E4M3, slice(0, R))
            else:
                for t in range(PACK):
                    mx(scores[j][:, t * P : (t + 1) * P], x_q, E4M3, slice(t * P, (t + 1) * P), w_half, E4M3, w_cols)

        xm_q = [operand(f"xm{m}", P) for m in range(PACK)]

        def xm_block(lo, hi, copy, buffer):
            xm_bf = tile(f"xm_bf{lo}", [P, (hi - lo) * PACK], BF16, buffer)
            copy(
                out=xm_bf[:].rearrange("p (c e t) -> p c t e", e=PACK, t=PACK),
                in_=(xm_first[:] if lo == 0 else xm_rest[:, :, lo - P : hi - P]).rearrange("p t (c e) -> p c t e", e=PACK),
            )
            return xm_bf

        def xm_block_gpsimd(lo, hi, buffer):
            xm_bf = tile(f"xm_bf{lo}", [P, (hi - lo) * PACK], BF16, buffer)
            nc.gpsimd.tensor_scalar(
                out=xm_bf[:].rearrange("p (c t) -> p c t", t=PACK),
                in0=xm_rest[:, :, lo - P : hi - P].rearrange("p t c -> p c t"),
                scalar1=1.0,
                scalar2=0.0,
                op0=MULT,
                op1=ADD,
            )
            return xm_bf

        def quantize_xm(lo, hi, xm_bf):
            quantize(xm_q[lo // P], 0, P, xm_bf[:], E4M3)

        h_bf = tile("h_bf", [P, N * PACK], BF16)
        a = [tile(f"a{j}", [P, R], F32, {0: 26624, 3: 25600}.get(j)) for j in range(CHUNKS)]
        q = [tile(f"q{j}", [P, R], F32, "a1" if j == CHUNKS - 1 else None) for j in range(CHUNKS)]
        sq, root, rec = ([tile(f"{kind}{j}", [P, R], F32) for j in range(CHUNKS)] for kind in ("sq", "root", "rec"))
        num = [tile(f"num{j}", [P, R], F32, 1024 if j == 2 else None) for j in range(CHUNKS)]

        def planes_of(flat):
            return flat[:].rearrange("p (t i) -> p t i", t=PACK)

        def slots(j):
            return slice(j * CHUNK, (j + 1) * CHUNK)

        def times_ts(j):
            if j not in TURNED:
                ts_chunk = ts_all[:, slots(j)].unsqueeze(1).to_broadcast([P, PACK, CHUNK])
                nc.vector.tensor_tensor(planes_of(a[j]), planes_of(scores[j]), ts_chunk, MULT)
                return a[j]
            nc.scalar.activation(out=a[j][:], in_=scores[j][:], func=ACT.Copy, scale=ts_slot[:, j : j + 1])
            turned = bank(f"B{TURNED.index(j)}", f"turned{j}")
            for t in range(PACK):
                nc.tensor.transpose(turned[:, t * P : (t + 1) * P], a[j][:, t * P : (t + 1) * P], ident[:])
            return turned

        def residual(j, scaled_chunk):
            nc.vector.tensor_tensor(planes_of(q[j]), planes_of(scaled_chunk), y_sb[j // 2][:, :, slots(j % 2)], SUB)

        def square(j, cols=slice(0, R)):
            if j == VECTOR_SQUARE:
                nc.vector.tensor_tensor(sq[j][:], q[j][:], q[j][:], MULT)
            else:
                nc.scalar.activation(out=sq[j][:, cols], in_=q[j][:, cols], func=ACT.Square)

        def inverse_root(j, cols=slice(0, R)):
            nc.scalar.activation(out=root[j][:, cols], in_=sq[j][:, cols], func=ACT.Abs_reciprocal_sqrt, bias=root_bias[:])

        def inverse(j, cols=slice(0, R)):
            nc.scalar.activation(out=rec[j][:, cols], in_=root[j][:, cols], func=ACT.Square)

        def numerator(j):
            engine = nc.gpsimd if j == GPSIMD_NUMERATOR else nc.vector
            engine.tensor_tensor(planes_of(num[j]), planes_of(q[j]), factor[:, :, slots(j)], MULT)

        def finish(j):
            nc.vector.tensor_tensor(
                h_bf[:, j * CHUNK * PACK : (j + 1) * CHUNK * PACK].rearrange("p (c e t) -> p c t e", e=2, t=PACK),
                num[j][:].rearrange("p (t c e) -> p c t e", t=PACK, e=2),
                rec[j][:].rearrange("p (t c e) -> p c t e", t=PACK, e=2),
                MULT,
            )

        def quantize_h(lo, hi):
            quantize(h_q, lo, hi, h_bf[:, lo * PACK : hi * PACK], E5M2)

        def table_product(m, tag, name, lo=0, hi=N):
            acc = bank(tag, name)
            mx(acc[:, 0 : hi - lo], xm_q[m], E4M3, slice(0, P), h_q, E5M2, slice(lo, hi))
            return acc

        def to_sbuf(copy, acc, width, name, buffer=None):
            dw = tile(name, [P, width], F32, buffer)
            copy(out=dw[:], in_=acc[:, 0:width])
            return dw

        def store(m):
            nc.sync.dma_start(out=out_0[m * P : (m + 1) * P, :], in_=windows[m][:])

        def vector_scatter(m, dw, lo, hi):
            nc.vector.tensor_copy(windows[m][:].indirect(offsets[:, lo // 16 : hi // 16]), dw)

        def scalar_scatter(m, dw, lo, hi):
            for part in range(lo, hi, HALF):
                nc.scalar.activation(
                    out=windows[m][:].indirect(offsets[:, part // 16 : (part + HALF) // 16]),
                    in_=dw[:, part - lo : part - lo + HALF],
                    func=ACT.Copy,
                )

        xm0 = xm_block(0, P, nc.scalar.copy, 18432)
        ts_first = ts_all[:, slots(0)].unsqueeze(1).to_broadcast([P, 2, CHUNK])
        for u in range(2):
            nc.vector.tensor_tensor(planes_of(a[0])[:, 2 * u : 2 * u + 2], planes_of(first_scores[u])[:, 0:2], ts_first, MULT)
        s1 = times_ts(1)
        s2 = times_ts(2)
        for u in range(2):
            nc.vector.tensor_tensor(
                planes_of(q[0])[:, 2 * u : 2 * u + 2], planes_of(a[0])[:, 2 * u : 2 * u + 2], y_sb[0][:, 2 * u : 2 * u + 2, slots(0)], SUB
            )
        quantize_xm(0, P, xm0)
        halves = (slice(0, R // 2), slice(R // 2, R))
        for cols in halves:
            square(0, cols)
        numerator(0)
        xm1 = xm_block_gpsimd(P, 2 * P, 27648)
        s3 = times_ts(3)
        residual(1, s1)
        for cols in halves:
            inverse_root(0, cols)
        inverse(0, halves[0])
        square(1)
        residual(2, s2)
        residual(3, s3)
        inverse(0, halves[1])
        inverse_root(1)
        square(2, halves[0])
        numerator(1)
        square(3)
        inverse(1)
        square(2, halves[1])
        finish(0)
        numerator(3)
        finish(1)
        inverse_root(3)
        inverse_root(2)
        numerator(2)
        quantize_h(0, HALF)
        FIRST, SECOND = (0, HALF), (HALF, N)
        first = {0: table_product(0, "A0", "first0", *FIRST)}
        inverse(3)
        inverse(2)
        finish(3)
        finish(2)

        def first_copy(m, buffer=None):
            return to_sbuf(nc.scalar.copy, first[m], HALF, f"dw_first{m}", buffer)

        def second_copy(m, buffer=None):
            return to_sbuf(nc.vector.tensor_copy, second[m], HALF, f"dw_second{m}", buffer)

        f0 = first_copy(0, "root3")
        quantize_xm(P, 2 * P, xm1)
        first[1] = table_product(1, "C1", "first1", *FIRST)
        scalar_scatter(0, f0, *FIRST)
        quantize_h(HALF + CHUNK, N)
        part3 = table_product(0, "A1", "part3", HALF + CHUNK, N)
        xm2 = xm_block(2 * P, 3 * P, nc.vector.tensor_copy, 1024)
        quantize_h(HALF, HALF + CHUNK)
        part2 = table_product(0, "A2", "part2", HALF, HALF + CHUNK)
        second = {1: table_product(1, "B0", "second1", *SECOND)}
        xm3 = xm_block(3 * P, D, nc.vector.tensor_copy, 2048)
        quantize_xm(2 * P, 3 * P, xm2)
        first[2] = table_product(2, "A3", "first2", *FIRST)
        second[2] = table_product(2, "B1", "second2", *SECOND)
        quantize_xm(3 * P, D, xm3)
        first[3] = table_product(3, "C0", "first3", *FIRST)
        second[3] = table_product(3, "A0", "second3", *SECOND)
        l0 = tile("dw_second0", [P, HALF], F32)
        nc.vector.tensor_copy(l0[:, CHUNK:HALF], part3[:, 0:CHUNK])
        nc.vector.tensor_copy(l0[:, 0:CHUNK], part2[:, 0:CHUNK])
        l1 = second_copy(1)
        vector_scatter(0, l0[:], *SECOND)
        store(0)
        f1 = first_copy(1)
        scalar_scatter(1, f1, *FIRST)
        l2 = second_copy(2)
        vector_scatter(1, l1[:], *SECOND)
        store(1)
        f2 = first_copy(2)
        f3 = first_copy(3, 6144)
        scalar_scatter(2, f2, *FIRST)
        l3 = second_copy(3)
        vector_scatter(2, l2[:], *SECOND)
        store(2)
        scalar_scatter(3, f3, *FIRST)
        vector_scatter(3, l3[:], *SECOND)
        store(3)

        hi_q = operand("hi")
        gx = [tile(f"gx{u}", [P, 2, D], F32) for u in range(2)]
        gx_rows = out_1[0].rearrange("(p t) d -> p t d", t=PACK)

        def h_by_slots(u, tag, copy, buffer):
            h_turn = bank(tag, f"h_turn{u}")
            turn(h_bf, u, h_turn)
            hi_bf = tile(f"hi_bf{u}", [P, R * 2], BF16, buffer)
            copy(
                out=hi_bf[:].rearrange("g (e p s) -> g p s e", e=2, s=PACK),
                in_=h_turn[:].bitcast(BF16).rearrange("g (s p e) -> g p s e", s=PACK, e=2),
            )
            return hi_bf

        def quantize_hi(u, hi_bf):
            quantize(hi_q, u * R // 2, (u + 1) * R // 2, hi_bf[:], E5M2)

        def row_block(t, tag, copy):
            acc = bank(tag, f"gx_acc{t}")
            mx(acc[:], hi_q, E5M2, slice(t * P, (t + 1) * P), wi_q, E4M3, slice(0, D))
            copy(
                out=gx[t // 2][:, t % 2, :].rearrange("r (p u e) -> r p u e", u=2, e=2),
                in_=acc[:].rearrange("r (u p e) -> r p u e", u=2, e=2),
            )

        def store_rows(u):
            nc.sync.dma_start(out=gx_rows[:, 2 * u : 2 * u + 2, :], in_=gx[u][:])

        hi_bf0 = h_by_slots(0, "B1", nc.scalar.copy, 6656)
        hi_bf1 = h_by_slots(1, "A0", nc.scalar.copy, 4608)
        quantize_hi(0, hi_bf0)
        row_block(0, "A1", nc.vector.tensor_copy)
        row_block(1, "A2", nc.scalar.copy)
        store_rows(0)
        quantize_hi(1, hi_bf1)
        row_block(2, "A3", nc.vector.tensor_copy)
        row_block(3, "C1", nc.scalar.copy)
        store_rows(1)
